import numpy as np, ml_dtypes
CORES = [5,29,101,125,133,157,229,253]
N = 8
BF = ml_dtypes.bfloat16
V, K, LA, LF, Q, RO, AS, FS = 2048, 768, 256, 192, 3, 3, 170, 255
def lanes(flag, start, cap):
    order = (np.arange(K) + start) % K; fl = flag[:, order]
    o = np.argsort(~fl, axis=1, kind="stable")[:, :cap]
    return order[o], np.take_along_axis(fl, o, 1)
def judge(X, C, ids, T):
    n = ids.shape[1]; lit = np.take_along_axis(C, ids[:, None, :], 2); v = np.where(lit >= V, lit - V, lit)
    s = np.take_along_axis(X, v.reshape(8, 1, 16 * n), 2).reshape(8, 16, 16, n)
    s = np.where((lit >= V)[:, None], 63 - s, s)
    return lit, v, s, np.max(s, axis=2) < T
def states(rng, pa, pd):
    a = rng.choice(np.array(pa), (N, 8, 1)); b = rng.choice(np.array(pd), (N, 8, 1)); u = rng.random((N, 8, K))
    return np.where(u < a, 0, np.where(u >= 1 - b, 4, rng.integers(1, 4, (N, 8, K))))
def parts(rng):
    u = rng.random((N, 8, 16, K)); v = np.minimum((V * u * np.sqrt(u)).astype(np.int64), V - 1)
    T = rng.integers(58, 60, (N, 8, 1, 1)) + rng.integers(0, 2, (N, 8, 16, 1))
    return rng.integers(0, 64, (N, 8, 16, V)), v + V * rng.integers(0, 2, v.shape), states(rng, [0.3, 0.4, 0.5], [0.01, 0.05, 0.2]), T
def at(a, v):
    return np.take_along_axis(a, v.reshape(N, 8, -1), 2).reshape(v.shape)
def first(X, C, F, T):
    ia, ok = lanes(F == 0, 0, LA)
    return ia, ok & (np.sum(judge(X, C, ia, T)[3], axis=1) > Q)
def laid(rng, own, place, rest):
    X = np.zeros((8, 16, V), np.int64); C = np.zeros((8, 16, K), np.int64)
    for g in range(8):
        o = rng.permutation(V); sign = rng.integers(0, 2, V)
        s = rng.integers(0, rest[g] + 1, (16, V)); s[:, o[:K]] = own[g]
        X[g] = np.where(sign == 1, 63 - s, s)
        v = o[rng.integers(K, V, (16, K))]; v[place[g], np.arange(K)] = o[:K]
        C[g] = v + V * sign[v]
    return X, C
def full(rng):
    T = rng.integers(50, 61, (8, 16, 1)); own = rng.integers(10, 18, (8, 16, K)); place = rng.integers(0, 16, (8, K)); F = np.zeros((8, K), np.int64)
    own[[2, 7]] = 0; place[[2, 7]] = 0
    for g in range(8):
        o = rng.permutation(K); n = int(rng.integers(16, LF + 1))
        F[g, o[:n]] = rng.integers(1, 4, n); F[g, o[:16]] = 1
        own[g][:, o[:16]] = T[g] + rng.integers(0, 3, (16, 16))
    X, C = laid(rng, own, place, [9, 9, 0, 9, 9, 9, 9, 0])
    return X, C, F, T
def calm(rng):
    T = rng.integers(20, 51, (8, 16, 1)); own = np.repeat(T, K, axis=2); place = rng.integers(0, 16, (8, K)); F = rng.integers(1, 3, (8, K)); e = int(rng.integers(1, 4))
    for g in range(8):
        o = rng.permutation(K); n = 4 * int(rng.integers(2, LA >> 4)) + (e if g == 0 else 0); m = n + int(rng.integers(0, LA - n + 1)); h = m + ((K - m) >> 1)
        F[g, o[:m]] = 0
        own[g][:, o[n:h]] = 63; own[g][:, o[:n]] = T[g] - rng.integers(1, 6, (16, n))
    X, C = laid(rng, own, place, [9] * 8)
    return X, C, F, T
def pack(X, C, F, T):
    return {"xv": np.ascontiguousarray(X).reshape(N, 128, V).astype(np.float32).astype(BF), "cl": np.ascontiguousarray(C).reshape(N, 128, K).astype(np.int32),
            "fr": np.ascontiguousarray(F).astype(np.int32), "th": np.ascontiguousarray(T).reshape(N, 128, 1).astype(np.int32)}
def setup_inputs(rng):
    X, C, F, T = parts(rng)
    return pack(X, C, F, T)
def setup_inputs_spread(rng):
    low = np.minimum(np.exp2(6 * rng.random((N, 8, 1, V))) * rng.random((N, 8, 16, V)), 63).astype(np.int64)
    flip = rng.random((N, 8, V)) < 0.5; X = np.where(flip[:, :, None], 63 - low, low)
    u = rng.random((N, 8, 16, K)); v = np.minimum((V * u * u).astype(np.int64), V - 1)
    up = rng.random(v.shape) < rng.choice(np.array([0.0, 0.02, 0.06, 0.12]), (N, 8, 1, K))
    T = np.clip(61 - np.exp2(5.907 * rng.random((N, 8, 16, 1))).astype(np.int64), 1, 60)
    return pack(X, v + V * (at(flip, v) ^ up).astype(np.int64), states(rng, [0.1, 0.3, 0.6, 0.9], [0.0, 0.02, 0.3]), T)
def setup_inputs_ends(rng):
    X = 63 * rng.integers(0, 2, (N, 8, 16, V)); k = np.arange(16)[:, None]
    T = np.where(rng.random((N, 8, 16, 1)) < 0.75, 60, 1); T[:, [3, 7]] = 60; T[:, 0, 0] = 1
    u = rng.random((N, 8, K)); F = np.where(u < 0.45, 0, np.where(u < 0.75, 4, rng.choice(np.array([1, 3]), (N, 8, K))))
    m = rng.choice(np.array([16, 16, Q + 1, Q]), (N, 8, 1)); m[:, 1] = Q + 1; m[:, 2] = Q; m[:, [3, 7]] = 16
    low = np.argsort(np.argsort(rng.random((N, 8, 16)), axis=2), axis=2) < m
    X[..., 0] = np.where(low, 0, 63); X[..., V - 1] = np.where(low, 63, 0); X[..., 65] = 63
    sp = np.concatenate([np.arange(1, 65), np.arange(V - 65, V - 1)]); j = np.arange(128); cls = (j >> 1) % 3
    s = np.where(cls == 0, 59, np.where((cls == 2) & (k > Q), 63, 62)) - ((j // 6) % 2) * (k == j % 16)
    X[..., sp] = np.where(j % 2 == 1, 63 - s, s); lit = sp + V * (j % 2)
    C = np.where(rng.random((N, 8, 16, K)) < rng.choice(np.array([0.0, 0.5, 0.5, 1.0]), (N, 8, 1, K)), 0, 2 * V - 1)
    kind = rng.choice(np.array([0, 0, 0, 0, 0, 0, 0, 1, 2, 3]), (N, 8, K)); frm = rng.integers(0, 16, (N, 8, K))
    for q in range(N):
        F[q, 7] = 4; kind[q, 7] = rng.choice(np.array([0, 0, 1]), K)
        b = np.append(np.sort(AS + rng.permutation(K - 1 - AS)[:LA - 1]), K - 1)
        F[q, 7, rng.permutation(AS)[:32]] = 0; F[q, 7, b] = 0
        kind[q, 7, b[-32:]] = 2; kind[q, 7, b[-2:]] = 3; frm[q, 7, b[-2:]] = 0
    for c in range(3):
        a = lit[cls == c]; fill = a[rng.integers(0, len(a), C.shape)]
        C = np.where((kind == c + 1)[:, :, None] & (k >= frm[:, :, None]), fill, C)
    for q in range(N):
        ia, bad = first(X[q], C[q], F[q], T[q]); b = np.flatnonzero(bad[3])[:(int(np.sum(bad)) - 3) % 4]
        C[q, 3, 8, ia[3, b]] = 65
    return pack(X, C, F, T)
def setup_inputs_corners(rng):
    X, C, F, T = parts(rng); w = rng.random((N, 8, 1, K)); e = np.array([0, V - 1, V, 2 * V - 1])
    C = np.where(w < 0.15, rng.choice(e, (N, 8, 1, K)), np.where(w < 0.3, np.arange(K) + V * rng.integers(0, 2, (N, 8, 1, K)), np.where(w < 0.45, rng.choice(e, (N, 8, 16, K)), C)))
    T[:, 1] = np.where(rng.random((N, 16, 1)) < 0.3, 1, 60); T[:, 5] = 1; T[:, 6] = 60
    cases = ((0, K), (K, 0), (LA, LF), (LA + 1, LF + 1), (LA - 1, LF - 1), (1, 0), (2, K - 2), (0, 0))
    for q in range(N):
        for g in range(8):
            na, nz = cases[(g + q) % 8]; o = rng.permutation(K)
            F[q, g] = 4; F[q, g, o[:na]] = 0; F[q, g, o[na:na + nz]] = rng.integers(1, 4, nz)
    for q in range(0, N - 1, 2):
        bad = first(X[q], C[q], F[q], T[q])[1]; n = np.sum(bad[:, 0::2] & bad[:, 1::2], axis=1); c = 0
        for g in range(8):
            if n[g] < 2: continue
            d = int(n[g]) + (0, 1, -1)[c % 3]; c += 1
            z = rng.integers(0, 4, K); z[rng.permutation(K)[:d]] = 4; F[q + 1, g] = z
    return pack(X, C, F, T)
def setup_inputs_ties(rng):
    b = rng.choice(np.array([9, 30, 60]), (N, 8, 1, 1)); T = np.zeros((N, 8, 16, 1), np.int64) + b; i = np.arange(16)[:, None]
    mul = 2 * rng.integers(0, 8, (N, 8, 1, V)) + 1; sh = rng.integers(0, 16, (N, 8, 1, V)); n = Q + rng.integers(0, 2, (N, 8, 1, V))
    odd = np.arange(V) % 2 == 1
    s = np.where(odd & ((i * mul + sh) % 16 >= n), b + rng.integers(0, 4, (N, 8, 1, V)), b - 1 - rng.integers(0, 2, (N, 8, 1, V)))
    flip = rng.random((N, 8, V)) < 0.5; X = np.where(flip[:, :, None], 63 - s, s)
    lim = rng.choice(np.array([V // 2, V // 2, V // 16]), (N, 8, 1, 1))
    v = 2 * np.minimum((rng.random((N, 8, 16, K)) * lim).astype(np.int64), lim - 1)
    one = (i == rng.integers(0, 16, (N, 8, 1, K))) & (rng.random((N, 8, 1, K)) < 0.9)
    v = np.where(one, 2 * rng.integers(0, V // 2, v.shape) + 1, v)
    return pack(X, v + V * at(flip, v).astype(np.int64), states(rng, [0.3, 0.4, 0.5], [0.02, 0.1, 0.2]), T)
def setup_inputs_alike(rng):
    X, C, F, T = parts(rng); few = rng.integers(0, V, (N, 8, 24)); few[:, :, 0] = 0; few[:, :, 1] = V - 1
    v = np.take_along_axis(few, rng.integers(0, 24, (N, 8, 16 * K)), 2).reshape(N, 8, 16, K) + V * rng.integers(0, 2, (N, 8, 16, K))
    C[:, ::2] = v[:, ::2]
    for q in range(N): C[q, 5] = C[q, 5][:, rng.integers(0, 8, K)]
    o = rng.permutation(N)
    X[o[0]], C[o[0]], F[o[0]], T[o[0]] = full(rng)
    X[o[1]], C[o[1]], F[o[1]], T[o[1]] = calm(rng)
    return pack(X, C, F, T)
def check_inputs(d):
    bad = []
    for k, lo, hi in (("xv", 0, 63), ("cl", 0, 2 * V - 1), ("fr", 0, 4), ("th", 1, 60)):
        a = np.asarray(d[k]).astype(np.float64)
        if not np.all((a >= lo) & (a <= hi)): bad.append("range of " + k)
        elif not np.all(a == np.floor(a)): bad.append("whole numbers of " + k)
    return bad
def reference(xv, cl, fr, th):
    X = xv.astype(np.float32).astype(np.int64).reshape(N, 8, 16, V); C = cl.astype(np.int64).reshape(N, 8, 16, K); F = fr.astype(np.int64).reshape(N, 8, K)
    TH = th.astype(np.int64).reshape(N, 8, 16, 1); A = np.zeros(N, np.int64)
    for t in range(RO):
        nX = np.array(X); nC = np.array(C); nF = np.array(F); sent = []
        for r in range(N):
            T = TH[r] + (A[r] & 3)
            ia, oka = lanes(F[r] == 0, AS * t % K, LA); iz, okz = lanes((F[r] >= 1) & (F[r] <= 3), FS * t % K, LF)
            lit, v, s, fail = judge(X[r], C[r], ia, T); bad = oka & (np.sum(fail, axis=1) > Q); A[r] = np.sum(bad)
            m = oka & ~bad; nF[r][np.nonzero(m)[0], ia[m]] = 1
            wake = np.sum(judge(X[r], C[r], iz, T)[3], axis=1) > Q
            old = np.take_along_axis(F[r], iz, 1); nF[r][np.nonzero(okz)[0], iz[okz]] = np.where(wake, 0, old + 1)[okz]
            kk = np.argmax(np.sum(s * fail[:, :, None, :], axis=1), axis=1)[:, None, :]
            pick = np.take_along_axis(lit, kk, 1); pv = np.take_along_axis(v, kk, 1)[:, 0]
            up = np.minimum(np.take_along_axis(s, kk[:, None], 2)[:, :, 0] + 8, 63); new = np.where(pick >= V, 63 - up, up)
            for g in range(8):
                b = np.flatnonzero(bad[g]); u, ix = np.unique(pv[g, b], return_index=True); w = b[ix]
                nX[r, g][:, u] = np.where(fail[g][:, w], new[g][:, w], X[r, g][:, u])
            tot = np.sum(s, axis=1)
            sent.append((bad[:, 0::2] & bad[:, 1::2], np.where(tot[:, :, 1::2] > tot[:, :, 0::2], lit[:, :, 1::2], lit[:, :, 0::2])))
        for r in range(N):
            a = (r + 1 + t % 3) % N; both, joint = sent[r]
            for g in range(8):
                come = joint[g][:, both[g]]; dead = np.flatnonzero(F[a, g] == 4); n = min(come.shape[1], len(dead))
                nC[a, g][:, dead[:n]] = come[:, :n]; nF[a, g][dead[:n]] = 0
        X = nX; C = nC; F = nF
    return {"yx": X.reshape(N, 128, V).astype(np.float32).astype(BF), "yc": C.reshape(N, 128, K).astype(np.float32), "yf": F.astype(np.float32)}

@@ -1,0 +1,624 @@
+import numpy as np
+from concourse.mybir import dt, AluOpType, AxisListType, ActivationFunctionType
+
+A_, F_ = AluOpType, ActivationFunctionType
+N, V, K, LA, LF, RO, AS, FS = 8, 2048, 768, 256, 192, 3, 170, 255
+BRK = sorted(set([0] + [AS * t % K for t in range(RO)] + [FS * t % K for t in range(RO)])) + [K]
+SEG = []
+_p = 0
+for _a, _b in zip(BRK[:-1], BRK[1:]):
+    SEG.append((_a, _p, _b - _a))
+    _p += -(-(_b - _a) // 16) * 16
+NP = _p
+Q = NP // 16
+START = {a: p // 16 for a, p, n in SEG}
+XB = 256
+SB = XB + 2 * V
+WW = SB + 16
+FB0 = K
+LW = 2 * K + NP
+JW = 128
+CW = NP + JW
+JT = JW + 128
+OFF = 64.0
+CH = 64
+NA, NF = LA // CH, LF // CH
+
+SCRATCH = {
+    "W": ("sbuf", [128, WW], "bfloat16"), "S": ("sbuf", [128, 16 * LA], "bfloat16"), "M": ("sbuf", [128, 16 * LA], "bfloat16"),
+    "Z": ("sbuf", [128, 16 * LA], "bfloat16"), "S2": ("sbuf", [128, 16 * LF], "bfloat16"), "M2": ("sbuf", [128, 16 * LF], "bfloat16"),
+    "C0": ("sbuf", [128, CW], "float32"), "C1": ("sbuf", [128, CW], "float32"), "C2": ("sbuf", [128, CW], "float32"),
+    "C3": ("sbuf", [128, CW], "float32"), "CI": ("sbuf", [128, K], "int32"), "LN": ("sbuf", [128, LW], "float32"),
+    "YW": ("sbuf", [128, LW], "bfloat16"), "OA": ("sbuf", [128, LA], "uint16"), "OF": ("sbuf", [128, LF], "uint16"),
+    "FR": ("sbuf", [8, K], "int32"), "FRB": ("sbuf", [8, NP], "bfloat16"), "TI": ("sbuf", [128, 1], "int32"),
+    "TH": ("sbuf", [128, 1], "float32"), "TT": ("sbuf", [128, 1], "float32"), "AI": ("sbuf", [128, 2], "int32"),
+    "ONE": ("sbuf", [128, NP], "bfloat16"), "PM": ("sbuf", [16, 416], "bfloat16"), "QM": ("sbuf", [8, 128], "bfloat16"),
+    "QM0": ("sbuf", [8, 128], "bfloat16"), "LT": ("sbuf", [16, 256], "bfloat16"), "ID": ("sbuf", [128, 128], "bfloat16"),
+    "DM": ("sbuf", [128, NP], "bfloat16"), "TRI": ("sbuf", [128, 256], "bfloat16"), "BO": ("sbuf", [128, 128], "bfloat16"),
+    "BOF": ("sbuf", [128, 128], "float32"), "TS": ("sbuf", [128, 128], "bfloat16"), "SH": ("sbuf", [128, 128], "float32"),
+    "DF": ("sbuf", [128, 128], "float32"), "D1024": ("sbuf", [128, 128], "bfloat16"), "D8": ("sbuf", [128, 128], "bfloat16"),
+    "I4": ("sbuf", [128, 128], "bfloat16"), "NI4": ("sbuf", [128, 128], "bfloat16"), "I16": ("sbuf", [128, 8], "bfloat16"),
+    "NIN": ("sbuf", [128, 8], "bfloat16"), "O32": ("sbuf", [128, 128], "float32"), "KV": ("sbuf", [128, 1], "float32"),
+    "KC0": ("sbuf", [1, 256], "bfloat16"), "KC1": ("sbuf", [1, 256], "bfloat16"), "KW": ("sbuf", [128, 128], "bfloat16"),
+    "WC": ("sbuf", [128, 128], "bfloat16"), "L15": ("sbuf", [128, 16], "uint16"),
+    "LQI": ("sbuf", [128, 68], "int32"), "LQ": ("sbuf", [128, 52], "uint16"), "CL0": ("sbuf", [2, 128], "bfloat16"),
+    "CL": ("sbuf", [2, 128], "bfloat16"), "CR0": ("sbuf", [2, 2 * Q], "bfloat16"), "CR": ("sbuf", [2, 2 * Q], "bfloat16"),
+    "PD": ("sbuf", [128, Q], "float32"), "J0": ("sbuf", [128, Q], "float32"), "JD": ("sbuf", [128, 8], "float32"),
+    "U0": ("sbuf", [2 * Q, 2 * Q], "bfloat16"), "U1": ("sbuf", [2 * Q, 2 * Q], "bfloat16"), "U2": ("sbuf", [2 * Q, 2 * Q], "bfloat16"),
+    "UT": ("sbuf", [2 * Q, 2 * Q], "bfloat16"), "SEGM": ("sbuf", [128, 1024], "bfloat16"), "RST": ("sbuf", [128, 1024], "bfloat16"),
+    "DC": ("sbuf", [128, Q], "float32"), "T2": ("sbuf", [128, Q], "float32"), "T1": ("sbuf", [128, Q], "float32"),
+    "FW": ("sbuf", [128, NP], "bfloat16"), "FWS": ("sbuf", [128, NP], "bfloat16"), "FL": ("sbuf", [128, 3 * Q], "bfloat16"),
+    "GE": ("sbuf", [128, Q], "bfloat16"), "O1": ("sbuf", [2 * Q, 128], "bfloat16"), "O2": ("sbuf", [Q, 128], "bfloat16"),
+    "MM": ("sbuf", [128, 2 * Q], "float32"), "PS": ("sbuf", [128, 2 * Q], "float32"), "PL": ("sbuf", [128, 52], "uint16"),
+    "F1": ("sbuf", [128, Q], "float32"), "DD": ("sbuf", [128, Q], "float32"), "EN": ("sbuf", [128, 3 * Q], "float32"), "LX": ("sbuf", [128, LA], "float32"),
+    "NN": ("sbuf", [128, 4], "float32"), "RN": ("sbuf", [128, 4], "float32"),
+    "IXF": ("sbuf", [128, 2 * Q], "float32"),
+    "IX": ("sbuf", [128, 52], "uint16"), "FA": ("sbuf", [128, LA], "bfloat16"), "FA2": ("sbuf", [128, LF], "bfloat16"),
+    "VV": ("sbuf", [128, LA], "bfloat16"), "SG": ("sbuf", [128, LA], "bfloat16"), "DLV": ("sbuf", [128, LA], "float32"),
+    "DLS": ("sbuf", [128, LA], "bfloat16"), "DEO": ("sbuf", [128, 128], "float32"), "VI": ("sbuf", [128, LA], "bfloat16"),
+    "BT": ("sbuf", [128, 128], "bfloat16"), "INC": ("sbuf", [128, 128], "float32"), "IB": ("sbuf", [128, 128], "float32"),
+    "IBD": ("sbuf", [128, 128], "float32"), "IS": ("sbuf", [128, 128], "float32"), "JL": ("sbuf", [128, 8], "float32"),
+    "JLU": ("sbuf", [128, 8], "uint16"), "R": ("sbuf", [128, 256], "float32"), "EQ": ("sbuf", [128, 256], "bfloat16"),
+    "HV": ("sbuf", [128, 256], "float32"), "HS": ("sbuf", [128, 256], "bfloat16"), "VM": ("sbuf", [128, 256], "float32"),
+    "CS": ("sbuf", [128, 256], "float32"), "GL": ("sbuf", [128, 16], "uint16"), "VT": ("sbuf", [128, 256], "float32"),
+    "EE": ("sbuf", [128, 256], "bfloat16"), "ES": ("sbuf", [128, 256], "bfloat16"), "W1": ("sbuf", [128, 48], "float32"),
+    "SL": ("sbuf", [128, 32], "uint16"), "FSG": ("sbuf", [128, 256], "float32"), "XN": ("sbuf", [128, 256], "bfloat16"),
+    "XC": ("sbuf", [128, 256], "bfloat16"), "GT": ("sbuf", [128, 128], "bfloat16"), "PJ": ("sbuf", [128, 128], "float32"),
+    "JB": ("sbuf", [128, JT], "float32"), "SGA": ("sbuf", [128, 1], "float32"), "SGJ": ("sbuf", [128, LA], "float32"),
+    "YF8": ("sbuf", [8, NP], "float32"), "FBB": ("sbuf", [128, 64], "bfloat16"),
+    "RL": ("sbuf", [128, RO * JW], "float32"),
+}
+for _i in range(8):
+    SCRATCH["B%d" % _i] = ("psum", [128, 512], "float32")
+SEMAPHORES = ["sV", "sS", "sP", "sG"] + ["ld%d" % i for i in range(6)] + ["st%d" % i for i in range(14)] \
+    + [s + str(i) for s in ("arr", "ls", "ra", "na", "nl", "rn") for i in range(RO)]
+
+
+CYC, GAT, SCA, WAKE, SLACK = 0.001, 1.5, 3.8, 0.15, 0.1
+PLAN = {}
+SEED = [8067, 0.3]
+QW = {"V": 1.0, "S": 1.0, "P": 1.0, "G": 1.0, "Y": 1.0, "N": 1.0}
+NEGV = V
+
+
+def plan(ops):
+    n = len(ops)
+    pred = [dict() for _ in range(n)]
+    succ = [[] for _ in range(n)]
+    hist, last = {}, {}
+    for i, (q, tag, reads, writes, occ, dur, _) in enumerate(ops):
+        for w, lst in ((False, reads), (True, writes)):
+            for _a, buf, m in lst:
+                ps = buf in SCRATCH and SCRATCH[buf][0] == "psum"
+                for em, ew, j in hist.get(buf, []):
+                    same = ops[j][1] == tag
+                    if j == i or (not (em & m and (w or ew)) and not ps) or (ps and same and q == "V" and not (em & m and (w or ew))):
+                        continue
+                    lat = 0.0 if same and (q == "P" or not ew) else WAKE
+                    if pred[i].get(j, -1.0) < lat:
+                        pred[i][j] = lat
+        for w, lst in ((False, reads), (True, writes)):
+            for _a, buf, m in lst:
+                h = hist.setdefault(buf, [])
+                ps = buf in SCRATCH and SCRATCH[buf][0] == "psum"
+                if w and not ps:
+                    h[:] = [e for e in h if e[0] & ~m or e[2] == i]
+                h.append((m, w, i))
+                if ps and len(h) > 150:
+                    h[:] = h[-150:]
+    for i in range(n):
+        for j, lat in pred[i].items():
+            succ[j].append((i, lat))
+    pr = [0.0] * n
+    for i in range(n - 1, -1, -1):
+        pr[i] = ops[i][5] * QW[ops[i][0]] + max([lat + pr[k] for k, lat in succ[i]] + [0.0])
+    if SEED[0]:
+        pr = [float(x) for x in np.array(pr) + SEED[1] * np.random.default_rng(SEED[0]).random(n)]
+    left = [len(p) for p in pred]
+    est = [0.0] * n
+    ready, free = {}, {}
+    for i in range(n):
+        free[ops[i][0]] = 0.0
+        ready.setdefault(ops[i][0], [])
+        if not left[i]:
+            ready[ops[i][0]].append(i)
+    out = []
+    for _ in range(n):
+        best = None
+        for q in ready:
+            if ready[q]:
+                s0 = min(max(free[q], est[i]) for i in ready[q])
+                k = max((i for i in ready[q] if max(free[q], est[i]) <= s0 + SLACK), key=lambda i: (pr[i], -i))
+                s = max(free[q], est[k])
+                if best is None or s < best[0]:
+                    best = (s, q, k)
+        s, q, k = best
+        ready[q].remove(k)
+        free[q] = s + ops[k][4]
+        out.append(k)
+        for i, lat in succ[k]:
+            est[i] = max(est[i], s + ops[k][5] + lat)
+            left[i] -= 1
+            if not left[i]:
+                ready[ops[i][0]].append(i)
+    return out
+
+
+def route(topo, src, dst):
+    if topo.may_write(src, dst):
+        return None
+    c = [r for r in topo.cores_of(src) if r != src and topo.may_write(r, dst)]
+    return sorted(c, key=lambda r: (topo.die(r) != topo.die(src), r))[0]
+
+
+def emask(topo, src, dst):
+    m = 0
+    for e in topo.engines(src, dst)[:8]:
+        m |= 1 << e
+    return m
+
+
+def relay_program(g, core, T, topo):
+    for r in range(N):
+        src = T.cores[r]
+        for t in range(RO):
+            dst = T.cores[(r + 1 + t % 3) % N]
+            if route(topo, src, dst) == core:
+                rid, pid = topo.addr(dst, core)
+                m = emask(topo, core, dst)
+                g.wait_ge(T.sem["rn%d" % t], 8)
+                g.remote_dma(T.NN[:, t:t + 1], T.RN[:, t:t + 1], T.sem["na%d" % t], T.sem["nl%d" % t], pid, rid, m)
+                g.wait_ge(T.sem["ra%d" % t], 8)
+                g.remote_dma(T["C%d" % t][:, NP:CW], T.RL[:, t * JW:(t + 1) * JW], T.sem["arr%d" % t], T.sem["ls%d" % t], pid, rid, m)
+    for r in range(N):
+        for t in range(RO):
+            if route(topo, T.cores[r], T.cores[(r + 1 + t % 3) % N]) == core:
+                g.wait_ge(T.sem["nl%d" % t], 8)
+                g.wait_ge(T.sem["ls%d" % t], 8)
+
+
+def rank_program(g, core, T, topo):
+    rank = T.rank_of(core)
+    if rank is None:
+        relay_program(g, core, T, topo)
+        return
+    eng = {"V": g.vector, "S": g.scalar, "P": g.tensor, "G": g, "Y": g.sync}
+    cnt = {"V": 0, "S": 0, "P": 0, "G": 0}
+    known = {q: {} for q in eng}
+    hist = {}
+    bits = {}
+    serial = [0]
+
+    def cols(lo, n, step):
+        k = (lo, n, step)
+        if k not in bits:
+            m = 0
+            for i in range(n):
+                m |= 1 << (lo + i * step)
+            bits[k] = m
+        return bits[k]
+
+    def a(buf, lo=0, n=None, step=1, p=None, p0=0):
+        if n is None:
+            n = T[buf].shape[1] - lo
+        p = T[buf].shape[0] if p is None else p
+        return (T[buf][p0:p0 + p, lo:lo + (n - 1) * step + 1:step] if step > 1 else T[buf][p0:p0 + p, lo:lo + n], buf, cols(lo, n, step))
+
+    def ind(w, o):
+        return (w[0].indirect(o[0]), w, o)
+
+    def acc(x):
+        return [x] if len(x) == 3 and isinstance(x[1], str) else [x[1], x[2]]
+
+    def need(q, tag, reads, writes):
+        want = {}
+        for w, lst in ((False, reads), (True, writes)):
+            for _, buf, m in lst:
+                ps = buf[0] == "B" and buf[1:].isdigit()
+                for (em, ew, eq, sem, val, snap) in hist.get(buf, []):
+                    hit = em & m
+                    if ps and eq != tag:
+                        pass
+                    elif not hit or not (w or ew):
+                        continue
+                    elif eq == tag and (not ew or (w and q == "P")):
+                        continue
+                    if known[q].get(sem, 0) >= val:
+                        continue
+                    if sem not in want or want[sem][0] < val:
+                        want[sem] = (val, snap)
+        for sem in list(want):
+            val = want[sem][0]
+            if any(o != sem and want[o][1].get(sem, 0) >= val for o in want):
+                del want[sem]
+        for sem in want:
+            val, snap = want[sem]
+            eng[q].wait_ge(T.sem[sem], val)
+            for k, x in snap.items():
+                if known[q].get(k, 0) < x:
+                    known[q][k] = x
+            known[q][sem] = max(known[q].get(sem, 0), val)
+
+    def note(tag, reads, writes, sem, val, snap):
+        for _, buf, m in writes:
+            h = hist.setdefault(buf, [])
+            h[:] = [e for e in h if e[0] & ~m] if not (buf[0] == "B" and buf[1:].isdigit()) else [e for e in h if e[2] != tag or e[0] & ~m]
+            h.append((m, True, tag, sem, val, snap))
+        for _, buf, m in reads:
+            h = hist.setdefault(buf, [])
+            h[:] = [e for e in h if e[1] or e[2] != tag or e[0] & ~m]
+            h.append((m, False, tag, sem, val, snap))
+
+    ops = []
+
+    def run(q, fn, out, ins, cost):
+        writes = acc(out)[:1] if isinstance(out, tuple) else out
+        reads = acc(out)[1:] if isinstance(out, tuple) else []
+        for x in ins:
+            reads = reads + acc(x)
+
+        def issue():
+            need(q, q, reads, writes)
+            cnt[q] += 1
+            fn().then_inc(T.sem["s" + q], 1)
+            snap = dict(known[q])
+            snap["s" + q] = cnt[q]
+            note(q, reads, writes, "s" + q, cnt[q], snap)
+        ops.append((q, q, reads, writes, cost, cost, issue))
+
+    def dma(q, out, in_, sem, reads, writes, dur=2.5):
+        serial[0] += 1
+        tag = "d%d" % serial[0]
+
+        def issue():
+            need(q, None, reads, writes)
+            eng[q].dma_start(out, in_).then_inc(T.sem[sem], 16)
+            note(tag, reads, writes, sem, 16, dict(known[q]))
+        ops.append((q, tag, reads, writes, 0.05, dur, issue))
+
+    def cost(out, ins, per):
+        for x in ins:
+            if isinstance(x[1], tuple):
+                return 0.05 + GAT * CYC * 16 * bin(x[2][2]).count("1")
+        if isinstance(out[1], tuple):
+            return 0.05 + SCA * CYC * 16 * bin(out[2][2]).count("1")
+        two = all(SCRATCH[x[1]][2] in ("bfloat16", "uint16") for x in [out] + ins)
+        return CYC * max(64, bin(out[2]).count("1") * (per if per == 2 or not two else 0.5))
+
+    def ap(x):
+        return x[0]
+
+    def copy(out, in_):
+        run("V", lambda: g.vector.tensor_copy(ap(out), ap(in_)), out, [in_], cost(out, [in_], 1))
+
+    def tt(out, x, y, op):
+        ps = any(isinstance(z[1], str) and SCRATCH[z[1]][0] == "psum" for z in (x, y))
+        run("V", lambda: g.vector.tensor_tensor(ap(out), ap(x), ap(y), op), out, [x, y], cost(out, [x, y], 1 if ps else 2))
+
+    def ts(out, x, s1, op0, s2=None, op1=None):
+        ins = [x] + [s for s in (s1, s2) if isinstance(s, tuple)]
+        u1 = s1[0] if isinstance(s1, tuple) else s1
+        if op1 is None:
+            run("V", lambda: g.vector.tensor_scalar(ap(out), ap(x), u1, None, op0), out, ins, cost(out, [x], 1))
+        else:
+            run("V", lambda: g.vector.tensor_scalar(ap(out), ap(x), u1, s2, op0, op1), out, ins, cost(out, [x], 1))
+
+    def scan(out, d0, d1, ini, op0, op1):
+        run("V", lambda: g.vector.tensor_tensor_scan(ap(out), ap(d0), ap(d1), ini, op0, op1), out, [d0, d1], cost(out, [d0, d1], 1))
+
+    def fill(out, c):
+        run("V", lambda: g.vector.memset(ap(out), c), out, [], cost(out, [], 1))
+
+    def act(out, x, func, bias=0.0, scale=1.0, accum=None):
+        ins = [x] + ([bias] if isinstance(bias, tuple) else [])
+        b = bias[0] if isinstance(bias, tuple) else bias
+        if accum is None:
+            if isinstance(out[1], tuple):
+                run("S", lambda: g.scalar.activation(ap(out), ap(x), func), out, ins, cost(out, [x], 1))
+                return
+            c = cost(out, [x], 2) if isinstance(x[1], tuple) else CYC * max(64, bin(out[2]).count("1"))
+            run("S", lambda: g.scalar.activation(ap(out), ap(x), func, bias=b, scale=scale), out, ins, c)
+        else:
+            run("S", lambda: g.scalar.activation(ap(out), ap(x), func, bias=b, scale=scale, accum_out=ap(accum)), [out, accum], ins,
+                CYC * bin(out[2]).count("1"))
+
+    def mm(out, l, r, start, stop):
+        c = CYC * max(min(64, bin(l[2]).count("1")), bin(r[2]).count("1")) * (4 if SCRATCH[l[1]][2] == "float32" else 1)
+        run("P", lambda: g.tensor.matmul(ap(out), ap(l), ap(r), start, stop), out, [l, r], c)
+
+    def iota(out, pat, base, cm):
+        run("G", lambda: g.iota(ap(out), pat, base, cm, allow_small_or_imprecise_dtypes=True), out, [], 0.13 + 2 * CYC * bin(out[2]).count("1"))
+
+    def sel(out, x, pat, op, fl, base, cm):
+        run("G", lambda: g.affine_select(ap(out), ap(x), pat, op, fl, base, cm), out, [x], 0.17 + 2 * CYC * bin(out[2]).count("1"))
+
+    def send(t, src, land, relay, arr, ra, ls, lat):
+        dst = T.cores[(rank + 1 + t % 3) % N]
+        first = route(topo, core, dst)
+        to = dst if first is None else first
+        net = ("", "net" + arr, 1)
+
+        def issue():
+            need("G", None, [src], [])
+            rid, pid = topo.addr(to, core)
+            g.remote_dma(land[0] if first is None else relay, src[0], T.sem[(arr if first is None else ra) + str(t)], T.sem[ls + str(t)],
+                         pid, rid, emask(topo, core, to))
+            note("r%s%d" % (ls, t), [src], [], ls + str(t), 8, dict(known["G"]))
+        ops.append(("G", "r%s%d" % (ls, t), [src], [net], 0.3, 2.0, issue))
+        ops.append(("N", "q%s%d" % (arr, t), [net], [land], 0.0, lat * (1 if first is None else 2),
+                    lambda: note("q%s%d" % (arr, t), [], [land], arr + str(t), 8, {})))
+
+    dma("Y", T.FR[:], T.fr[:], "ld0", [], [a("FR")], 2.2)
+    dma("Y", T.CI[:], T.cl[:], "ld2", [], [a("CI")], 4.0)
+    dma("Y", T.W[:, XB:XB + V], T.xv[:], "ld3", [], [a("W", XB, V)], 6.0)
+    dma("Y", T.TI[:], T.th[:], "ld1", [], [a("TI")], 6.0)
+    fill(a("VM", 0, 16), 200.0)
+    act(a("W", SB, 16), a("VM", 0, 16), F_.Silu)
+
+    fill(a("ONE"), 1.0)
+    fill(a("FRB"), 8.0)
+    sel(a("PM"), a("ONE", 0, 416, p=16), [[0, 26], [1, 16]], A_.is_equal, 0.0, 0, -1)
+    sel(a("QM0"), a("ONE", 0, 128, p=8), [[1, 128]], A_.is_ge, 0.0, 0, -16)
+    sel(a("QM"), a("QM0"), [[-1, 128]], A_.is_ge, 0.0, 15, 16)
+    fill(a("SEGM"), 1.0)
+    fill(a("SEGM", 0, 64, 16), 0.0)
+    mm(a("B1", 0, 416), a("PM", 0, 128), a("PM", 0, 416), True, True)
+    mm(a("B2", 0, NP - 416), a("PM", 0, 128), a("PM", 0, NP - 416), True, True)
+    mm(a("B3", 0, 128), a("QM"), a("QM"), True, True)
+    copy(a("DM", 0, 416), a("B1", 0, 416))
+    act(a("DM", 416, NP - 416), a("B2", 0, NP - 416), F_.Identity)
+    copy(a("BO"), a("B3", 0, 128))
+    for s0, p0, n in SEG:
+        copy(a("FRB", p0, n), a("FR", s0, n))
+    mm(a("B4", 0, 512), a("QM"), a("FRB", 0, 512), True, True)
+    mm(a("B5", 0, NP - 512), a("QM"), a("FRB", 512, NP - 512), True, True)
+    tt(a("FW", 0, 512), a("B4", 0, 512), a("DM", 0, 512), A_.mult)
+    tt(a("FW", 512, NP - 512), a("B5", 0, NP - 512), a("DM", 512, NP - 512), A_.mult)
+    scan(a("FWS"), a("SEGM", 0, NP), a("FW"), 0.0, A_.mult, A_.add)
+    copy(a("T2"), a("FWS", 15, Q, 16))
+    sel(a("TS"), a("BO"), [[1, 128]], A_.is_ge, 0.0, -1, -1)
+    iota(a("CL0"), [[0, 8], [1, 16]], 0, 0)
+    sel(a("CL"), a("CL0"), [[0, 128]], A_.is_gt, 1.0, 0, 1)
+    iota(a("CR0", 0, Q), [[-16, Q]], -2 * K, 0)
+    iota(a("CR0", Q, Q), [[-16, Q]], -K, 0)
+    sel(a("CR"), a("CR0"), [[0, 2 * Q]], A_.is_equal, -1.0, 0, 1)
+
+    def order(t):
+        for b, s in ((0, START[AS * t % K]), (Q, START[FS * t % K])):
+            u = "U%d" % t
+            n = Q - s
+            sel(a("UT", b + s, n, p=2 * Q), a("ONE", 0, n, p=2 * Q), [[1, n]], A_.is_gt, 0.0, b + s, -1)
+            sel(a(u, b + s, n), a("UT", b + s, n), [[0, n]], A_.is_ge, 0.0, -(b + s), 1)
+            if s:
+                sel(a(u, b, s), a("ONE", 0, s, p=2 * Q), [[0, s]], A_.is_ge, 0.0, b + Q - 1, -1)
+                sel(a("UT", b, s), a(u, b, s), [[0, s]], A_.is_ge, 0.0, -(b + s), 1)
+                sel(a(u, b, s), a("UT", b, s), [[-1, s]], A_.is_ge, 1.0, -b, 1)
+                if b:
+                    sel(a("UT", b, s), a(u, b, s), [[0, s]], A_.is_ge, 0.0, -b, 1)
+                    sel(a(u, b, s), a("UT", b, s), [[0, s]], A_.is_ge, 0.0, -b, 1)
+
+    order(0)
+    mm(a("B6", 0, Q), a("CL"), a("CR", 0, Q), True, True)
+    ts(a("PD"), a("B6", 0, Q), -1.0, A_.mult)
+    ts(a("J0"), a("PD"), -2.0 * K, A_.add)
+    ts(a("JD"), a("J0", 0, 8), float(JW - 512), A_.add)
+    iota(a("LN", 0, LA), [[0, LA]], 2 * V + int(OFF), 0)
+    iota(a("LN", FB0, LF), [[0, LF]], 2 * V + int(OFF), 0)
+
+    def lists(t):
+        ts(a("FL", 0, Q), a("T2"), 0.0, A_.is_le)
+        ts(a("GE"), a("T2"), 0.0, A_.is_gt)
+        ts(a("FL", 2 * Q, Q), a("T2"), 3.5, A_.is_ge)
+        tt(a("FL", Q, Q), a("GE"), a("FL", 2 * Q, Q), A_.subtract)
+        mm(a("B7", 0, 128, p=2 * Q), a("FL", 0, 2 * Q), a("BO"), True, True)
+        act(a("O1"), a("B7", 0, 128, p=2 * Q), F_.Identity)
+        mm(a("B6", 0, 2 * Q), a("TS"), a("FL", 0, 2 * Q), True, False)
+        mm(a("B6", 0, 2 * Q), a("CL"), a("CR"), False, False)
+        mm(a("B6", 0, 2 * Q), a("O1"), a("U%d" % t), False, True)
+        ts(a("F1"), a("T2"), 0.0, A_.max, 1.0, A_.add)
+        tt(a("MM"), a("B6", 0, 2 * Q), a("FL", 0, 2 * Q), A_.mult)
+        tt(a("PS", 0, Q), a("MM", 0, Q), a("MM", Q, Q), A_.add)
+        tt(a("PS", Q, Q), a("PS", 0, Q), a("PD"), A_.add)
+        copy(a("PL", 0, Q), a("PS", Q, Q))
+        act(ind(a("LN"), a("PL", 0, Q)), a("C%d" % t, 0, NP), F_.Silu)
+        ts(a("OA"), a("LN", 0, LA), 0.25 - OFF, A_.add)
+        ts(a("OF"), a("LN", FB0, LF), 0.25 - OFF, A_.add)
+        mm(a("B5", 0, 128, p=Q), a("FL", 2 * Q, Q), a("BO"), True, True)
+        act(a("O2"), a("B5", 0, 128, p=Q), F_.Identity)
+        mm(a("B5", 128, Q), a("TS"), a("FL", 2 * Q, Q), True, False)
+        mm(a("B5", 128, Q), a("NI4"), a("FL", 2 * Q, Q), False, False)
+        mm(a("B5", 128, Q), a("O2"), a("U0", 0, Q, p=Q), False, True)
+
+    def gather(q, c, out, off):
+        w = ind(a("W", XB, WW - XB), a(off, CH * c, CH))
+        if q == "V":
+            copy(a(out, 16 * CH * c, 16 * CH), w)
+        else:
+            act(a(out, 16 * CH * c, 16 * CH), w, F_.Identity)
+
+    def negate(lo, n, q):
+        if q == "V":
+            ts(a("W", XB + V + lo, n), a("W", XB + lo, n), -1.0, A_.mult, 63.0, A_.add)
+        else:
+            act(a("W", XB + V + lo, n), a("W", XB + lo, n), F_.Identity, 63.0, -1.0)
+
+    for s0, p0, n in SEG:
+        fill(a("C0", p0 + n, -(-n // 16) * 16 - n), OFF)
+        ts(a("C0", p0, n), a("CI", s0, n), OFF, A_.add)
+    sel(a("ID"), a("ONE", 0, 128), [[-1, 128]], A_.is_equal, 0.0, 0, 1)
+    ts(a("NI4"), a("ID"), -4096.0, A_.mult)
+    lists(0)
+    negate(0, V, "S")
+    fill(a("W", 0, XB), 0.0)
+    fill(a("RST"), 64.0)
+    fill(a("RST", 0, 64, 16), 8192.0)
+    copy(a("TH"), a("TI"))
+    copy(a("TT"), a("TI"))
+    pads = 0
+    for s0, p0, n in SEG:
+        fill(a("DC", p0 // 16, -(-n // 16)), 4096.0 - 513.0 - pads)
+        pads += -(-n // 16) * 16 - n
+    ts(a("PS", 0, Q), a("T2"), 6.0, A_.is_ge, 4096.0, A_.mult)
+    tt(a("DC"), a("DC"), a("PS", 0, Q), A_.add)
+    fill(a("YW"), 1.0)
+    fill(a("FBB"), 0.0)
+    fill(a("JB"), 0.0)
+    fill(a("O32"), 1.0 / 32)
+    copy(a("BOF"), a("BO"))
+    sel(a("SH"), a("BOF"), [[-1, 128]], A_.is_equal, 0.0, -1, 1)
+    tt(a("DF"), a("ID"), a("SH"), A_.subtract)
+    ts(a("D1024"), a("DF"), -1024.0, A_.mult)
+    ts(a("D8"), a("DF"), -8.0, A_.mult)
+    ts(a("I4"), a("ID"), 4096.0, A_.mult)
+    ts(a("I16"), a("BO", 0, 8, 16), 16.0, A_.mult)
+    ts(a("NIN"), a("BO", 0, 8, 16), -1.0, A_.mult)
+    ts(a("KV"), a("DM", 15, 1), float(XB - V // 2 - 4096 - OFF), A_.mult)
+    iota(a("KC0"), [[0, 16], [-16384, 16]], 262144, 0)
+    iota(a("KC1"), [[0, 16], [-1, 16]], 15, 0)
+    iota(a("KW"), [[0, 8], [1024, 16]], -16384, 0)
+    tt(a("WC"), a("BO"), a("KW"), A_.mult)
+    iota(a("LQI", 52, 16), [[16, 16]], 15, 0)
+    copy(a("L15"), a("LQI", 52, 16))
+    iota(a("LQI", 0, 52), [[1, 52]], 0, 0)
+    copy(a("LQ"), a("LQI", 0, 52))
+    sel(a("LT"), a("ONE", 0, 256, p=16), [[0, 16], [-1, 16]], A_.is_ge, 0.0, -1, 1)
+    mm(a("B4", 0, 256), a("PM", 0, 128), a("LT"), True, True)
+    act(a("TRI"), a("B4", 0, 256), F_.Identity)
+
+    for t in range(RO):
+        C = "C%d" % t
+        gather("S", 0, "S", "OA")
+        gather("V", 1, "S", "OA")
+        gather("S", 2, "S", "OA")
+        gather("S", 3, "S", "OA")
+        ts(a("LX"), a("OA"), OFF, A_.add)
+        tt(a("DEO"), a("LX", 1, 128, 2), a("LX", 0, 128, 2), A_.subtract)
+        tt(a("DD"), a("B5", 128, Q), a("DC"), A_.add)
+        ts(a("EN", Q, Q), a("DD"), 513.0 + NP, A_.add)
+        tt(a("EN", 0, Q), a("J0"), a("EN", Q, Q), A_.subtract)
+        act(a("SG"), a("LN", 0, LA), F_.Sign, 0.5 - V - OFF)
+        for h in range(2):
+            mm(a("B2", 128 * h, 128), a("DF"), a("LX", h, 128, 2), True, False)
+            mm(a("B2", 128 * h, 128), a("D1024"), a("SG", h, 128, 2), False, True)
+            mm(a("B2", 256 + 128 * h, 128), a("D8"), a("SG", h, 128, 2), True, True)
+        act(a("DLV"), a("B2", 0, 256), F_.Identity, a("KV"))
+        act(a("DLS"), a("B2", 256, 256), F_.Identity)
+        mm(a("B0", 0, 256), a("ONE", 0, 128, p=1), a("KC0"), True, False)
+        for c in range(NF):
+            gather("S", c, "S2", "OF")
+        for c in range(NA):
+            lo = 16 * CH * c
+            scan(a("M", lo, 16 * CH), a("SEGM"), a("S", lo, 16 * CH), 0.0, A_.mult, A_.max)
+            ts(a("FA", CH * c, CH), a("M", lo + 15, CH, 16), a("TT"), A_.is_lt)
+            ts(a("VV", CH * c, CH), a("FA", CH * c, CH), 2048.0, A_.mult, -1024.0, A_.add)
+            tt(a("S", lo, CH, 16), a("VV", CH * c, CH), a("M", lo, CH, 16), A_.min)
+            scan(a("Z", lo, 16 * CH), a("RST"), a("S", lo, 16 * CH), 0.0, A_.add, A_.min)
+            if c == NA - 1:
+                mm(a("B4", 0, LA), a("BO"), a("FA"), True, True)
+            for h in range(2):
+                mm(a("B0", 128 * h, 128, p=32, p0=32 * c), a("FA", CH * c + h, 32, 2), a("WC"), False, False)
+            for h in range(2):
+                for k in range(16):
+                    mm(a("B0", 128 * h + k, 8, 16, p=32, p0=32 * c), a("Z", lo + 16 * h + k, 32, 32), a("I16"), False, False)
+        mm(a("B0", 0, 256), a("ONE", 0, 128, p=1), a("KC1"), False, True)
+        ts(a("VI"), a("B4", 0, LA), 3.5, A_.is_gt)
+        act(a("YW", 0, LA), a("B4", 0, LA), F_.Relu, -25.0, 8.0)
+        act(a("SGJ"), a("B4", 0, LA), F_.Sign, -3.5, 1.0, a("SGA"))
+        tt(a("BT"), a("VI", 0, 128, 2), a("VI", 1, 128, 2), A_.mult)
+        scan(a("INC"), a("ONE", 0, 128), a("BT"), -513.0, A_.mult, A_.add)
+        tt(a("IB"), a("INC"), a("BT"), A_.mult)
+        tt(a("IBD"), a("IB"), a("DM", 0, 128), A_.mult)
+        scan(a("IS"), a("SEGM", 0, 128), a("IBD"), 0.0, A_.mult, A_.add)
+        tt(a("JL"), a("IS", 15, 8, 16), a("JD"), A_.min)
+        ts(a("JLU"), a("JL"), 512.0, A_.add)
+        send(t, a("INC", 127, 1), a("NN", t, 1), T.RN[:, t:t + 1], "na", "rn", "nl", 2.0)
+        scan(a("R"), a("SEGM", 0, 256), a("B0", 0, 256), 0.0, A_.mult, A_.max)
+        scan(a("VT"), a("SEGM", 0, 256), a("B0", 0, 256), 0.0, A_.mult, A_.max)
+        tt(a("EQ"), ind(a("R"), a("L15")), a("VT"), A_.is_equal)
+        for h in range(2):
+            mm(a("B3", 128 * h, 128), a("EQ", 128 * h, 128), a("ID"), True, True)
+        scan(a("M2", 0, 1024), a("SEGM"), a("S2", 0, 1024), 0.0, A_.mult, A_.max)
+        tt(a("HV"), a("B3", 0, 256), a("DLV"), A_.mult)
+        tt(a("HS"), a("B3", 0, 256), a("DLS"), A_.mult)
+        for h in range(2):
+            mm(a("B1", h, 128, 2), a("BOF"), a("HV", 128 * h, 128), True, False)
+            mm(a("B1", h, 128, 2), a("I4"), a("VI", h, 128, 2), False, True)
+        for h in range(2):
+            mm(a("B7", h, 128, 2), a("BO"), a("HS", 128 * h, 128), True, True)
+        scan(a("M2", 1024, 1024), a("SEGM"), a("S2", 1024, 1024), 0.0, A_.mult, A_.max)
+        for k in range(16):
+            mm(a("B2", k, 8, 16), a("S", 16 + k, 128, 32) if k else a("M", 16, 128, 32), a("BO", 0, 8, 16), True, False)
+            mm(a("B2", k, 8, 16), a("S", k, 128, 32) if k else a("M", 0, 128, 32), a("NIN"), False, True)
+        tt(a("VM"), a("B1", 0, 256), a("DM", 0, 256), A_.mult)
+        tt(a("VT"), a("B1", 0, 256), a("TRI"), A_.mult)
+        scan(a("CS"), a("SEGM", 0, 256), a("VM"), 0.0, A_.mult, A_.add)
+        tt(a("FSG"), a("B7", 0, 256), a("FA"), A_.mult)
+        tt(a("EE"), ind(a("CS"), a("L15")), a("VT"), A_.is_equal)
+        copy(a("GL"), a("CS", 15, 16, 16))
+        scan(a("ES"), a("SEGM", 0, 256), a("EE"), 0.0, A_.mult, A_.add)
+        ts(a("W1", 0, 16), a("ES", 15, 16, 16), -8192.0, A_.mult)
+        tt(a("W1", 16, 16), a("W1", 0, 16), a("CS", 15, 16, 16), A_.add)
+        tt(a("W1", 32, 16), a("W1", 16, 16), a("J0", 0, 16), A_.max)
+        copy(a("SL", 0, 16, 2), a("W1", 32, 16))
+        ts(a("GT"), a("B2", 0, 128), 0.0, A_.is_gt)
+        mm(a("B3", 256, 128), a("GT"), a("ID"), True, True)
+        tt(a("XN"), ind(a("W", 0, XB + V), a("GL")), a("FSG"), A_.add)
+        tt(a("PJ"), a("B3", 256, 128), a("DEO"), A_.mult)
+        tt(ind(a("JB"), a("JLU")), a("PJ"), a("LX", 0, 128, 2), A_.add)
+        send(t, a("JB", 0, JW), a(C, NP, JW), T.RL[:, t * JW:(t + 1) * JW], "arr", "ra", "ls", 2.2)
+        ts(a("XC"), a("XN"), 0.0, A_.max, 63.0, A_.min)
+        for b in range(15, -1, -1):
+            copy(ind(a("W", 0, XB + V), a("SL", 2 * b, 1)), a("XC", 16 * b, 16))
+        if t < RO - 1:
+            iota(a("LN", 0, LA), [[0, LA]], 2 * V + int(OFF), 0)
+            iota(a("LN", FB0, LF), [[0, LF]], 2 * V + int(OFF), 0)
+            order(t + 1)
+            if NEGV:
+                negate(0, NEGV, "V")
+            if NEGV < V:
+                negate(NEGV, V - NEGV, "S")
+        else:
+            dma("Y", T.yx[:], T.W[:, XB:XB + V], "st0", [a("W", XB, V)], [], 4.5)
+        scan(a("M2", 2048, 1024), a("SEGM"), a("S2", 2048, 1024), 0.0, A_.mult, A_.max)
+        ts(a("FA2"), a("M2", 15, LF, 16), a("TT"), A_.is_lt)
+        mm(a("B6", 0, LF), a("BO"), a("FA2"), True, True)
+        act(a("YW", FB0, LF), a("B6", 0, LF), F_.Relu, -25.0, 8.0)
+        if t < RO - 1:
+            mm(a("B7", 256, 1), a("O32"), a("SGA"), True, True)
+            copy(a("AI", 0, 1), a("B7", 256, 1))
+            ts(a("AI", 1, 1), a("AI", 0, 1), 3, A_.bitwise_and)
+            tt(a("TT"), a("TH"), a("AI", 1, 1), A_.add)
+        tt(a("FW"), ind(a("YW"), a("PL", 0, Q)), a("DM"), A_.mult)
+        ts(a("EN", 2 * Q, Q), a("DD"), a("NN", t, 1), A_.is_ge)
+        tt(a("IXF", 0, Q), a("EN", 0, Q), a("EN", 2 * Q, Q), A_.mult)
+        tt(a("IXF", Q, Q), a("IXF", 0, Q), a("EN", Q, Q), A_.add)
+        copy(a("IX", 0, Q), a("IXF", Q, Q))
+        act(a("C%d" % (t + 1), 0, NP), ind(a(C), a("IX", 0, Q)), F_.Identity, -OFF if t == RO - 1 else 0.0)
+        scan(a("FWS"), a("SEGM", 0, NP), a("FW"), 0.0, A_.mult, A_.add)
+        tt(a("T1"), a("F1"), a("FWS", 15, Q, 16), A_.subtract)
+        tt(a("T2"), a("T1"), a("EN", 2 * Q, Q), A_.mult)
+        if t < RO - 1:
+            lists(t + 1)
+    for i, (s0, p0, n) in enumerate(SEG):
+        dma("Y" if i % 2 else "S", T.yc[:, s0:s0 + n], T.C3[:, p0:p0 + n], "st%d" % (1 + i), [a("C3", p0, n)], [])
+    ts(a("FBB", 0, Q), a("T2"), 0.0, A_.max)
+    tt(a("FW"), ind(a("FBB"), a("LQ", 0, Q)), a("DM"), A_.mult)
+    mm(a("B4", 0, 512, p=8), a("BO", 0, 8, 16), a("FW", 0, 512), True, True)
+    mm(a("B6", 0, NP - 512, p=8), a("BO", 0, 8, 16), a("FW", 512, NP - 512), True, True)
+    act(a("YF8", 0, 512), a("B4", 0, 512, p=8), F_.Identity)
+    copy(a("YF8", 512, NP - 512), a("B6", 0, NP - 512, p=8))
+    for i, (s0, p0, n) in enumerate(SEG):
+        dma("Y" if i % 2 else "S", T.yf[:, s0:s0 + n], T.YF8[:, p0:p0 + n], "st%d" % (6 + i), [a("YF8", p0, n)], [])
+    if "order" not in PLAN:
+        PLAN["order"] = plan(ops)
+    for i in PLAN["order"]:
+        ops[i][6]()
+    for q in cnt:
+        g.wait_ge(T.sem["s" + q], cnt[q])
+    for i in range(4):
+        g.wait_ge(T.sem["ld%d" % i], 16)
+    for i in range(11):
+        g.wait_ge(T.sem["st%d" % i], 16)
+    for t in range(RO):
+        for s in ("ls", "arr", "nl", "na"):
+            g.wait_ge(T.sem[s + str(t)], 8)

@@ -3,96 +3,65 @@ from concourse.mybir import dt, AluOpType, AxisListType, ActivationFunctionType
 
 A_, F_ = AluOpType, ActivationFunctionType
 N, V, K, LA, LF, RO, AS, FS = 8, 2048, 768, 256, 192, 3, 170, 255
-BRK = sorted(set([0] + [AS * t % K for t in range(RO)] + [FS * t % K for t in range(RO)])) + [K]
-SEG = []
-_p = 0
-for _a, _b in zip(BRK[:-1], BRK[1:]):
-    SEG.append((_a, _p, _b - _a))
-    _p += -(-(_b - _a) // 16) * 16
-NP = _p
-Q = NP // 16
-START = {a: p // 16 for a, p, n in SEG}
-XB = 256
+Q = K // 16
+XB = 16
 SB = XB + 2 * V
 WW = SB + 16
-FB0 = K
-LW = 2 * K + NP
+LW = 2 * K + 880
 JW = 128
-CW = NP + JW
-JT = JW + 128
+CW = JW + K
 OFF = 64.0
 CH = 64
 NA, NF = LA // CH, LF // CH
+EPS, BIGM, MAGIC = 2.0 ** -60, 2.0 ** 70, 1.5 * 2.0 ** 29
+H = "float16"
 
-SCRATCH = {
-    "W": ("sbuf", [128, WW], "bfloat16"), "S": ("sbuf", [128, 16 * LA], "bfloat16"), "M": ("sbuf", [128, 16 * LA], "bfloat16"),
-    "Z": ("sbuf", [128, 16 * LA], "bfloat16"), "S2": ("sbuf", [128, 16 * LF], "bfloat16"), "M2": ("sbuf", [128, 16 * LF], "bfloat16"),
-    "C0": ("sbuf", [128, CW], "float32"), "C1": ("sbuf", [128, CW], "float32"), "C2": ("sbuf", [128, CW], "float32"),
-    "C3": ("sbuf", [128, CW], "float32"), "CI": ("sbuf", [128, K], "int32"), "LN": ("sbuf", [128, LW], "float32"),
-    "YW": ("sbuf", [128, LW], "bfloat16"), "OA": ("sbuf", [128, LA], "uint16"), "OF": ("sbuf", [128, LF], "uint16"),
-    "FR": ("sbuf", [8, K], "int32"), "FRB": ("sbuf", [8, NP], "bfloat16"), "TI": ("sbuf", [128, 1], "int32"),
-    "TH": ("sbuf", [128, 1], "float32"), "TT": ("sbuf", [128, 1], "float32"), "AI": ("sbuf", [128, 2], "int32"),
-    "ONE": ("sbuf", [128, NP], "bfloat16"), "PM": ("sbuf", [16, 416], "bfloat16"), "QM": ("sbuf", [8, 128], "bfloat16"),
-    "QM0": ("sbuf", [8, 128], "bfloat16"), "LT": ("sbuf", [16, 256], "bfloat16"), "ID": ("sbuf", [128, 128], "bfloat16"),
-    "DM": ("sbuf", [128, NP], "bfloat16"), "TRI": ("sbuf", [128, 256], "bfloat16"), "BO": ("sbuf", [128, 128], "bfloat16"),
-    "BOF": ("sbuf", [128, 128], "float32"), "TS": ("sbuf", [128, 128], "bfloat16"), "SH": ("sbuf", [128, 128], "float32"),
-    "DF": ("sbuf", [128, 128], "float32"), "D1024": ("sbuf", [128, 128], "bfloat16"), "D8": ("sbuf", [128, 128], "bfloat16"),
-    "I4": ("sbuf", [128, 128], "bfloat16"), "NI4": ("sbuf", [128, 128], "bfloat16"), "I16": ("sbuf", [128, 8], "bfloat16"),
-    "NIN": ("sbuf", [128, 8], "bfloat16"), "O32": ("sbuf", [128, 128], "float32"), "KV": ("sbuf", [128, 1], "float32"),
-    "KC0": ("sbuf", [1, 256], "bfloat16"), "KC1": ("sbuf", [1, 256], "bfloat16"), "KW": ("sbuf", [128, 128], "bfloat16"),
-    "WC": ("sbuf", [128, 128], "bfloat16"), "L15": ("sbuf", [128, 16], "uint16"),
-    "LQI": ("sbuf", [128, 68], "int32"), "LQ": ("sbuf", [128, 52], "uint16"), "CL0": ("sbuf", [2, 128], "bfloat16"),
-    "CL": ("sbuf", [2, 128], "bfloat16"), "CR0": ("sbuf", [2, 2 * Q], "bfloat16"), "CR": ("sbuf", [2, 2 * Q], "bfloat16"),
-    "PD": ("sbuf", [128, Q], "float32"), "J0": ("sbuf", [128, Q], "float32"), "JD": ("sbuf", [128, 8], "float32"),
-    "U0": ("sbuf", [2 * Q, 2 * Q], "bfloat16"), "U1": ("sbuf", [2 * Q, 2 * Q], "bfloat16"), "U2": ("sbuf", [2 * Q, 2 * Q], "bfloat16"),
-    "UT": ("sbuf", [2 * Q, 2 * Q], "bfloat16"), "SEGM": ("sbuf", [128, 1024], "bfloat16"), "RST": ("sbuf", [128, 1024], "bfloat16"),
-    "DC": ("sbuf", [128, Q], "float32"), "T2": ("sbuf", [128, Q], "float32"), "T1": ("sbuf", [128, Q], "float32"),
-    "FW": ("sbuf", [128, NP], "bfloat16"), "FWS": ("sbuf", [128, NP], "bfloat16"), "FL": ("sbuf", [128, 3 * Q], "bfloat16"),
-    "GE": ("sbuf", [128, Q], "bfloat16"), "O1": ("sbuf", [2 * Q, 128], "bfloat16"), "O2": ("sbuf", [Q, 128], "bfloat16"),
-    "MM": ("sbuf", [128, 2 * Q], "float32"), "PS": ("sbuf", [128, 2 * Q], "float32"), "PL": ("sbuf", [128, 52], "uint16"),
-    "F1": ("sbuf", [128, Q], "float32"), "DD": ("sbuf", [128, Q], "float32"), "EN": ("sbuf", [128, 3 * Q], "float32"), "LX": ("sbuf", [128, LA], "float32"),
-    "NN": ("sbuf", [128, 4], "float32"), "RN": ("sbuf", [128, 4], "float32"),
-    "IXF": ("sbuf", [128, 2 * Q], "float32"),
-    "IX": ("sbuf", [128, 52], "uint16"), "FA": ("sbuf", [128, LA], "bfloat16"), "FA2": ("sbuf", [128, LF], "bfloat16"),
-    "VV": ("sbuf", [128, LA], "bfloat16"), "SG": ("sbuf", [128, LA], "bfloat16"), "DLV": ("sbuf", [128, LA], "float32"),
-    "DLS": ("sbuf", [128, LA], "bfloat16"), "DEO": ("sbuf", [128, 128], "float32"), "VI": ("sbuf", [128, LA], "bfloat16"),
-    "BT": ("sbuf", [128, 128], "bfloat16"), "INC": ("sbuf", [128, 128], "float32"), "IB": ("sbuf", [128, 128], "float32"),
-    "IBD": ("sbuf", [128, 128], "float32"), "IS": ("sbuf", [128, 128], "float32"), "JL": ("sbuf", [128, 8], "float32"),
-    "JLU": ("sbuf", [128, 8], "uint16"), "R": ("sbuf", [128, 256], "float32"), "EQ": ("sbuf", [128, 256], "bfloat16"),
-    "HV": ("sbuf", [128, 256], "float32"), "HS": ("sbuf", [128, 256], "bfloat16"), "VM": ("sbuf", [128, 256], "float32"),
-    "CS": ("sbuf", [128, 256], "float32"), "GL": ("sbuf", [128, 16], "uint16"), "VT": ("sbuf", [128, 256], "float32"),
-    "EE": ("sbuf", [128, 256], "bfloat16"), "ES": ("sbuf", [128, 256], "bfloat16"), "W1": ("sbuf", [128, 48], "float32"),
-    "SL": ("sbuf", [128, 32], "uint16"), "FSG": ("sbuf", [128, 256], "float32"), "XN": ("sbuf", [128, 256], "bfloat16"),
-    "XC": ("sbuf", [128, 256], "bfloat16"), "GT": ("sbuf", [128, 128], "bfloat16"), "PJ": ("sbuf", [128, 128], "float32"),
-    "JB": ("sbuf", [128, JT], "float32"), "SGA": ("sbuf", [128, 1], "float32"), "SGJ": ("sbuf", [128, LA], "float32"),
-    "YF8": ("sbuf", [8, NP], "float32"), "FBB": ("sbuf", [128, 64], "bfloat16"),
-    "RL": ("sbuf", [128, RO * JW], "float32"),
+B, F, U, I = "bfloat16", "float32", "uint16", "int32"
+SHAPES = {
+    B: {"W": WW, "S": 16 * LA, "M": 16 * LA, "Z": 16 * LA, "S2": 16 * LF, "YW": LW, "ONE": 512, "BO": 128, "NBO": 128, "TS": 128,
+        "NTS": 128, "ID": 128, "NI": 128, "I4": 128, "NI4": 128, "NK": 128, "I128": 128, "NQ": 128, "N2K": 128, "HI": 128, "NHI": 128,
+        "MZ": 128, "MA": 128, "MB": 128, "DC": 512, "SEGM": 1024, "RST": 1024, "I2K": 16, "NIN": 8, "RA": 256, "RB": 256,
+        "RX": 128, "RY": 128, "MH": 512, "SE": 512, "MX": 512, "FL": 2 * Q, "PRE": 3 * Q, "XS": Q, "DR": Q, "DRN": Q, "NT": Q,
+        "NTN": Q, "LH": 384, "FW": K, "FWS": K, "FA": LA, "FA2": LF, "HB": LA, "BTM": 128, "CUM": 144, "GT": 128, "EE": 256, "ES": 256,
+        "XN": 256, "XC": 256},
+    H: {"CZ": LA, "HD": 512, "VB": 512, "VM": 256, "FSG": 256},
+    F: {"C0": CW, "C1": CW, "C2": CW, "C3": K, "LN": LW, "TH": 1, "TT": 1, "NT1": 1, "O32": 128, "JC": 132, "P3": 3 * Q, "P4": 3 * Q,
+        "RS3": 3 * Q, "ALT": 32, "R": 512, "KR": 32, "DD": 32, "VC": 32, "W1": 16, "DEO": 128, "LXM": 128, "PJ": 128, "JB": 256,
+        "JL": 8, "NS": 4, "NN": 4, "RN": 4, "IXF": Q, "SGA": 1, "YF": Q, "RL": RO * JW, "SIL": 16},
+    U: {"OA": LA, "OF": LF, "PL": Q, "IX": Q, "L2": 16, "LT": 24, "GL": 16, "SL": 32, "JLU": 8},
+    I: {"CI": K, "FR": Q, "TI": 1, "AI": 2, "LQI": 16},
 }
+SCRATCH = {n: ("sbuf", [128, w], d) for d, tab in SHAPES.items() for n, w in tab.items()}
+SCRATCH.update({"PM": ("sbuf", [16, 512], B), "PN": ("sbuf", [16, 256], B), "CT": ("sbuf", [16, 256], B), "CT0": ("sbuf", [16, 256], B),
+                "PMF": ("sbuf", [16, 128], F), "TB": ("sbuf", [16, 132], F), "CU": ("sbuf", [16, 108], F), "CV": ("sbuf", [16, 8], F),
+                "KC": ("sbuf", [65, 256], B), "KL": ("sbuf", [65, 128], B), "ROW": ("sbuf", [1, 320], B)})
 for _i in range(8):
-    SCRATCH["B%d" % _i] = ("psum", [128, 512], "float32")
-SEMAPHORES = ["sV", "sS", "sP", "sG"] + ["ld%d" % i for i in range(6)] + ["st%d" % i for i in range(14)] \
+    SCRATCH["B%d" % _i] = ("psum", [128, 512], F)
+SEMAPHORES = ["sV", "sS", "sP", "sG"] + ["ld%d" % i for i in range(4)] + ["st%d" % i for i in range(3)] \
     + [s + str(i) for s in ("arr", "ls", "ra", "na", "nl", "rn") for i in range(RO)]
 
 
-CYC, GAT, SCA, WAKE, SLACK = 0.001, 1.5, 3.8, 0.15, 0.1
-PLAN = {}
-SEED = [8067, 0.3]
-QW = {"V": 1.0, "S": 1.0, "P": 1.0, "G": 1.0, "Y": 1.0, "N": 1.0}
-NEGV = V
+CYC, GAT, SCA, WAKE, SLACK = 0.001, 1.5, 3.5, 0.12, 0.1
+PEC = 0.0007
+PLAN, FIRST = {}, {}
+GA = ["SVSS", "SVSS", "SVSS"]
+GF = ["SSS", "SSS", "SSS"]
+NEGV = [V, 1408, 1408]
+KB = ((0, 0, 128), (1, 0, 128))
 
 
 def plan(ops):
     n = len(ops)
     pred = [dict() for _ in range(n)]
     succ = [[] for _ in range(n)]
-    hist, last = {}, {}
+    hist = {}
     for i, (q, tag, reads, writes, occ, dur, _) in enumerate(ops):
         for w, lst in ((False, reads), (True, writes)):
             for _a, buf, m in lst:
                 ps = buf in SCRATCH and SCRATCH[buf][0] == "psum"
                 for em, ew, j in hist.get(buf, []):
                     same = ops[j][1] == tag
-                    if j == i or (not (em & m and (w or ew)) and not ps) or (ps and same and q == "V" and not (em & m and (w or ew))):
+                    if j == i or (not (em & m and (w or ew)) and not ps) or (ps and same and q != "P" and not (em & m and (w or ew))):
                         continue
                     lat = 0.0 if same and (q == "P" or not ew) else WAKE
                     if pred[i].get(j, -1.0) < lat:
@@ -111,9 +80,9 @@ def plan(ops):
             succ[j].append((i, lat))
     pr = [0.0] * n
     for i in range(n - 1, -1, -1):
-        pr[i] = ops[i][5] * QW[ops[i][0]] + max([lat + pr[k] for k, lat in succ[i]] + [0.0])
-    if SEED[0]:
-        pr = [float(x) for x in np.array(pr) + SEED[1] * np.random.default_rng(SEED[0]).random(n)]
+        pr[i] = ops[i][5] + max([lat + pr[k] for k, lat in succ[i]] + [0.0])
+    for i in FIRST:
+        pr[i] += 1000.0 * FIRST[i]
     left = [len(p) for p in pred]
     est = [0.0] * n
     ready, free = {}, {}
@@ -169,7 +138,7 @@ def relay_program(g, core, T, topo):
                 g.wait_ge(T.sem["rn%d" % t], 8)
                 g.remote_dma(T.NN[:, t:t + 1], T.RN[:, t:t + 1], T.sem["na%d" % t], T.sem["nl%d" % t], pid, rid, m)
                 g.wait_ge(T.sem["ra%d" % t], 8)
-                g.remote_dma(T["C%d" % t][:, NP:CW], T.RL[:, t * JW:(t + 1) * JW], T.sem["arr%d" % t], T.sem["ls%d" % t], pid, rid, m)
+                g.remote_dma(T["C%d" % t][:, 0:JW], T.RL[:, t * JW:(t + 1) * JW], T.sem["arr%d" % t], T.sem["ls%d" % t], pid, rid, m)
     for r in range(N):
         for t in range(RO):
             if route(topo, T.cores[r], T.cores[(r + 1 + t % 3) % N]) == core:
@@ -187,7 +156,7 @@ def rank_program(g, core, T, topo):
     known = {q: {} for q in eng}
     hist = {}
     bits = {}
-    serial = [0]
+    serial, solo = [0], [False]
 
     def cols(lo, n, step):
         k = (lo, n, step)
@@ -210,11 +179,14 @@ def rank_program(g, core, T, topo):
     def acc(x):
         return [x] if len(x) == 3 and isinstance(x[1], str) else [x[1], x[2]]
 
+    def psum(buf):
+        return buf in SCRATCH and SCRATCH[buf][0] == "psum"
+
     def need(q, tag, reads, writes):
         want = {}
         for w, lst in ((False, reads), (True, writes)):
             for _, buf, m in lst:
-                ps = buf[0] == "B" and buf[1:].isdigit()
+                ps = psum(buf)
                 for (em, ew, eq, sem, val, snap) in hist.get(buf, []):
                     hit = em & m
                     if ps and eq != tag:
@@ -242,7 +214,7 @@ def rank_program(g, core, T, topo):
     def note(tag, reads, writes, sem, val, snap):
         for _, buf, m in writes:
             h = hist.setdefault(buf, [])
-            h[:] = [e for e in h if e[0] & ~m] if not (buf[0] == "B" and buf[1:].isdigit()) else [e for e in h if e[2] != tag or e[0] & ~m]
+            h[:] = [e for e in h if e[0] & ~m] if not psum(buf) else [e for e in h if e[2] != tag or e[0] & ~m]
             h.append((m, True, tag, sem, val, snap))
         for _, buf, m in reads:
             h = hist.setdefault(buf, [])
@@ -259,6 +231,12 @@ def rank_program(g, core, T, topo):
 
         def issue():
             need(q, q, reads, writes)
+            if q == "G":
+                alone = writes[0][1] == "KC"
+                if (alone or solo[0]) and known[q].get("sG", 0) < cnt[q]:
+                    g.wait_ge(T.sem["sG"], cnt[q])
+                    known[q]["sG"] = cnt[q]
+                solo[0] = alone
             cnt[q] += 1
             fn().then_inc(T.sem["s" + q], 1)
             snap = dict(known[q])
@@ -266,9 +244,11 @@ def rank_program(g, core, T, topo):
             note(q, reads, writes, "s" + q, cnt[q], snap)
         ops.append((q, q, reads, writes, cost, cost, issue))
 
-    def dma(q, out, in_, sem, reads, writes, dur=2.5):
+    def dma(q, out, in_, sem, reads, writes, dur=2.5, first=0):
         serial[0] += 1
         tag = "d%d" % serial[0]
+        if first:
+            FIRST[len(ops)] = first
 
         def issue():
             need(q, None, reads, writes)
@@ -276,32 +256,34 @@ def rank_program(g, core, T, topo):
             note(tag, reads, writes, sem, 16, dict(known[q]))
         ops.append((q, tag, reads, writes, 0.05, dur, issue))
 
+    def width(x):
+        return bin(x[2]).count("1")
+
     def cost(out, ins, per):
         for x in ins:
             if isinstance(x[1], tuple):
-                return 0.05 + GAT * CYC * 16 * bin(x[2][2]).count("1")
+                return 0.05 + GAT * CYC * 16 * width(x[2])
         if isinstance(out[1], tuple):
-            return 0.05 + SCA * CYC * 16 * bin(out[2][2]).count("1")
-        two = all(SCRATCH[x[1]][2] in ("bfloat16", "uint16") for x in [out] + ins)
-        return CYC * max(64, bin(out[2]).count("1") * (per if per == 2 or not two else 0.5))
+            return 0.05 + SCA * CYC * 16 * width(out[2])
+        two = all(SCRATCH[x[1]][2] in (B, U, "float16") for x in [out] + ins)
+        return CYC * max(64, width(out) * (per if per == 2 or not two else 0.5))
 
     def ap(x):
-        return x[0]
+        return x[0] if isinstance(x, tuple) else x
 
     def copy(out, in_):
         run("V", lambda: g.vector.tensor_copy(ap(out), ap(in_)), out, [in_], cost(out, [in_], 1))
 
     def tt(out, x, y, op):
-        ps = any(isinstance(z[1], str) and SCRATCH[z[1]][0] == "psum" for z in (x, y))
+        ps = any(isinstance(z[1], str) and psum(z[1]) for z in (x, y))
         run("V", lambda: g.vector.tensor_tensor(ap(out), ap(x), ap(y), op), out, [x, y], cost(out, [x, y], 1 if ps else 2))
 
     def ts(out, x, s1, op0, s2=None, op1=None):
         ins = [x] + [s for s in (s1, s2) if isinstance(s, tuple)]
-        u1 = s1[0] if isinstance(s1, tuple) else s1
         if op1 is None:
-            run("V", lambda: g.vector.tensor_scalar(ap(out), ap(x), u1, None, op0), out, ins, cost(out, [x], 1))
+            run("V", lambda: g.vector.tensor_scalar(ap(out), ap(x), ap(s1), None, op0), out, ins, cost(out, [x], 1))
         else:
-            run("V", lambda: g.vector.tensor_scalar(ap(out), ap(x), u1, s2, op0, op1), out, ins, cost(out, [x], 1))
+            run("V", lambda: g.vector.tensor_scalar(ap(out), ap(x), ap(s1), ap(s2), op0, op1), out, ins, cost(out, [x], 1))
 
     def scan(out, d0, d1, ini, op0, op1):
         run("V", lambda: g.vector.tensor_tensor_scan(ap(out), ap(d0), ap(d1), ini, op0, op1), out, [d0, d1], cost(out, [d0, d1], 1))
@@ -311,26 +293,24 @@ def rank_program(g, core, T, topo):
 
     def act(out, x, func, bias=0.0, scale=1.0, accum=None):
         ins = [x] + ([bias] if isinstance(bias, tuple) else [])
-        b = bias[0] if isinstance(bias, tuple) else bias
-        if accum is None:
-            if isinstance(out[1], tuple):
-                run("S", lambda: g.scalar.activation(ap(out), ap(x), func), out, ins, cost(out, [x], 1))
-                return
-            c = cost(out, [x], 2) if isinstance(x[1], tuple) else CYC * max(64, bin(out[2]).count("1"))
-            run("S", lambda: g.scalar.activation(ap(out), ap(x), func, bias=b, scale=scale), out, ins, c)
+        if isinstance(out[1], tuple):
+            run("S", lambda: g.scalar.activation(ap(out), ap(x), func), out, ins, cost(out, [x], 1))
+        elif accum is None:
+            c = cost(out, [x], 2) if isinstance(x[1], tuple) else CYC * max(64, width(out)) + (1.3 if func == F_.Silu else 0.0)
+            run("S", lambda: g.scalar.activation(ap(out), ap(x), func, bias=ap(bias), scale=scale), out, ins, c)
         else:
-            run("S", lambda: g.scalar.activation(ap(out), ap(x), func, bias=b, scale=scale, accum_out=ap(accum)), [out, accum], ins,
-                CYC * bin(out[2]).count("1"))
+            run("S", lambda: g.scalar.activation(ap(out), ap(x), func, bias=ap(bias), scale=scale, accum_out=ap(accum)), [out, accum], ins,
+                CYC * width(out))
 
     def mm(out, l, r, start, stop):
-        c = CYC * max(min(64, bin(l[2]).count("1")), bin(r[2]).count("1")) * (4 if SCRATCH[l[1]][2] == "float32" else 1)
+        c = PEC * max(min(64, width(l)), width(r)) * (4 if SCRATCH[l[1]][2] == F else 1)
         run("P", lambda: g.tensor.matmul(ap(out), ap(l), ap(r), start, stop), out, [l, r], c)
 
     def iota(out, pat, base, cm):
-        run("G", lambda: g.iota(ap(out), pat, base, cm, allow_small_or_imprecise_dtypes=True), out, [], 0.13 + 2 * CYC * bin(out[2]).count("1"))
+        run("G", lambda: g.iota(ap(out), pat, base, cm, allow_small_or_imprecise_dtypes=True), out, [], 0.13 + 2 * CYC * width(out))
 
     def sel(out, x, pat, op, fl, base, cm):
-        run("G", lambda: g.affine_select(ap(out), ap(x), pat, op, fl, base, cm), out, [x], 0.17 + 2 * CYC * bin(out[2]).count("1"))
+        run("G", lambda: g.affine_select(ap(out), ap(x), pat, op, fl, base, cm), out, [x], 0.17 + 2 * CYC * width(out))
 
     def send(t, src, land, relay, arr, ra, ls, lat):
         dst = T.cores[(rank + 1 + t % 3) % N]
@@ -345,270 +325,305 @@ def rank_program(g, core, T, topo):
                          pid, rid, emask(topo, core, to))
             note("r%s%d" % (ls, t), [src], [], ls + str(t), 8, dict(known["G"]))
         ops.append(("G", "r%s%d" % (ls, t), [src], [net], 0.3, 2.0, issue))
-        ops.append(("N", "q%s%d" % (arr, t), [net], [land], 0.0, lat * (1 if first is None else 2),
+        ops.append(("N", "q%s%d" % (arr, t), [net], [land], 0.0, lat * (0.2 if first is None else 1),
                     lambda: note("q%s%d" % (arr, t), [], [land], arr + str(t), 8, {})))
 
-    dma("Y", T.FR[:], T.fr[:], "ld0", [], [a("FR")], 2.2)
-    dma("Y", T.CI[:], T.cl[:], "ld2", [], [a("CI")], 4.0)
-    dma("Y", T.W[:, XB:XB + V], T.xv[:], "ld3", [], [a("W", XB, V)], 6.0)
+    dma("Y", T.FR[:], T.fr[:], "ld0", [], [a("FR")], 2.2, 3)
+    dma("Y", T.CI[:], T.cl[:], "ld2", [], [a("CI")], 4.0, 2)
+    dma("Y", T.W[:, XB:XB + V], T.xv[:], "ld3", [], [a("W", XB, V)], 6.0, 1)
     dma("Y", T.TI[:], T.th[:], "ld1", [], [a("TI")], 6.0)
-    fill(a("VM", 0, 16), 200.0)
-    act(a("W", SB, 16), a("VM", 0, 16), F_.Silu)
+    fill(a("SIL"), 100.0)
+    act(a("W", SB, 16), a("SIL"), F_.Silu)
 
+    GP, KP = [[-16, 8], [0, 16]], [[0, 8], [1, 16]]
+    DM, CWM = a("DC", 0, 256), a("DC", 256, 256)
     fill(a("ONE"), 1.0)
-    fill(a("FRB"), 8.0)
-    sel(a("PM"), a("ONE", 0, 416, p=16), [[0, 26], [1, 16]], A_.is_equal, 0.0, 0, -1)
-    sel(a("QM0"), a("ONE", 0, 128, p=8), [[1, 128]], A_.is_ge, 0.0, 0, -16)
-    sel(a("QM"), a("QM0"), [[-1, 128]], A_.is_ge, 0.0, 15, 16)
+    sel(a("RX"), a("ONE", 0, 128), GP, A_.is_ge, 0.0, 0, 1)
+    sel(a("BO"), a("RX"), [[16, 8], [0, 16]], A_.is_ge, 0.0, 15, -1)
+    sel(a("TS"), a("BO"), [[1, 128]], A_.is_ge, 0.0, -1, -1)
+    sel(a("ID"), a("ONE", 0, 128), [[-1, 128]], A_.is_equal, 0.0, 0, 1)
+    sel(a("PM", 0, 256), a("ONE", 0, 256, p=16), [[0, 16], [1, 16]], A_.is_equal, 0.0, 0, -1)
+    copy(a("PMF"), a("PM", 0, 128))
+    for name, c in (("NI", -1.0), ("I4", 4096.0), ("NI4", -4096.0)):
+        ts(a(name), a("ID"), c, A_.mult)
+    ts(a("NTS"), a("TS"), -1.0, A_.mult)
+    starts = [[divmod(AS * t % K, Q), divmod(FS * t % K, Q)] for t in range(RO)]
+    iota(a("CU", 0, Q), [[0, Q]], 4095, 0)
+    iota(a("CU", Q, Q), [[1, Q]], K, 0)
+    iota(a("CU", 2 * Q, 12), [[0, 12]], 0, 0)
+    iota(a("CV"), [[0, 8]], K, 0)
+    for t in range(RO):
+        p0, q0 = starts[t][1]
+        iota(a("CU", 2 * Q + 4 * t + 2, 1), [[0, 1]], -Q * p0 - q0, Q)
+        if t:
+            sel(a("CV", 2 * t, 1), a("CV", 6, 1), [[0, 1]], A_.is_ge, 0.0, p0 - 1, -1)
+            sel(a("CV", 2 * t + 1, 1), a("CV", 6, 1), [[0, 1]], A_.is_equal, 0.0, p0, -1)
+    iota(a("P3", 0, Q, 3), [[16, Q]], 2 * K, 1)
+    fill(a("RS3"), 0.0)
+    fill(a("RS3", 0, Q, 3), 1e6)
+    fill(a("ROW", 0, 256), 8.0)
+    fill(a("ROW", 256, Q), 4096.0)
+    fill(a("ROW", 256 + Q, 16), 0.0)
+
+    def sentinels():
+        iota(a("LN", 0, LA), [[0, LA]], 2 * V + int(OFF), 0)
+        iota(a("LN", K, LF), [[0, LF]], 2 * V + int(OFF), 0)
+
+    def consts_of_lists(t):
+        mm(a("B6", 0, 108), a("PMF"), a("CU"), True, False)
+        if t:
+            mm(a("B6", 2 * Q + 4 * t + 2, 2), a("PMF"), a("CV", 2 * t, 2), False, False)
+
+    def cyclic(t):
+        for c in range(2):
+            p0, i = starts[t][c][0], 128 * (2 * (t - 1) + c)
+            sel(a("RX"), a("BO"), [[16, 8], [0, 16]], A_.is_ge, 0.0, p0 - 1, -1)
+            sel(a("RY"), a("NBO"), [[0, 8], [-1, 16]], A_.is_ge, 0.0, p0 - 1, 0)
+            sel(a("SE", i, 128), a("BO"), GP, A_.is_equal, 0.0, -p0, 1)
+            sel(a("MX", i, 128), a("NBO"), KP, A_.is_equal, 0.0, -p0, 0)
+            for j, m in enumerate(("NTS", "RX", "RY")):
+                mm(a("B7", 256, 128), a("ID"), a(m), j == 0, j == 2)
+            act(a("MH", i, 128), a("B7", 256, 128), F_.Identity)
+
+    def lists(t, x, off):
+        fa, fd = a("FL", 0, Q), a("FL", Q, Q)
+        ts(fa, x, off + 0.5, A_.is_lt)
+        ts(fd, x, off + 3.5, A_.is_gt)
+        scan(a("PRE", 0, Q), a("ONE", 0, Q), fa, 0.0, A_.mult, A_.subtract)
+        scan(a("PRE", Q, Q), fa, fd, 0.0, A_.add, A_.add)
+        ts(a("XS"), x, -off, A_.add, 0.0, A_.max)
+        mm(a("B6", 0, Q), a("NI4"), fa, False, False)
+        mm(a("B6", Q, Q), a("I4"), fa, False, False)
+        mm(a("B6", Q, Q), a("I4"), fd, False, False)
+        for c in range(2):
+            q0, i, b = starts[t][c][1], 128 * (2 * (t - 1) + c), 2 * Q + 4 * t + 2 * c
+            mm(a("B6", b, 1), a("MH", i, 128) if t else a("NTS"), a("PRE", Q * c + Q - 1, 1), False, False)
+            if t:
+                mm(a("B6", b, 1), a("SE", i, 128), a("PRE", Q * c + q0 - 1, 1), False, False)
+                mm(a("B6", b + 1, 1), a("MX", i, 128), a("PRE", Q * c + Q - 1, 1), False, False)
+        mm(a("B6", 0, 2 * Q), a("NI"), a("PRE", 0, 2 * Q), False, True)
+        for c in range(2):
+            q0, b = starts[t][c][1], 2 * Q + 4 * t + 2 * c
+            ts(a("P3", 3 * q0 + 1 + c, Q - q0, 3), a("B6", Q * c + q0, Q - q0), a("B6", b, 1), A_.add)
+            if q0:
+                ts(a("P3", 1 + c, q0, 3), a("B6", Q * c, q0), a("B6", b, 1), A_.add, a("B6", b + 1, 1), A_.add)
+        scan(a("P4"), a("RS3"), a("P3"), 0.0, A_.add, A_.min)
+        copy(a("PL"), a("P4", 2, Q, 3))
+        act(ind(a("LN"), a("PL")), a("C%d" % t, JW, K), F_.Silu)
+        ts(a("OA"), a("LN", 0, LA), 0.25 - OFF, A_.add)
+        ts(a("OF"), a("LN", K, LF), 0.25 - OFF, A_.add)
+        if t < RO - 1:
+            sentinels()
+            consts_of_lists(t + 1)
+        scan(a("PRE", 2 * Q, Q), a("ONE", 0, Q), fd, 0.0, A_.mult, A_.add)
+        mm(a("B7", 0, Q + 1), a("ONE", 0, 128, p=1), a("ROW", 256, Q + 1), True, False)
+        mm(a("B7", 0, Q), a("NI4"), fd, False, False)
+        mm(a("B7", 0, Q), a("ID"), a("PRE", 2 * Q, Q), False, False)
+        mm(a("B7", Q, 1), a("TS"), a("PRE", 3 * Q - 1, 1), False, True)
+        ts(a("DR"), a("B7", 0, Q), a("B7", Q, 1), A_.add, 256.0, A_.min)
+        if t == RO - 1:
+            for j in range(3):
+                tt(a("LH", 128 * j, 128), ind(a("DR"), a("LT", 8 * j, 8)), a("BO"), A_.mult)
+                mm(a("B7", 64 + j, 16, 3), a("LH", 128 * j, 128), a("DC", 0, 16), True, True)
+            copy(a("DRN"), a("B7", 64, Q))
+
+    def gather(q, c, frozen):
+        w = ind(a("W", XB, WW - XB), a("OF" if frozen else "OA", CH * c, CH))
+        out = a("S2" if frozen else "S", 16 * CH * c, 16 * CH)
+        if frozen:
+            if q == "V":
+                ts(out, w, 64.0, A_.add, a("TT"), A_.is_ge)
+            else:
+                act(out, w, F_.Relu, a("NT1"))
+        elif q == "V":
+            ts(out, w, 64.0, A_.add)
+        else:
+            act(out, w, F_.Identity, 64.0)
+
+    def negate(t):
+        n = NEGV[t]
+        if n:
+            ts(a("W", XB + V, n), a("W", XB, n), -1.0, A_.mult, 63.0, A_.add)
+        if n < V:
+            act(a("W", XB + V + n, V - n), a("W", XB + n, V - n), F_.Identity, 63.0, -1.0)
+
+    sentinels()
+    consts_of_lists(0)
+    for p in range(16):
+        ts(a("C0", JW + p, Q, 16), a("CI", Q * p, Q), OFF, A_.add)
+    lists(0, a("FR"), 0.0)
+    negate(0)
+    ts(a("TH"), a("TI"), 64.0, A_.add)
+    ts(a("TT"), a("TI"), 64.0, A_.add)
+    ts(a("NT1"), a("TT"), -1.0, A_.mult, 65.0, A_.add)
+    fill(a("W", 0, XB), 0.0)
     fill(a("SEGM"), 1.0)
     fill(a("SEGM", 0, 64, 16), 0.0)
-    mm(a("B1", 0, 416), a("PM", 0, 128), a("PM", 0, 416), True, True)
-    mm(a("B2", 0, NP - 416), a("PM", 0, 128), a("PM", 0, NP - 416), True, True)
-    mm(a("B3", 0, 128), a("QM"), a("QM"), True, True)
-    copy(a("DM", 0, 416), a("B1", 0, 416))
-    act(a("DM", 416, NP - 416), a("B2", 0, NP - 416), F_.Identity)
-    copy(a("BO"), a("B3", 0, 128))
-    for s0, p0, n in SEG:
-        copy(a("FRB", p0, n), a("FR", s0, n))
-    mm(a("B4", 0, 512), a("QM"), a("FRB", 0, 512), True, True)
-    mm(a("B5", 0, NP - 512), a("QM"), a("FRB", 512, NP - 512), True, True)
-    tt(a("FW", 0, 512), a("B4", 0, 512), a("DM", 0, 512), A_.mult)
-    tt(a("FW", 512, NP - 512), a("B5", 0, NP - 512), a("DM", 512, NP - 512), A_.mult)
-    scan(a("FWS"), a("SEGM", 0, NP), a("FW"), 0.0, A_.mult, A_.add)
-    copy(a("T2"), a("FWS", 15, Q, 16))
-    sel(a("TS"), a("BO"), [[1, 128]], A_.is_ge, 0.0, -1, -1)
-    iota(a("CL0"), [[0, 8], [1, 16]], 0, 0)
-    sel(a("CL"), a("CL0"), [[0, 128]], A_.is_gt, 1.0, 0, 1)
-    iota(a("CR0", 0, Q), [[-16, Q]], -2 * K, 0)
-    iota(a("CR0", Q, Q), [[-16, Q]], -K, 0)
-    sel(a("CR"), a("CR0"), [[0, 2 * Q]], A_.is_equal, -1.0, 0, 1)
-
-    def order(t):
-        for b, s in ((0, START[AS * t % K]), (Q, START[FS * t % K])):
-            u = "U%d" % t
-            n = Q - s
-            sel(a("UT", b + s, n, p=2 * Q), a("ONE", 0, n, p=2 * Q), [[1, n]], A_.is_gt, 0.0, b + s, -1)
-            sel(a(u, b + s, n), a("UT", b + s, n), [[0, n]], A_.is_ge, 0.0, -(b + s), 1)
-            if s:
-                sel(a(u, b, s), a("ONE", 0, s, p=2 * Q), [[0, s]], A_.is_ge, 0.0, b + Q - 1, -1)
-                sel(a("UT", b, s), a(u, b, s), [[0, s]], A_.is_ge, 0.0, -(b + s), 1)
-                sel(a(u, b, s), a("UT", b, s), [[-1, s]], A_.is_ge, 1.0, -b, 1)
-                if b:
-                    sel(a("UT", b, s), a(u, b, s), [[0, s]], A_.is_ge, 0.0, -b, 1)
-                    sel(a(u, b, s), a("UT", b, s), [[0, s]], A_.is_ge, 0.0, -b, 1)
-
-    order(0)
-    mm(a("B6", 0, Q), a("CL"), a("CR", 0, Q), True, True)
-    ts(a("PD"), a("B6", 0, Q), -1.0, A_.mult)
-    ts(a("J0"), a("PD"), -2.0 * K, A_.add)
-    ts(a("JD"), a("J0", 0, 8), float(JW - 512), A_.add)
-    iota(a("LN", 0, LA), [[0, LA]], 2 * V + int(OFF), 0)
-    iota(a("LN", FB0, LF), [[0, LF]], 2 * V + int(OFF), 0)
-
-    def lists(t):
-        ts(a("FL", 0, Q), a("T2"), 0.0, A_.is_le)
-        ts(a("GE"), a("T2"), 0.0, A_.is_gt)
-        ts(a("FL", 2 * Q, Q), a("T2"), 3.5, A_.is_ge)
-        tt(a("FL", Q, Q), a("GE"), a("FL", 2 * Q, Q), A_.subtract)
-        mm(a("B7", 0, 128, p=2 * Q), a("FL", 0, 2 * Q), a("BO"), True, True)
-        act(a("O1"), a("B7", 0, 128, p=2 * Q), F_.Identity)
-        mm(a("B6", 0, 2 * Q), a("TS"), a("FL", 0, 2 * Q), True, False)
-        mm(a("B6", 0, 2 * Q), a("CL"), a("CR"), False, False)
-        mm(a("B6", 0, 2 * Q), a("O1"), a("U%d" % t), False, True)
-        ts(a("F1"), a("T2"), 0.0, A_.max, 1.0, A_.add)
-        tt(a("MM"), a("B6", 0, 2 * Q), a("FL", 0, 2 * Q), A_.mult)
-        tt(a("PS", 0, Q), a("MM", 0, Q), a("MM", Q, Q), A_.add)
-        tt(a("PS", Q, Q), a("PS", 0, Q), a("PD"), A_.add)
-        copy(a("PL", 0, Q), a("PS", Q, Q))
-        act(ind(a("LN"), a("PL", 0, Q)), a("C%d" % t, 0, NP), F_.Silu)
-        ts(a("OA"), a("LN", 0, LA), 0.25 - OFF, A_.add)
-        ts(a("OF"), a("LN", FB0, LF), 0.25 - OFF, A_.add)
-        mm(a("B5", 0, 128, p=Q), a("FL", 2 * Q, Q), a("BO"), True, True)
-        act(a("O2"), a("B5", 0, 128, p=Q), F_.Identity)
-        mm(a("B5", 128, Q), a("TS"), a("FL", 2 * Q, Q), True, False)
-        mm(a("B5", 128, Q), a("NI4"), a("FL", 2 * Q, Q), False, False)
-        mm(a("B5", 128, Q), a("O2"), a("U0", 0, Q, p=Q), False, True)
-
-    def gather(q, c, out, off):
-        w = ind(a("W", XB, WW - XB), a(off, CH * c, CH))
-        if q == "V":
-            copy(a(out, 16 * CH * c, 16 * CH), w)
-        else:
-            act(a(out, 16 * CH * c, 16 * CH), w, F_.Identity)
-
-    def negate(lo, n, q):
-        if q == "V":
-            ts(a("W", XB + V + lo, n), a("W", XB + lo, n), -1.0, A_.mult, 63.0, A_.add)
-        else:
-            act(a("W", XB + V + lo, n), a("W", XB + lo, n), F_.Identity, 63.0, -1.0)
-
-    for s0, p0, n in SEG:
-        fill(a("C0", p0 + n, -(-n // 16) * 16 - n), OFF)
-        ts(a("C0", p0, n), a("CI", s0, n), OFF, A_.add)
-    sel(a("ID"), a("ONE", 0, 128), [[-1, 128]], A_.is_equal, 0.0, 0, 1)
-    ts(a("NI4"), a("ID"), -4096.0, A_.mult)
-    lists(0)
-    negate(0, V, "S")
-    fill(a("W", 0, XB), 0.0)
-    fill(a("RST"), 64.0)
-    fill(a("RST", 0, 64, 16), 8192.0)
-    copy(a("TH"), a("TI"))
-    copy(a("TT"), a("TI"))
-    pads = 0
-    for s0, p0, n in SEG:
-        fill(a("DC", p0 // 16, -(-n // 16)), 4096.0 - 513.0 - pads)
-        pads += -(-n // 16) * 16 - n
-    ts(a("PS", 0, Q), a("T2"), 6.0, A_.is_ge, 4096.0, A_.mult)
-    tt(a("DC"), a("DC"), a("PS", 0, Q), A_.add)
-    fill(a("YW"), 1.0)
-    fill(a("FBB"), 0.0)
+    fill(a("RST"), 2.0)
+    fill(a("RST", 0, 64, 16), BIGM)
+    for lo in range(0, LW, 1024):
+        act(a("YW", lo, min(1024, LW - lo)), a("RST", 0, min(1024, LW - lo)), F_.Identity, -0.5, 0.0)
     fill(a("JB"), 0.0)
+    fill(a("HD"), 0.0)
+    fill(a("CUM", 0, 16), 0.0)
     fill(a("O32"), 1.0 / 32)
-    copy(a("BOF"), a("BO"))
-    sel(a("SH"), a("BOF"), [[-1, 128]], A_.is_equal, 0.0, -1, 1)
-    tt(a("DF"), a("ID"), a("SH"), A_.subtract)
-    ts(a("D1024"), a("DF"), -1024.0, A_.mult)
-    ts(a("D8"), a("DF"), -8.0, A_.mult)
-    ts(a("I4"), a("ID"), 4096.0, A_.mult)
-    ts(a("I16"), a("BO", 0, 8, 16), 16.0, A_.mult)
+    fill(a("ALT"), 32.0)
+    fill(a("ALT", 0, 16, 2), 0.0)
+    for name, c in (("NK", -1.0 / 1024), ("I128", 1.0 / 128), ("NQ", -0.25), ("N2K", -2048.0), ("HI", 0.5), ("NHI", -0.5)):
+        ts(a(name), a("ID"), c, A_.mult)
+    ts(a("NBO"), a("BO"), -1.0, A_.mult)
+    ts(a("I2K"), a("BO", 0, 16, 8), 2048.0, A_.mult)
     ts(a("NIN"), a("BO", 0, 8, 16), -1.0, A_.mult)
-    ts(a("KV"), a("DM", 15, 1), float(XB - V // 2 - 4096 - OFF), A_.mult)
-    iota(a("KC0"), [[0, 16], [-16384, 16]], 262144, 0)
-    iota(a("KC1"), [[0, 16], [-1, 16]], 15, 0)
-    iota(a("KW"), [[0, 8], [1024, 16]], -16384, 0)
-    tt(a("WC"), a("BO"), a("KW"), A_.mult)
-    iota(a("LQI", 52, 16), [[16, 16]], 15, 0)
-    copy(a("L15"), a("LQI", 52, 16))
-    iota(a("LQI", 0, 52), [[1, 52]], 0, 0)
-    copy(a("LQ"), a("LQI", 0, 52))
-    sel(a("LT"), a("ONE", 0, 256, p=16), [[0, 16], [-1, 16]], A_.is_ge, 0.0, -1, 1)
-    mm(a("B4", 0, 256), a("PM", 0, 128), a("LT"), True, True)
-    act(a("TRI"), a("B4", 0, 256), F_.Identity)
+    P16 = [[0, 16], [1, 16]]
+    sel(a("PN"), a("ONE", 0, 256, p=16), P16, A_.is_ge, 0.0, 0, -1)
+    sel(a("CT0"), a("PN"), P16, A_.not_equal, 1024.0, 0, -1)
+    sel(a("PM", 256, 256), a("CT0"), P16, A_.not_equal, 0.0, -15, -16)
+    mm(a("B0"), a("PM", 0, 128), a("PM"), True, True)
+    act(a("DC"), a("B0"), F_.Identity)
+    ts(a("MZ"), a("NK"), a("DC", 0, 1), A_.mult)
+    iota(a("PN"), [[0, 256]], 2048, 0)
+    sel(a("CT0"), a("PN"), [[0, 16], [-1, 16]], A_.is_ge, 8192.0, 0, 1)
+    sel(a("CT"), a("CT0"), P16, A_.not_equal, -2048.0, 0, -1)
+    iota(a("TB", 0, Q), [[16, Q]], JW + 1, 1)
+    iota(a("TB", Q, Q), [[1, 16], [256, 3]], JW + 1, 16)
+    iota(a("TB", 2 * Q, 8), [[16, 8]], JW - 255, 1)
+    iota(a("TB", 104, 4), [[0, 4]], 0, 1)
+    iota(a("TB", 108, 24), [[16, 3], [0, 8]], 0, 1)
+    mm(a("B1", 0, 132), a("PMF"), a("TB"), True, True)
+    act(a("JC"), a("B1", 0, 132), F_.Identity)
+    copy(a("LT"), a("JC", 108, 24))
+    iota(a("LQI"), [[2, 16]], 1, 0)
+    copy(a("L2"), a("LQI"))
+    sel(a("MA"), a("TS"), [[-1, 128]], A_.not_equal, -255.0, 0, 1)
+    sel(a("GT"), a("BO"), [[-1, 128]], A_.is_ge, 0.0, 0, 1)
+    sel(a("MB"), a("GT"), [[-1, 128]], A_.not_equal, 256.0, 0, 1)
+    sel(a("RA"), a("ONE", 0, 256), [[-16, 8], [-1000, 2], [-1, 16]], A_.is_equal, 0.0, 1000, 1)
+    iota(a("EE"), [[0, 8], [-66, 2], [0, 16]], 2, 0)
+    sel(a("RB"), a("EE"), [[-16, 8], [0, 2], [-1, 16]], A_.is_equal, 0.0, 0, 1)
+    fill(a("KC"), 0.0)
+    fill(a("KL"), 1.0)
+    fill(a("KL", p=1, p0=64), 0.5)
+    iota(a("KC", p=1), [[0, 16], [-128, 16]], 1920, 0)
+    iota(a("KC", p=1, p0=32), [[0, 8], [10496, 2], [0, 16]], -256, 0)
+    iota(a("KC", p=1, p0=64), [[0, 8], [-1, 2], [0, 16]], -62, 0)
 
     for t in range(RO):
-        C = "C%d" % t
-        gather("S", 0, "S", "OA")
-        gather("V", 1, "S", "OA")
-        gather("S", 2, "S", "OA")
-        gather("S", 3, "S", "OA")
-        ts(a("LX"), a("OA"), OFF, A_.add)
-        tt(a("DEO"), a("LX", 1, 128, 2), a("LX", 0, 128, 2), A_.subtract)
-        tt(a("DD"), a("B5", 128, Q), a("DC"), A_.add)
-        ts(a("EN", Q, Q), a("DD"), 513.0 + NP, A_.add)
-        tt(a("EN", 0, Q), a("J0"), a("EN", Q, Q), A_.subtract)
-        act(a("SG"), a("LN", 0, LA), F_.Sign, 0.5 - V - OFF)
-        for h in range(2):
-            mm(a("B2", 128 * h, 128), a("DF"), a("LX", h, 128, 2), True, False)
-            mm(a("B2", 128 * h, 128), a("D1024"), a("SG", h, 128, 2), False, True)
-            mm(a("B2", 256 + 128 * h, 128), a("D8"), a("SG", h, 128, 2), True, True)
-        act(a("DLV"), a("B2", 0, 256), F_.Identity, a("KV"))
-        act(a("DLS"), a("B2", 256, 256), F_.Identity)
-        mm(a("B0", 0, 256), a("ONE", 0, 128, p=1), a("KC0"), True, False)
+        C, last = "C%d" % t, t == RO - 1
+        SG = a("YW", 0, LA)
+        for c in range(NA):
+            gather(GA[t][c], c, False)
         for c in range(NF):
-            gather("S", c, "S2", "OF")
+            gather(GF[t][c], c, True)
+        ts(a("CZ"), a("OA"), -float(V), A_.add)
+        ts(a("HB"), a("OA"), 1.0 / 64, A_.mult, 128.0 - 63.0 / 128, A_.add)
+        for j, l in enumerate(("NHI", "HI")):
+            mm(a("B7", 256 + 128 * j, 128), a(l), a("CZ", 0, 128, 2), True, False)
+            mm(a("B7", 256 + 128 * j, 128), a("HI"), a("CZ", 1, 128, 2), False, True)
+        act(a("DEO"), a("B7", 256, 128), F_.Identity)
+        act(a("LXM"), a("B7", 384, 128), F_.Identity, V + OFF)
+        for h in range(2):
+            key = a("B%d" % h, 0, 256)
+            mm(key, a("KL"), a("KC"), True, False)
+            mm(key, a("CZ", 128 * h, 128), a("RA"), False, False)
+            mm(key, a("HB", 128 * h, 128), a("RB"), False, False)
         for c in range(NA):
             lo = 16 * CH * c
             scan(a("M", lo, 16 * CH), a("SEGM"), a("S", lo, 16 * CH), 0.0, A_.mult, A_.max)
-            ts(a("FA", CH * c, CH), a("M", lo + 15, CH, 16), a("TT"), A_.is_lt)
-            ts(a("VV", CH * c, CH), a("FA", CH * c, CH), 2048.0, A_.mult, -1024.0, A_.add)
-            tt(a("S", lo, CH, 16), a("VV", CH * c, CH), a("M", lo, CH, 16), A_.min)
-            scan(a("Z", lo, 16 * CH), a("RST"), a("S", lo, 16 * CH), 0.0, A_.add, A_.min)
-            if c == NA - 1:
-                mm(a("B4", 0, LA), a("BO"), a("FA"), True, True)
-            for h in range(2):
-                mm(a("B0", 128 * h, 128, p=32, p0=32 * c), a("FA", CH * c + h, 32, 2), a("WC"), False, False)
-            for h in range(2):
-                for k in range(16):
-                    mm(a("B0", 128 * h + k, 8, 16, p=32, p0=32 * c), a("Z", lo + 16 * h + k, 32, 32), a("I16"), False, False)
-        mm(a("B0", 0, 256), a("ONE", 0, 128, p=1), a("KC1"), False, True)
-        ts(a("VI"), a("B4", 0, LA), 3.5, A_.is_gt)
-        act(a("YW", 0, LA), a("B4", 0, LA), F_.Relu, -25.0, 8.0)
-        act(a("SGJ"), a("B4", 0, LA), F_.Sign, -3.5, 1.0, a("SGA"))
-        tt(a("BT"), a("VI", 0, 128, 2), a("VI", 1, 128, 2), A_.mult)
-        scan(a("INC"), a("ONE", 0, 128), a("BT"), -513.0, A_.mult, A_.add)
-        tt(a("IB"), a("INC"), a("BT"), A_.mult)
-        tt(a("IBD"), a("IB"), a("DM", 0, 128), A_.mult)
-        scan(a("IS"), a("SEGM", 0, 128), a("IBD"), 0.0, A_.mult, A_.add)
-        tt(a("JL"), a("IS", 15, 8, 16), a("JD"), A_.min)
-        ts(a("JLU"), a("JL"), 512.0, A_.add)
-        send(t, a("INC", 127, 1), a("NN", t, 1), T.RN[:, t:t + 1], "na", "rn", "nl", 2.0)
-        scan(a("R"), a("SEGM", 0, 256), a("B0", 0, 256), 0.0, A_.mult, A_.max)
-        scan(a("VT"), a("SEGM", 0, 256), a("B0", 0, 256), 0.0, A_.mult, A_.max)
-        tt(a("EQ"), ind(a("R"), a("L15")), a("VT"), A_.is_equal)
-        for h in range(2):
-            mm(a("B3", 128 * h, 128), a("EQ", 128 * h, 128), a("ID"), True, True)
-        scan(a("M2", 0, 1024), a("SEGM"), a("S2", 0, 1024), 0.0, A_.mult, A_.max)
-        tt(a("HV"), a("B3", 0, 256), a("DLV"), A_.mult)
-        tt(a("HS"), a("B3", 0, 256), a("DLS"), A_.mult)
-        for h in range(2):
-            mm(a("B1", h, 128, 2), a("BOF"), a("HV", 128 * h, 128), True, False)
-            mm(a("B1", h, 128, 2), a("I4"), a("VI", h, 128, 2), False, True)
-        for h in range(2):
-            mm(a("B7", h, 128, 2), a("BO"), a("HS", 128 * h, 128), True, True)
-        scan(a("M2", 1024, 1024), a("SEGM"), a("S2", 1024, 1024), 0.0, A_.mult, A_.max)
+            ts(a("FA", CH * c, CH), a("M", lo + 15, CH, 16), a("TT"), A_.is_lt, EPS, A_.max)
+            tt(a("S", lo, CH, 16), a("FA", CH * c, CH), a("M", lo, CH, 16), A_.mult)
+            scan(a("Z", lo, 16 * CH), a("RST"), a("S", lo, 16 * CH), 1.0, A_.mult, A_.min)
+        for h, m0, n in KB:
+            for k in range(16):
+                mm(a("B%d" % h, k, 16, 16, p=n, p0=m0), a("Z", 16 * (128 * h + m0) + k, n, 16), a("I2K"), False, k == 15 and m0 + n == 128)
+        mm(a("B4", 0, LA), a("BO"), a("FA"), True, True)
+        act(SG, a("B4", 0, LA), F_.Sign, -3.5, 1.0, a("SGA"))
+        mm(a("B3", 256, 128), a("ID"), a("DC", 0, 128), True, False)
+        mm(a("B3", 256, 128), a("ID"), a("YW", 0, 128, 2), False, False)
+        mm(a("B3", 256, 128), a("ID"), a("YW", 1, 128, 2), False, True)
+        ts(a("BTM"), a("B3", 256, 128), 2.5, A_.is_gt)
+        scan(a("CUM", 16, 128), a("ONE", 0, 128), a("BTM"), 0.0, A_.mult, A_.add)
+        mm(a("B3", 392, 1), a("BO"), a("CUM", 143, 1), True, True)
+        mm(a("B3", 384, 8), a("MA"), a("CUM", 31, 8, 16), True, False)
+        mm(a("B3", 384, 8), a("MB"), a("CUM", 15, 8, 16), False, True)
+        copy(a("NS", t, 1), a("B3", 392, 1))
+        send(t, a("NS", t, 1), a("NN", t, 1), T.RN[:, t:t + 1], "na", "rn", "nl", 2.0)
+        tt(a("JL"), a("B3", 384, 8), a("JC", 2 * Q, 8), A_.min)
+        ts(a("JLU"), a("JL"), 255.0, A_.add)
         for k in range(16):
             mm(a("B2", k, 8, 16), a("S", 16 + k, 128, 32) if k else a("M", 16, 128, 32), a("BO", 0, 8, 16), True, False)
             mm(a("B2", k, 8, 16), a("S", k, 128, 32) if k else a("M", 0, 128, 32), a("NIN"), False, True)
-        tt(a("VM"), a("B1", 0, 256), a("DM", 0, 256), A_.mult)
-        tt(a("VT"), a("B1", 0, 256), a("TRI"), A_.mult)
-        scan(a("CS"), a("SEGM", 0, 256), a("VM"), 0.0, A_.mult, A_.add)
-        tt(a("FSG"), a("B7", 0, 256), a("FA"), A_.mult)
-        tt(a("EE"), ind(a("CS"), a("L15")), a("VT"), A_.is_equal)
-        copy(a("GL"), a("CS", 15, 16, 16))
+        act(a("GT"), a("B2", 0, 128), F_.Sign, -0.5)
+        mm(a("B2", 128, 128), a("GT"), a("ID"), True, True)
+        tt(a("PJ"), a("B2", 128, 128), a("DEO"), A_.mult)
+        tt(ind(a("JB"), a("JLU")), a("PJ"), a("LXM"), A_.add)
+        send(t, a("JB", 0, JW), a(C, 0, JW), T.RL[:, t * JW:(t + 1) * JW], "arr", "ra", "ls", 2.5)
+        for h in range(2):
+            scan(a("R", 256 * h, 256), a("SEGM", 0, 256), a("B%d" % h, 0, 256), 0.0, A_.mult, A_.max)
+        ts(a("KR"), a("R", 15, 32, 16), MAGIC, A_.add, MAGIC, A_.subtract)
+        tt(a("DD"), a("R", 15, 32, 16), a("KR"), A_.subtract)
+        scan(a("VC"), a("ALT"), a("DD"), 0.0, A_.mult, A_.add)
+        tt(a("HD", 256, 16, 16), a("KR", 0, 16, 2), a("KR", 1, 16, 2), A_.subtract)
+        tt(a("VM"), ind(a("VC"), a("L2")), DM, A_.mult)
+        copy(a("HD", 0, 16, 16), a("VC", 1, 16, 2))
+        scan(a("VB"), a("SEGM", 0, 512), a("HD"), 0.0, A_.mult, A_.add)
+        for h in range(2):
+            mm(a("B0", 256 + 8 * h, 8), a("VM", 128 * h, 128), a("BO", 0, 8, 16), True, True)
+        mm(a("B1", 256, 256), a("PM", 0, 128), a("CT"), True, False)
+        mm(a("B1", 256, 256), a("N2K"), SG, False, False)
+        for h in range(2):
+            mm(a("B1", 256 + 128 * h, 128), a("VM", 128 * h, 128), a("BO"), False, False)
+            mm(a("B1", 256 + 128 * h, 128), a("VB", 128 * h, 128), a("NI"), False, h == 1)
+        mm(a("B3", 0, 256), a("ONE", 0, 128, p=1), a("ROW", 0, 256), True, False)
+        for h in range(2):
+            mm(a("B3", 128 * h, 128), a("VB", 256 + 128 * h, 128), a("NQ"), False, h == 1)
+        ts(a("GL"), a("B0", 256, 16), 1023.5 + XB, A_.add, V + XB - 1.0, A_.min)
+        ts(a("EE"), a("B1", 256, 256), 0.0, A_.is_equal, -4096.0, A_.mult)
         scan(a("ES"), a("SEGM", 0, 256), a("EE"), 0.0, A_.mult, A_.add)
-        ts(a("W1", 0, 16), a("ES", 15, 16, 16), -8192.0, A_.mult)
-        tt(a("W1", 16, 16), a("W1", 0, 16), a("CS", 15, 16, 16), A_.add)
-        tt(a("W1", 32, 16), a("W1", 16, 16), a("J0", 0, 16), A_.max)
-        copy(a("SL", 0, 16, 2), a("W1", 32, 16))
-        ts(a("GT"), a("B2", 0, 128), 0.0, A_.is_gt)
-        mm(a("B3", 256, 128), a("GT"), a("ID"), True, True)
+        tt(a("W1"), a("B0", 256, 16), a("ES", 15, 16, 16), A_.add)
+        ts(a("SL", 0, 16, 2), a("W1"), 1023.5 + XB, A_.add, a("JC", 104, 1), A_.max)
+        tt(a("FSG"), a("B3", 0, 256), a("FA"), A_.mult)
         tt(a("XN"), ind(a("W", 0, XB + V), a("GL")), a("FSG"), A_.add)
-        tt(a("PJ"), a("B3", 256, 128), a("DEO"), A_.mult)
-        tt(ind(a("JB"), a("JLU")), a("PJ"), a("LX", 0, 128, 2), A_.add)
-        send(t, a("JB", 0, JW), a(C, NP, JW), T.RL[:, t * JW:(t + 1) * JW], "arr", "ra", "ls", 2.2)
         ts(a("XC"), a("XN"), 0.0, A_.max, 63.0, A_.min)
         for b in range(15, -1, -1):
             copy(ind(a("W", 0, XB + V), a("SL", 2 * b, 1)), a("XC", 16 * b, 16))
-        if t < RO - 1:
-            iota(a("LN", 0, LA), [[0, LA]], 2 * V + int(OFF), 0)
-            iota(a("LN", FB0, LF), [[0, LF]], 2 * V + int(OFF), 0)
-            order(t + 1)
-            if NEGV:
-                negate(0, NEGV, "V")
-            if NEGV < V:
-                negate(NEGV, V - NEGV, "S")
+        if not last:
+            negate(t + 1)
+            cyclic(t + 1)
         else:
             dma("Y", T.yx[:], T.W[:, XB:XB + V], "st0", [a("W", XB, V)], [], 4.5)
-        scan(a("M2", 2048, 1024), a("SEGM"), a("S2", 2048, 1024), 0.0, A_.mult, A_.max)
-        ts(a("FA2"), a("M2", 15, LF, 16), a("TT"), A_.is_lt)
-        mm(a("B6", 0, LF), a("BO"), a("FA2"), True, True)
-        act(a("YW", FB0, LF), a("B6", 0, LF), F_.Relu, -25.0, 8.0)
-        if t < RO - 1:
-            mm(a("B7", 256, 1), a("O32"), a("SGA"), True, True)
-            copy(a("AI", 0, 1), a("B7", 256, 1))
+        for c in range(NF):
+            for k in range(16):
+                mm(a("B5", CH * c, CH), a("ID"), a("S2", 16 * CH * c + k, CH, 16), k == 0, k == 15)
+        act(a("FA2"), a("B5", 0, LF), F_.Relu, 1.0, -1.0)
+        mm(a("B5", LF, LF), a("BO"), a("FA2"), True, True)
+        act(a("YW", K, LF), a("B5", LF, LF), F_.Sign, -3.5)
+        if not last:
+            mm(a("B4", 256, 1), a("O32"), a("SGA"), True, True)
+            copy(a("AI", 0, 1), a("B4", 256, 1))
             ts(a("AI", 1, 1), a("AI", 0, 1), 3, A_.bitwise_and)
             tt(a("TT"), a("TH"), a("AI", 1, 1), A_.add)
-        tt(a("FW"), ind(a("YW"), a("PL", 0, Q)), a("DM"), A_.mult)
-        ts(a("EN", 2 * Q, Q), a("DD"), a("NN", t, 1), A_.is_ge)
-        tt(a("IXF", 0, Q), a("EN", 0, Q), a("EN", 2 * Q, Q), A_.mult)
-        tt(a("IXF", Q, Q), a("IXF", 0, Q), a("EN", Q, Q), A_.add)
-        copy(a("IX", 0, Q), a("IXF", Q, Q))
-        act(a("C%d" % (t + 1), 0, NP), ind(a(C), a("IX", 0, Q)), F_.Identity, -OFF if t == RO - 1 else 0.0)
-        scan(a("FWS"), a("SEGM", 0, NP), a("FW"), 0.0, A_.mult, A_.add)
-        tt(a("T1"), a("F1"), a("FWS", 15, Q, 16), A_.subtract)
-        tt(a("T2"), a("T1"), a("EN", 2 * Q, Q), A_.mult)
-        if t < RO - 1:
-            lists(t + 1)
-    for i, (s0, p0, n) in enumerate(SEG):
-        dma("Y" if i % 2 else "S", T.yc[:, s0:s0 + n], T.C3[:, p0:p0 + n], "st%d" % (1 + i), [a("C3", p0, n)], [])
-    ts(a("FBB", 0, Q), a("T2"), 0.0, A_.max)
-    tt(a("FW"), ind(a("FBB"), a("LQ", 0, Q)), a("DM"), A_.mult)
-    mm(a("B4", 0, 512, p=8), a("BO", 0, 8, 16), a("FW", 0, 512), True, True)
-    mm(a("B6", 0, NP - 512, p=8), a("BO", 0, 8, 16), a("FW", 512, NP - 512), True, True)
-    act(a("YF8", 0, 512), a("B4", 0, 512, p=8), F_.Identity)
-    copy(a("YF8", 512, NP - 512), a("B6", 0, NP - 512, p=8))
-    for i, (s0, p0, n) in enumerate(SEG):
-        dma("Y" if i % 2 else "S", T.yf[:, s0:s0 + n], T.YF8[:, p0:p0 + n], "st%d" % (6 + i), [a("YF8", p0, n)], [])
+            ts(a("NT1"), a("TT"), -1.0, A_.mult, 65.0, A_.add)
+        ts(a("NT"), a("DR"), a("NN", t, 1), A_.is_gt, 1024.0, A_.mult)
+        if last:
+            ts(a("NTN"), a("DRN"), a("NN", t, 1), A_.is_gt, 1024.0, A_.mult)
+        mm(a("B4", 320, Q), a("ID"), a("DRN" if last else "DR"), True, False)
+        mm(a("B4", 320, Q), a("ID"), a("NTN" if last else "NT"), False, True)
+        tt(a("IXF"), a("B4", 320, Q), a("JC", Q if last else 0, Q), A_.min)
+        ts(a("IX"), a("IXF"), -1.0, A_.add)
+        act(a("C%d" % (t + 1), 0 if last else JW, K), ind(a(C), a("IX")), F_.Identity, -OFF if last else 0.0)
+        act(a("FW"), ind(a("YW"), a("PL")), F_.Identity, 3.0, 2.0)
+        for j in range(3):
+            scan(a("FWS", 256 * j, 256), a("FW", 256 * j, 256), CWM, 0.0, A_.max, A_.mult)
+        X1 = a("B5", 2 * LF, Q)
+        mm(X1, a("ID"), a("XS"), True, False)
+        mm(X1, a("I128"), a("NT"), False, False)
+        mm(X1, a("MZ"), a("FWS", 14, Q, 16), False, False)
+        mm(X1, a("NK"), a("FWS", 15, Q, 16), False, True)
+        if not last:
+            lists(t + 1, X1, 6.0)
+    dma("S", T.yc[:], T.C3[:], "st1", [a("C3")], [], 4.0)
+    ts(a("YF"), a("B5", 2 * LF, Q), -6.0, A_.add, 0.0, A_.max)
+    dma("Y", T.yf[:], T.YF[:], "st2", [a("YF")], [], 2.2)
     if "order" not in PLAN:
         PLAN["order"] = plan(ops)
     for i in PLAN["order"]:
@@ -617,7 +632,7 @@ def rank_program(g, core, T, topo):
         g.wait_ge(T.sem["s" + q], cnt[q])
     for i in range(4):
         g.wait_ge(T.sem["ld%d" % i], 16)
-    for i in range(11):
+    for i in range(3):
         g.wait_ge(T.sem["st%d" % i], 16)
     for t in range(RO):
         for s in ("ls", "arr", "nl", "na"):

@@ -4,7 +4,8 @@ from concourse.mybir import dt, AluOpType, AxisListType, ActivationFunctionType
 A_, F_ = AluOpType, ActivationFunctionType
 N, V, K, LA, LF, RO, AS, FS = 8, 2048, 768, 256, 192, 3, 170, 255
 Q = K // 16
-XB = 16
+J = 2
+XB = 16 * J
 SB = XB + 2 * V
 WW = SB + 16
 LW = 2 * K + 880
@@ -20,9 +21,9 @@ B, F, U, I = "bfloat16", "float32", "uint16", "int32"
 SHAPES = {
     B: {"W": WW, "S": 16 * LA, "M": 16 * LA, "Z": 16 * LA, "S2": 16 * LF, "YW": LW, "ONE": 512, "BO": 128, "NBO": 128, "TS": 128,
         "NTS": 128, "ID": 128, "NI": 128, "I4": 128, "NI4": 128, "NK": 128, "I128": 128, "NQ": 128, "N2K": 128, "HI": 128, "NHI": 128,
-        "MZ": 128, "MA": 128, "MB": 128, "DC": 512, "SEGM": 1024, "RST": 1024, "I2K": 16, "NIN": 8, "RA": 256, "RB": 256,
+        "MZ": 128, "MA": 128, "MB": 128, "DC": 512, "SEGM": 1024, "RST": 1024, "I2K": 16, "NIN": 8, "RA": 512,
         "RX": 128, "RY": 128, "MH": 512, "SE": 512, "MX": 512, "FL": 2 * Q, "PRE": 3 * Q, "XS": Q, "DR": Q, "DRN": Q, "NT": Q,
-        "NTN": Q, "LH": 384, "FW": K, "FWS": K, "FA": LA, "FA2": LF, "HB": LA, "BTM": 128, "CUM": 144, "GT": 128, "EE": 256, "ES": 256,
+        "NTN": Q, "LH": 384, "FW": K, "FWS": K, "FA": LA, "FA2": LF, "HB": LA, "BTM": 128, "CUM": 144, "GT": 128, "EE": 256 * J, "ES": 256 * J, "SEJ": 512, "BJ": 128 * J,
         "XN": 256, "XC": 256},
     H: {"CZ": LA, "HD": 512, "VB": 512, "VM": 256, "FSG": 256},
     F: {"C0": CW, "C1": CW, "C2": CW, "C3": K, "LN": LW, "TH": 1, "TT": 1, "NT1": 1, "O32": 128, "JC": 132, "P3": 3 * Q, "P4": 3 * Q,
@@ -32,25 +33,31 @@ SHAPES = {
     I: {"CI": K, "FR": Q, "TI": 1, "AI": 2, "LQI": 16},
 }
 SCRATCH = {n: ("sbuf", [128, w], d) for d, tab in SHAPES.items() for n, w in tab.items()}
-SCRATCH.update({"PM": ("sbuf", [16, 512], B), "PN": ("sbuf", [16, 256], B), "CT": ("sbuf", [16, 256], B), "CT0": ("sbuf", [16, 256], B),
+SCRATCH.update({"PM": ("sbuf", [16, 512], B), "PN": ("sbuf", [16, 256], B), "CT": ("sbuf", [16, 256 * J], B), "CT0": ("sbuf", [16, 256], B),
                 "PMF": ("sbuf", [16, 128], F), "TB": ("sbuf", [16, 132], F), "CU": ("sbuf", [16, 108], F), "CV": ("sbuf", [16, 8], F),
-                "KC": ("sbuf", [65, 256], B), "KL": ("sbuf", [65, 128], B), "ROW": ("sbuf", [1, 320], B)})
+                "KC": ("sbuf", [1, 256], H), "SN": ("sbuf", [128, LA], F), "ROW": ("sbuf", [1, 320], H)})
 for _i in range(8):
     SCRATCH["B%d" % _i] = ("psum", [128, 512], F)
-SEMAPHORES = ["sV", "sS", "sP", "sG"] + ["ld%d" % i for i in range(4)] + ["st%d" % i for i in range(3)] \
+SEMAPHORES = ["sV", "sS", "sP", "sG"] + ["ld%d" % i for i in range(5)] + ["st%d" % i for i in range(3)] + ["sn%d" % i for i in range(4)] \
     + [s + str(i) for s in ("arr", "ls", "ra", "na", "nl", "rn") for i in range(RO)]
 
 
-CYC, GAT, SCA, WAKE, SLACK = 0.001, 1.5, 3.5, 0.12, 0.1
-PEC = 0.0007
-PLAN, FIRST = {}, {}
-GA = ["SVSS", "SVSS", "SVSS"]
-GF = ["SSS", "SSS", "SSS"]
+CYC, GAT, SCA, WAKE, SLACK = 0.00083, 1.5, 3.5, 0.22, 0.1
+PEC, PASSES, HOPN, HOPJ = 0.0005, 8, 2.0, 2.6
+PLAN, SHORT, RLEN = {}, 0.0, 18.0
+INORDER = "P"
+WAR = "P"
+XH = 1024
+D0 = {"A0": 0.0, "A1": 0.0, "A2": 1.6, "A3": 3.2, "F0": 3.1, "F1": 4.8, "F2": 6.7, "lit": 1.7, "viol": 6.3, "send": 9.0, "keys": 9.5,
+      "wake": 9.5, "lanes": 13.0, "moves": 14.0, "out": 15.0}
+DUE = [dict(D0), dict(D0), dict(D0)]
+GA = [(("S", 64), ("V", 64), ("S", 96), ("V", 32))] * RO
+GF = [(("S", 64), ("S", 64), ("S", 64))] * RO
 NEGV = [V, 1408, 1408]
 KB = ((0, 0, 128), (1, 0, 128))
 
 
-def plan(ops):
+def plan(ops, dues):
     n = len(ops)
     pred = [dict() for _ in range(n)]
     succ = [[] for _ in range(n)]
@@ -63,7 +70,7 @@ def plan(ops):
                     same = ops[j][1] == tag
                     if j == i or (not (em & m and (w or ew)) and not ps) or (ps and same and q != "P" and not (em & m and (w or ew))):
                         continue
-                    lat = 0.0 if same and (q == "P" or not ew) else WAKE
+                    lat = 0.0 if same and (q == "P" or (not ew and q in WAR)) else WAKE
                     if pred[i].get(j, -1.0) < lat:
                         pred[i][j] = lat
         for w, lst in ((False, reads), (True, writes)):
@@ -81,36 +88,41 @@ def plan(ops):
     pr = [0.0] * n
     for i in range(n - 1, -1, -1):
         pr[i] = ops[i][5] + max([lat + pr[k] for k, lat in succ[i]] + [0.0])
-    for i in FIRST:
-        pr[i] += 1000.0 * FIRST[i]
-    left = [len(p) for p in pred]
-    est = [0.0] * n
-    ready, free = {}, {}
-    for i in range(n):
-        free[ops[i][0]] = 0.0
-        ready.setdefault(ops[i][0], [])
-        if not left[i]:
-            ready[ops[i][0]].append(i)
-    out = []
-    for _ in range(n):
-        best = None
-        for q in ready:
-            if ready[q]:
-                s0 = min(max(free[q], est[i]) for i in ready[q])
-                k = max((i for i in ready[q] if max(free[q], est[i]) <= s0 + SLACK), key=lambda i: (pr[i], -i))
-                s = max(free[q], est[k])
-                if best is None or s < best[0]:
-                    best = (s, q, k)
-        s, q, k = best
-        ready[q].remove(k)
-        free[q] = s + ops[k][4]
-        out.append(k)
-        for i, lat in succ[k]:
-            est[i] = max(est[i], s + ops[k][5] + lat)
-            left[i] -= 1
-            if not left[i]:
-                ready[ops[i][0]].append(i)
-    return out
+
+    def place(key, back):
+        before, after = (succ, [list(p.items()) for p in pred]) if back else ([list(p.items()) for p in pred], succ)
+        left, est, start, busy = [len(p) for p in before], [0.0] * n, [0.0] * n, {}
+        ready = [i for i in range(n) if not left[i]]
+        while ready:
+            k = min(ready, key=lambda i: (key[i], i))
+            ready.remove(k)
+            occ, dur = ops[k][4], ops[k][5]
+            s, lst, at = est[k] + (dur - occ if back else 0.0), busy.setdefault(ops[k][0], []), 0
+            while at < len(lst) and lst[at][0] < s + occ - 1e-9:
+                s = max(s, lst[at][1])
+                at += 1
+            lst.insert(at, (s, s + occ))
+            start[k] = s
+            for i, lat in after[k]:
+                est[i] = max(est[i], s + (occ if back else dur) + lat)
+                left[i] -= 1
+                if not left[i]:
+                    ready.append(i)
+        return start
+
+    key, best = [0.0] * n, None
+    for i in range(n - 1, -1, -1):
+        key[i] = min([dues.get(i, 200.0)] + [key[k] - lat - ops[i][5] for k, lat in succ[i]])
+    for _ in range(PASSES):
+        start = place(key, False)
+        end = max(start[i] + ops[i][5] for i in range(n))
+        if best is None or end < best[0]:
+            best = (end, start)
+        late = place([-start[i] - ops[i][5] for i in range(n)], True)
+        key = [-late[i] - ops[i][4] - (SHORT if ops[i][4] < 0.3 else 0.0) for i in range(n)]
+    PLAN["end"] = best[0]
+    PLAN["dbg"] = (ops, pr, succ, best[1])
+    return sorted(range(n), key=lambda i: (round(best[1][i], 6), i))
 
 
 def route(topo, src, dst):
@@ -156,7 +168,7 @@ def rank_program(g, core, T, topo):
     known = {q: {} for q in eng}
     hist = {}
     bits = {}
-    serial, solo = [0], [False]
+    serial = [0]
 
     def cols(lo, n, step):
         k = (lo, n, step)
@@ -193,7 +205,7 @@ def rank_program(g, core, T, topo):
                         pass
                     elif not hit or not (w or ew):
                         continue
-                    elif eq == tag and (not ew or (w and q == "P")):
+                    elif eq == tag and ((not ew and q in WAR) or (w and q in INORDER)):
                         continue
                     if known[q].get(sem, 0) >= val:
                         continue
@@ -223,6 +235,11 @@ def rank_program(g, core, T, topo):
 
     ops = []
 
+    dues = {}
+
+    def due(t, name):
+        dues[len(ops) - 1] = RLEN * t + DUE[t][name]
+
     def run(q, fn, out, ins, cost):
         writes = acc(out)[:1] if isinstance(out, tuple) else out
         reads = acc(out)[1:] if isinstance(out, tuple) else []
@@ -231,12 +248,6 @@ def rank_program(g, core, T, topo):
 
         def issue():
             need(q, q, reads, writes)
-            if q == "G":
-                alone = writes[0][1] == "KC"
-                if (alone or solo[0]) and known[q].get("sG", 0) < cnt[q]:
-                    g.wait_ge(T.sem["sG"], cnt[q])
-                    known[q]["sG"] = cnt[q]
-                solo[0] = alone
             cnt[q] += 1
             fn().then_inc(T.sem["s" + q], 1)
             snap = dict(known[q])
@@ -244,17 +255,15 @@ def rank_program(g, core, T, topo):
             note(q, reads, writes, "s" + q, cnt[q], snap)
         ops.append((q, q, reads, writes, cost, cost, issue))
 
-    def dma(q, out, in_, sem, reads, writes, dur=2.5, first=0):
+    def dma(q, out, in_, sem, reads, writes, dur=2.5):
         serial[0] += 1
         tag = "d%d" % serial[0]
-        if first:
-            FIRST[len(ops)] = first
 
         def issue():
             need(q, None, reads, writes)
             eng[q].dma_start(out, in_).then_inc(T.sem[sem], 16)
             note(tag, reads, writes, sem, 16, dict(known[q]))
-        ops.append((q, tag, reads, writes, 0.05, dur, issue))
+        ops.append((q, tag, reads, writes, 0.0 if sem[0] == "l" else 0.05, dur, issue))
 
     def width(x):
         return bin(x[2]).count("1")
@@ -306,6 +315,13 @@ def rank_program(g, core, T, topo):
         c = PEC * max(min(64, width(l)), width(r)) * (4 if SCRATCH[l[1]][2] == F else 1)
         run("P", lambda: g.tensor.matmul(ap(out), ap(l), ap(r), start, stop), out, [l, r], c)
 
+    def mms(calls):
+        def fn():
+            for out, l, r, start, stop in calls:
+                last = g.tensor.matmul(ap(out), ap(l), ap(r), start, stop)
+            return last
+        run("P", fn, [c[0] for c in calls], [x for c in calls for x in c[1:3]], sum(PEC * max(min(64, width(c[1])), width(c[2])) for c in calls))
+
     def iota(out, pat, base, cm):
         run("G", lambda: g.iota(ap(out), pat, base, cm, allow_small_or_imprecise_dtypes=True), out, [], 0.13 + 2 * CYC * width(out))
 
@@ -324,14 +340,15 @@ def rank_program(g, core, T, topo):
             g.remote_dma(land[0] if first is None else relay, src[0], T.sem[(arr if first is None else ra) + str(t)], T.sem[ls + str(t)],
                          pid, rid, emask(topo, core, to))
             note("r%s%d" % (ls, t), [src], [], ls + str(t), 8, dict(known["G"]))
-        ops.append(("G", "r%s%d" % (ls, t), [src], [net], 0.3, 2.0, issue))
-        ops.append(("N", "q%s%d" % (arr, t), [net], [land], 0.0, lat * (0.2 if first is None else 1),
+        ops.append(("G", "r%s%d" % (ls, t), [src], [net], 0.3, lat + (0.0 if t else 1.0), issue))
+        ops.append(("N", "q%s%d" % (arr, t), [net], [land], 0.0, 0.0 if first is None else lat + (0.0 if t else 1.0),
                     lambda: note("q%s%d" % (arr, t), [], [land], arr + str(t), 8, {})))
 
-    dma("Y", T.FR[:], T.fr[:], "ld0", [], [a("FR")], 2.2, 3)
-    dma("Y", T.CI[:], T.cl[:], "ld2", [], [a("CI")], 4.0, 2)
-    dma("Y", T.W[:, XB:XB + V], T.xv[:], "ld3", [], [a("W", XB, V)], 6.0, 1)
-    dma("Y", T.TI[:], T.th[:], "ld1", [], [a("TI")], 6.0)
+    dma("Y", T.FR[:], T.fr[:], "ld0", [], [a("FR")], 2.2)
+    dma("Y", T.CI[:], T.cl[:], "ld2", [], [a("CI")], 4.5)
+    dma("Y", T.W[:, XB:XB + XH], T.xv[:, 0:XH], "ld3", [], [a("W", XB, XH)], 6.0)
+    dma("Y", T.W[:, XB + XH:XB + V], T.xv[:, XH:V], "ld4", [], [a("W", XB + XH, V - XH)], 7.5)
+    dma("Y", T.TI[:], T.th[:], "ld1", [], [a("TI")], 7.5)
     fill(a("SIL"), 100.0)
     act(a("W", SB, 16), a("SIL"), F_.Silu)
 
@@ -361,13 +378,15 @@ def rank_program(g, core, T, topo):
     iota(a("P3", 0, Q, 3), [[16, Q]], 2 * K, 1)
     fill(a("RS3"), 0.0)
     fill(a("RS3", 0, Q, 3), 1e6)
-    fill(a("ROW", 0, 256), 8.0)
+    fill(a("ROW", 0, 256), 8.0 + 87 * 32)
     fill(a("ROW", 256, Q), 4096.0)
     fill(a("ROW", 256 + Q, 16), 0.0)
 
-    def sentinels():
-        iota(a("LN", 0, LA), [[0, LA]], 2 * V + int(OFF), 0)
-        iota(a("LN", K, LF), [[0, LF]], 2 * V + int(OFF), 0)
+    fill(a("SN"), 2 * V + OFF)
+
+    def sentinels(t):
+        dma("Y", T.LN[:, 0:LA], T.SN[:], "sn%d" % (2 * t), [a("SN")], [a("LN", 0, LA)])
+        dma("Y", T.LN[:, K:K + LF], T.SN[:, 0:LF], "sn%d" % (2 * t + 1), [a("SN")], [a("LN", K, LF)])
 
     def consts_of_lists(t):
         mm(a("B6", 0, 108), a("PMF"), a("CU"), True, False)
@@ -382,8 +401,8 @@ def rank_program(g, core, T, topo):
             sel(a("SE", i, 128), a("BO"), GP, A_.is_equal, 0.0, -p0, 1)
             sel(a("MX", i, 128), a("NBO"), KP, A_.is_equal, 0.0, -p0, 0)
             for j, m in enumerate(("NTS", "RX", "RY")):
-                mm(a("B7", 256, 128), a("ID"), a(m), j == 0, j == 2)
-            act(a("MH", i, 128), a("B7", 256, 128), F_.Identity)
+                mm(a("B6", 256 + 128 * c, 128), a("ID"), a(m), j == 0, j == 2)
+        act(a("MH", 256 * (t - 1), 256), a("B6", 256, 256), F_.Identity)
 
     def lists(t, x, off):
         fa, fd = a("FL", 0, Q), a("FL", Q, Q)
@@ -410,11 +429,14 @@ def rank_program(g, core, T, topo):
         scan(a("P4"), a("RS3"), a("P3"), 0.0, A_.add, A_.min)
         copy(a("PL"), a("P4", 2, Q, 3))
         act(ind(a("LN"), a("PL")), a("C%d" % t, JW, K), F_.Silu)
+        if t:
+            due(t - 1, "lanes")
+        else:
+            dues[len(ops) - 1] = -4.0
         ts(a("OA"), a("LN", 0, LA), 0.25 - OFF, A_.add)
         ts(a("OF"), a("LN", K, LF), 0.25 - OFF, A_.add)
         if t < RO - 1:
-            sentinels()
-            consts_of_lists(t + 1)
+            sentinels(t)
         scan(a("PRE", 2 * Q, Q), a("ONE", 0, Q), fd, 0.0, A_.mult, A_.add)
         mm(a("B7", 0, Q + 1), a("ONE", 0, 128, p=1), a("ROW", 256, Q + 1), True, False)
         mm(a("B7", 0, Q), a("NI4"), fd, False, False)
@@ -427,9 +449,9 @@ def rank_program(g, core, T, topo):
                 mm(a("B7", 64 + j, 16, 3), a("LH", 128 * j, 128), a("DC", 0, 16), True, True)
             copy(a("DRN"), a("B7", 64, Q))
 
-    def gather(q, c, frozen):
-        w = ind(a("W", XB, WW - XB), a("OF" if frozen else "OA", CH * c, CH))
-        out = a("S2" if frozen else "S", 16 * CH * c, 16 * CH)
+    def gather(q, lo, n, frozen):
+        w = ind(a("W", XB, WW - XB), a("OF" if frozen else "OA", lo, n))
+        out = a("S2" if frozen else "S", 16 * lo, 16 * n)
         if frozen:
             if q == "V":
                 ts(out, w, 64.0, A_.add, a("TT"), A_.is_ge)
@@ -447,12 +469,14 @@ def rank_program(g, core, T, topo):
         if n < V:
             act(a("W", XB + V + n, V - n), a("W", XB + n, V - n), F_.Identity, 63.0, -1.0)
 
-    sentinels()
+    fill(a("LN", 0, LA), 2 * V + OFF)
+    fill(a("LN", K, LF), 2 * V + OFF)
     consts_of_lists(0)
     for p in range(16):
         ts(a("C0", JW + p, Q, 16), a("CI", Q * p, Q), OFF, A_.add)
     lists(0, a("FR"), 0.0)
-    negate(0)
+    for lo, n in ((0, XH), (XH, V - XH)):
+        ts(a("W", XB + V + lo, n), a("W", XB + lo, n), -1.0, A_.mult, 63.0, A_.add)
     ts(a("TH"), a("TI"), 64.0, A_.add)
     ts(a("TT"), a("TI"), 64.0, A_.add)
     ts(a("NT1"), a("TT"), -1.0, A_.mult, 65.0, A_.add)
@@ -482,12 +506,17 @@ def rank_program(g, core, T, topo):
     act(a("DC"), a("B0"), F_.Identity)
     ts(a("MZ"), a("NK"), a("DC", 0, 1), A_.mult)
     iota(a("PN"), [[0, 256]], 2048, 0)
-    sel(a("CT0"), a("PN"), [[0, 16], [-1, 16]], A_.is_ge, 8192.0, 0, 1)
-    sel(a("CT"), a("CT0"), P16, A_.not_equal, -2048.0, 0, -1)
+    for j in range(J):
+        sel(a("CT0"), a("PN"), [[0, 16 // J], [-100, J], [-1, 16]], A_.is_ge, 8192.0, 100 * j, 1)
+        sel(a("CT", 256 * j, 256), a("CT0"), [[0, 16 // J], [100, J], [1, 16]], A_.not_equal, -2048.0, -100 * j, -1)
+        sel(a("BTM"), a("ONE", 0, 128), [[-XB, 8 // J], [0, XB]], A_.is_ge, 0.0, -16 * j, 1)
+        sel(a("BJ", 128 * j, 128), a("BTM"), [[XB, 8 // J], [0, XB]], A_.is_ge, 0.0, 16 * j + 15, -1)
+    fill(a("SEJ"), 1.0)
+    fill(a("SEJ", 0, 512 // XB, XB), 0.0)
     iota(a("TB", 0, Q), [[16, Q]], JW + 1, 1)
     iota(a("TB", Q, Q), [[1, 16], [256, 3]], JW + 1, 16)
     iota(a("TB", 2 * Q, 8), [[16, 8]], JW - 255, 1)
-    iota(a("TB", 104, 4), [[0, 4]], 0, 1)
+    iota(a("TB", 104, 4), [[16, 4]], 0, 1)
     iota(a("TB", 108, 24), [[16, 3], [0, 8]], 0, 1)
     mm(a("B1", 0, 132), a("PMF"), a("TB"), True, True)
     act(a("JC"), a("B1", 0, 132), F_.Identity)
@@ -497,25 +526,31 @@ def rank_program(g, core, T, topo):
     sel(a("MA"), a("TS"), [[-1, 128]], A_.not_equal, -255.0, 0, 1)
     sel(a("GT"), a("BO"), [[-1, 128]], A_.is_ge, 0.0, 0, 1)
     sel(a("MB"), a("GT"), [[-1, 128]], A_.not_equal, 256.0, 0, 1)
-    sel(a("RA"), a("ONE", 0, 256), [[-16, 8], [-1000, 2], [-1, 16]], A_.is_equal, 0.0, 1000, 1)
-    iota(a("EE"), [[0, 8], [-66, 2], [0, 16]], 2, 0)
-    sel(a("RB"), a("EE"), [[-16, 8], [0, 2], [-1, 16]], A_.is_equal, 0.0, 0, 1)
-    fill(a("KC"), 0.0)
-    fill(a("KL"), 1.0)
-    fill(a("KL", p=1, p0=64), 0.5)
-    iota(a("KC", p=1), [[0, 16], [-128, 16]], 1920, 0)
-    iota(a("KC", p=1, p0=32), [[0, 8], [10496, 2], [0, 16]], -256, 0)
-    iota(a("KC", p=1, p0=64), [[0, 8], [-1, 2], [0, 16]], -62, 0)
+    ts(a("EE", 0, 128), a("ID"), 2.0, A_.mult)
+    ts(a("EE", 128, 128), a("ID"), -64.0, A_.mult)
+    fill(a("EE", 256, 128), 0.0)
+    mms([(a("B2", 256 * i + 16 * j, 16), a("EE", 128 * (j % 2), 128) if i else a("ID") if j % 2 else a("EE", 256, 128),
+          a("ID", 16 * (j // 2), 16), True, True) for i in range(2) for j in range(16)])
+    act(a("RA"), a("B2"), F_.Identity)
+    iota(a("R", 0, 256, p=1), [[0, 8], [-1281, 2], [-256, 16]], 3266, 0)
+    ts(a("KC"), a("R", 0, 256, p=1), 0.5, A_.mult)
 
     for t in range(RO):
         C, last = "C%d" % t, t == RO - 1
         SG = a("YW", 0, LA)
-        for c in range(NA):
-            gather(GA[t][c], c, False)
-        for c in range(NF):
-            gather(GF[t][c], c, True)
+        if not last:
+            cyclic(t + 1)
+            consts_of_lists(t + 1)
+        for frozen, who in ((False, GA[t]), (True, GF[t])):
+            lo = 0
+            for q, n in who:
+                gather(q, lo, n, frozen)
+                due(t, "AF"[frozen] + str(lo // CH))
+                lo += n
         ts(a("CZ"), a("OA"), -float(V), A_.add)
+        due(t, "lit")
         ts(a("HB"), a("OA"), 1.0 / 64, A_.mult, 128.0 - 63.0 / 128, A_.add)
+        due(t, "lit")
         for j, l in enumerate(("NHI", "HI")):
             mm(a("B7", 256 + 128 * j, 128), a(l), a("CZ", 0, 128, 2), True, False)
             mm(a("B7", 256 + 128 * j, 128), a("HI"), a("CZ", 1, 128, 2), False, True)
@@ -523,9 +558,9 @@ def rank_program(g, core, T, topo):
         act(a("LXM"), a("B7", 384, 128), F_.Identity, V + OFF)
         for h in range(2):
             key = a("B%d" % h, 0, 256)
-            mm(key, a("KL"), a("KC"), True, False)
-            mm(key, a("CZ", 128 * h, 128), a("RA"), False, False)
-            mm(key, a("HB", 128 * h, 128), a("RB"), False, False)
+            mm(key, a("ONE", 0, 128, p=1), a("KC"), True, False)
+            mm(key, a("CZ", 128 * h, 128), a("RA", 0, 256), False, False)
+            mm(key, a("HB", 128 * h, 128), a("RA", 256, 256), False, False)
         for c in range(NA):
             lo = 16 * CH * c
             scan(a("M", lo, 16 * CH), a("SEGM"), a("S", lo, 16 * CH), 0.0, A_.mult, A_.max)
@@ -533,10 +568,11 @@ def rank_program(g, core, T, topo):
             tt(a("S", lo, CH, 16), a("FA", CH * c, CH), a("M", lo, CH, 16), A_.mult)
             scan(a("Z", lo, 16 * CH), a("RST"), a("S", lo, 16 * CH), 1.0, A_.mult, A_.min)
         for h, m0, n in KB:
-            for k in range(16):
-                mm(a("B%d" % h, k, 16, 16, p=n, p0=m0), a("Z", 16 * (128 * h + m0) + k, n, 16), a("I2K"), False, k == 15 and m0 + n == 128)
+            mms([(a("B%d" % h, k, 16, 16, p=n, p0=m0), a("Z", 16 * (128 * h + m0) + k, n, 16), a("I2K"), False, k == 15 and m0 + n == 128)
+                 for k in range(16)])
         mm(a("B4", 0, LA), a("BO"), a("FA"), True, True)
         act(SG, a("B4", 0, LA), F_.Sign, -3.5, 1.0, a("SGA"))
+        due(t, "viol")
         mm(a("B3", 256, 128), a("ID"), a("DC", 0, 128), True, False)
         mm(a("B3", 256, 128), a("ID"), a("YW", 0, 128, 2), False, False)
         mm(a("B3", 256, 128), a("ID"), a("YW", 1, 128, 2), False, True)
@@ -546,19 +582,21 @@ def rank_program(g, core, T, topo):
         mm(a("B3", 384, 8), a("MA"), a("CUM", 31, 8, 16), True, False)
         mm(a("B3", 384, 8), a("MB"), a("CUM", 15, 8, 16), False, True)
         copy(a("NS", t, 1), a("B3", 392, 1))
-        send(t, a("NS", t, 1), a("NN", t, 1), T.RN[:, t:t + 1], "na", "rn", "nl", 2.0)
+        send(t, a("NS", t, 1), a("NN", t, 1), T.RN[:, t:t + 1], "na", "rn", "nl", HOPN)
         tt(a("JL"), a("B3", 384, 8), a("JC", 2 * Q, 8), A_.min)
         ts(a("JLU"), a("JL"), 255.0, A_.add)
-        for k in range(16):
-            mm(a("B2", k, 8, 16), a("S", 16 + k, 128, 32) if k else a("M", 16, 128, 32), a("BO", 0, 8, 16), True, False)
-            mm(a("B2", k, 8, 16), a("S", k, 128, 32) if k else a("M", 0, 128, 32), a("NIN"), False, True)
+        for k0 in range(0, 16, 4):
+            mms([(a("B2", k, 8, 16), a("S" if k else "M", 16 * (1 - h) + k, 128, 32), a("NIN") if h else a("BO", 0, 8, 16), h == 0, h == 1)
+                 for k in range(15 - k0, 11 - k0, -1) for h in range(2)])
         act(a("GT"), a("B2", 0, 128), F_.Sign, -0.5)
         mm(a("B2", 128, 128), a("GT"), a("ID"), True, True)
         tt(a("PJ"), a("B2", 128, 128), a("DEO"), A_.mult)
         tt(ind(a("JB"), a("JLU")), a("PJ"), a("LXM"), A_.add)
-        send(t, a("JB", 0, JW), a(C, 0, JW), T.RL[:, t * JW:(t + 1) * JW], "arr", "ra", "ls", 2.5)
+        due(t, "send")
+        send(t, a("JB", 0, JW), a(C, 0, JW), T.RL[:, t * JW:(t + 1) * JW], "arr", "ra", "ls", HOPJ)
         for h in range(2):
             scan(a("R", 256 * h, 256), a("SEGM", 0, 256), a("B%d" % h, 0, 256), 0.0, A_.mult, A_.max)
+        due(t, "keys")
         ts(a("KR"), a("R", 15, 32, 16), MAGIC, A_.add, MAGIC, A_.subtract)
         tt(a("DD"), a("R", 15, 32, 16), a("KR"), A_.subtract)
         scan(a("VC"), a("ALT"), a("DD"), 0.0, A_.mult, A_.add)
@@ -568,47 +606,51 @@ def rank_program(g, core, T, topo):
         scan(a("VB"), a("SEGM", 0, 512), a("HD"), 0.0, A_.mult, A_.add)
         for h in range(2):
             mm(a("B0", 256 + 8 * h, 8), a("VM", 128 * h, 128), a("BO", 0, 8, 16), True, True)
-        mm(a("B1", 256, 256), a("PM", 0, 128), a("CT"), True, False)
-        mm(a("B1", 256, 256), a("N2K"), SG, False, False)
-        for h in range(2):
-            mm(a("B1", 256 + 128 * h, 128), a("VM", 128 * h, 128), a("BO"), False, False)
-            mm(a("B1", 256 + 128 * h, 128), a("VB", 128 * h, 128), a("NI"), False, h == 1)
+        nb = 8 // J
+        mms([(a("B0", 272 + 2 * nb * j + nb * h, nb), a("VM", 128 * h, 128), a("BO", 16 * j, nb, XB), True, True) for j in range(J) for h in range(2)])
+        for i, bank in enumerate(("B4", "B1")[:J // 2]):
+            mm(a(bank), a("PM", 0, 128), a("CT", 512 * i, 512), True, False)
+            mms([(a(bank, 256 * j, 256), a("N2K"), SG, False, False) for j in range(2)])
+            mms([(a(bank, 256 * j + 128 * h, 128), a("VM", 128 * h, 128), a("BJ", 128 * (2 * i + j), 128), False, False) for j in range(2) for h in range(2)])
+            mms([(a(bank, 256 * j + 128 * h, 128), a("VB", 128 * h, 128), a("NI"), False, j + h == 2) for j in range(2) for h in range(2)])
+            ts(a("EE", 512 * i, 512), a(bank), 0.0, A_.is_equal, -4096.0, A_.mult)
+            scan(a("ES", 512 * i, 512), a("SEJ"), a("EE", 512 * i, 512), 0.0, A_.mult, A_.add)
         mm(a("B3", 0, 256), a("ONE", 0, 128, p=1), a("ROW", 0, 256), True, False)
         for h in range(2):
             mm(a("B3", 128 * h, 128), a("VB", 256 + 128 * h, 128), a("NQ"), False, h == 1)
         ts(a("GL"), a("B0", 256, 16), 1023.5 + XB, A_.add, V + XB - 1.0, A_.min)
-        ts(a("EE"), a("B1", 256, 256), 0.0, A_.is_equal, -4096.0, A_.mult)
-        scan(a("ES"), a("SEGM", 0, 256), a("EE"), 0.0, A_.mult, A_.add)
-        tt(a("W1"), a("B0", 256, 16), a("ES", 15, 16, 16), A_.add)
-        ts(a("SL", 0, 16, 2), a("W1"), 1023.5 + XB, A_.add, a("JC", 104, 1), A_.max)
+        tt(a("W1"), a("B0", 272, 16), a("ES", XB - 1, 16, XB), A_.add)
+        for j in range(J):
+            ts(a("SL", j, 2 * nb, J), a("W1", 2 * nb * j, 2 * nb), 1023.5 + XB, A_.add, a("JC", 104 + j, 1), A_.max)
         tt(a("FSG"), a("B3", 0, 256), a("FA"), A_.mult)
         tt(a("XN"), ind(a("W", 0, XB + V), a("GL")), a("FSG"), A_.add)
         ts(a("XC"), a("XN"), 0.0, A_.max, 63.0, A_.min)
-        for b in range(15, -1, -1):
-            copy(ind(a("W", 0, XB + V), a("SL", 2 * b, 1)), a("XC", 16 * b, 16))
+        for b in range(2 * nb - 1, -1, -1):
+            copy(ind(a("W", 0, XB + V), a("SL", J * b, J)), a("XC", XB * b, XB))
+            if b == 2 * nb - 1:
+                due(t, "moves")
         if not last:
             negate(t + 1)
-            cyclic(t + 1)
         else:
             dma("Y", T.yx[:], T.W[:, XB:XB + V], "st0", [a("W", XB, V)], [], 4.5)
         for c in range(NF):
-            for k in range(16):
-                mm(a("B5", CH * c, CH), a("ID"), a("S2", 16 * CH * c + k, CH, 16), k == 0, k == 15)
+            mms([(a("B5", CH * c, CH), a("ID"), a("S2", 16 * CH * c + k, CH, 16), k == 0, k == 15) for k in range(16)])
         act(a("FA2"), a("B5", 0, LF), F_.Relu, 1.0, -1.0)
         mm(a("B5", LF, LF), a("BO"), a("FA2"), True, True)
         act(a("YW", K, LF), a("B5", LF, LF), F_.Sign, -3.5)
+        due(t, "wake")
         if not last:
-            mm(a("B4", 256, 1), a("O32"), a("SGA"), True, True)
-            copy(a("AI", 0, 1), a("B4", 256, 1))
+            mm(a("B2", 256, 1), a("O32"), a("SGA"), True, True)
+            copy(a("AI", 0, 1), a("B2", 256, 1))
             ts(a("AI", 1, 1), a("AI", 0, 1), 3, A_.bitwise_and)
             tt(a("TT"), a("TH"), a("AI", 1, 1), A_.add)
             ts(a("NT1"), a("TT"), -1.0, A_.mult, 65.0, A_.add)
         ts(a("NT"), a("DR"), a("NN", t, 1), A_.is_gt, 1024.0, A_.mult)
         if last:
             ts(a("NTN"), a("DRN"), a("NN", t, 1), A_.is_gt, 1024.0, A_.mult)
-        mm(a("B4", 320, Q), a("ID"), a("DRN" if last else "DR"), True, False)
-        mm(a("B4", 320, Q), a("ID"), a("NTN" if last else "NT"), False, True)
-        tt(a("IXF"), a("B4", 320, Q), a("JC", Q if last else 0, Q), A_.min)
+        mm(a("B2", 320, Q), a("ID"), a("DRN" if last else "DR"), True, False)
+        mm(a("B2", 320, Q), a("ID"), a("NTN" if last else "NT"), False, True)
+        tt(a("IXF"), a("B2", 320, Q), a("JC", Q if last else 0, Q), A_.min)
         ts(a("IX"), a("IXF"), -1.0, A_.add)
         act(a("C%d" % (t + 1), 0 if last else JW, K), ind(a(C), a("IX")), F_.Identity, -OFF if last else 0.0)
         act(a("FW"), ind(a("YW"), a("PL")), F_.Identity, 3.0, 2.0)
@@ -625,15 +667,17 @@ def rank_program(g, core, T, topo):
     ts(a("YF"), a("B5", 2 * LF, Q), -6.0, A_.add, 0.0, A_.max)
     dma("Y", T.yf[:], T.YF[:], "st2", [a("YF")], [], 2.2)
     if "order" not in PLAN:
-        PLAN["order"] = plan(ops)
+        PLAN["order"] = plan(ops, dues)
     for i in PLAN["order"]:
         ops[i][6]()
     for q in cnt:
         g.wait_ge(T.sem["s" + q], cnt[q])
-    for i in range(4):
+    for i in range(5):
         g.wait_ge(T.sem["ld%d" % i], 16)
     for i in range(3):
         g.wait_ge(T.sem["st%d" % i], 16)
+    for i in range(4):
+        g.wait_ge(T.sem["sn%d" % i], 16)
     for t in range(RO):
         for s in ("ls", "arr", "nl", "na"):
             g.wait_ge(T.sem[s + str(t)], 8)

@@ -20,45 +20,51 @@ H = "float16"
 B, F, U, I = "bfloat16", "float32", "uint16", "int32"
 SHAPES = {
     B: {"W": WW, "S": 16 * LA, "M": 16 * LA, "Z": 16 * LA, "S2": 16 * LF, "YW": LW, "ONE": 512, "BO": 128, "NBO": 128, "TS": 128,
-        "NTS": 128, "ID": 128, "NI": 128, "I4": 128, "NI4": 128, "NK": 128, "I128": 128, "NQ": 128, "N2K": 128, "HI": 128, "NHI": 128,
-        "MZ": 128, "MA": 128, "MB": 128, "DC": 512, "SEGM": 1024, "RST": 1024, "I2K": 16, "NIN": 8, "RA": 512,
+        "NTS": 128, "ID": 128, "NI": 128, "I4": 128, "NI4": 128, "PK": 128, "NQ": 128, "N2K": 128, "HI": 128, "NHI": 128,
+        "X1": Q, "BT": 128, "NN": 8 * RO, "RN": 8 * RO, "MA": 128, "MB": 128, "DC": 512, "SEGM": 1024, "RST": 1024, "I2K": 16, "NIN": 8, "RA": 512,
         "RX": 128, "RY": 128, "MH": 512, "SE": 512, "MX": 512, "FL": 2 * Q, "PRE": 3 * Q, "XS": Q, "DR": Q, "DRN": Q, "NT": Q,
-        "NTN": Q, "LH": 384, "FW": K, "FWS": K, "FA": LA, "FA2": LF, "HB": LA, "BTM": 128, "CUM": 144, "GT": 128, "EE": 256 * J, "ES": 256 * J, "SEJ": 512, "BJ": 128 * J,
+        "NTN": Q, "LH": 384, "FW": K, "FWS": K, "FA": LA, "FA2": LF, "HB": LA, "BTM": 128, "CUM": 144, "GT": 128, "EE": 256 * J, "ES": 256 * J, "SEJ": 256, "BJ": 128 * J,
         "XN": 256, "XC": 256},
     H: {"CZ": LA, "HD": 512, "VB": 512, "VM": 256, "FSG": 256},
     F: {"C0": CW, "C1": CW, "C2": CW, "C3": K, "LN": LW, "TH": 1, "TT": 1, "NT1": 1, "O32": 128, "JC": 132, "P3": 3 * Q, "P4": 3 * Q,
-        "RS3": 3 * Q, "ALT": 32, "R": 512, "KR": 32, "DD": 32, "VC": 32, "W1": 16, "DEO": 128, "LXM": 128, "PJ": 128, "JB": 256,
-        "JL": 8, "NS": 4, "NN": 4, "RN": 4, "IXF": Q, "SGA": 1, "YF": Q, "RL": RO * JW, "SIL": 16},
-    U: {"OA": LA, "OF": LF, "PL": Q, "IX": Q, "L2": 16, "LT": 24, "GL": 16, "SL": 32, "JLU": 8},
-    I: {"CI": K, "FR": Q, "TI": 1, "AI": 2, "LQI": 16},
+        "RS3": 3 * Q, "ALT": 16, "R": 512, "KR": 32, "DD": 32, "VC": 32, "W1": 16, "DEO": 128, "LXM": 128, "PJ": 128, "JB": 256,
+        "JL": 8, "IXF": Q, "SGA": 1, "YF": Q, "RL": RO * JW, "SIL": 16},
+    U: {"OA": LA, "OF": LF, "PL": Q, "IX": Q, "L2": 8, "LT": 24, "GL": 16, "SL": 32, "JLU": 8},
+    I: {"CI": K, "FR": Q, "TI": 1, "AI": 2, "LQI": 8},
 }
 SCRATCH = {n: ("sbuf", [128, w], d) for d, tab in SHAPES.items() for n, w in tab.items()}
-SCRATCH.update({"PM": ("sbuf", [16, 512], B), "PN": ("sbuf", [16, 256], B), "CT": ("sbuf", [16, 256 * J], B), "CT0": ("sbuf", [16, 256], B),
+SCRATCH.update({"PM": ("sbuf", [16, 128], B), "PN": ("sbuf", [16, 64 + XB * (J + 1)], B), "CT": ("sbuf", [16, XB * J], B),
                 "PMF": ("sbuf", [16, 128], F), "TB": ("sbuf", [16, 132], F), "CU": ("sbuf", [16, 108], F), "CV": ("sbuf", [16, 8], F),
-                "KC": ("sbuf", [1, 256], H), "SN": ("sbuf", [128, LA], F), "ROW": ("sbuf", [1, 320], H)})
+                "KC": ("sbuf", [1, 256], H), "SN": ("sbuf", [128, LA], F), "ROW": ("sbuf", [1, 544], H)})
 for _i in range(8):
     SCRATCH["B%d" % _i] = ("psum", [128, 512], F)
 SEMAPHORES = ["sV", "sS", "sP", "sG"] + ["ld%d" % i for i in range(5)] + ["st%d" % i for i in range(3)] + ["sn%d" % i for i in range(4)] \
     + [s + str(i) for s in ("arr", "ls", "ra", "na", "nl", "rn") for i in range(RO)]
 
 
-CYC, GAT, SCA, WAKE, SLACK = 0.00083, 1.5, 3.5, 0.22, 0.1
-PEC, PASSES, HOPN, HOPJ = 0.0005, 8, 2.0, 2.6
-PLAN, SHORT, RLEN = {}, 0.0, 18.0
+CYC, PEC = np.array([0.00083, 0.0012, 0.00083]), np.array([0.00045, 0.0006, 0.0008])
+GAT, SCA, WAKES, WEIGHT = np.array([1.5, 1.9, 1.5]), np.array([3.5, 5.0, 3.5]), [0.22, 0.22, 0.18], [1.0, 0.35, 0.3]
+PASSES, SEED, JITTER, HOPN, HOPJ = 800, 1, 0.8, 2.0, 2.6
+PLAN, RLEN, STRETCH, SHIFT = {}, 18.0, 2.0, 2.0
+PULL = {("send", 2): 2.0}
 INORDER = "P"
 WAR = "P"
 XH = 1024
+FB = (64, 64, 64)
 D0 = {"A0": 0.0, "A1": 0.0, "A2": 1.6, "A3": 3.2, "F0": 3.1, "F1": 4.8, "F2": 6.7, "lit": 1.7, "viol": 6.3, "send": 9.0, "keys": 9.5,
       "wake": 9.5, "lanes": 13.0, "moves": 14.0, "out": 15.0}
 DUE = [dict(D0), dict(D0), dict(D0)]
-GA = [(("S", 64), ("V", 64), ("S", 96), ("V", 32))] * RO
+GA = [(("S", 64), ("V", 64), ("S", 64), ("V", 32), ("S", 32))] * RO
 GF = [(("S", 64), ("S", 64), ("S", 64))] * RO
 NEGV = [V, 1408, 1408]
 KB = ((0, 0, 128), (1, 0, 128))
 
 
-def plan(ops, dues):
+def plan(ops, dues, parts):
     n = len(ops)
+    times = [[(np.zeros(len(WAKES)) + x).tolist() for x in o[4:6]] for o in ops]
+    ops = [o[:4] + (times[i][0][0], times[i][1][0], o[6]) for i, o in enumerate(ops)]
+    WAKE = WAKES[0]
     pred = [dict() for _ in range(n)]
     succ = [[] for _ in range(n)]
     hist = {}
@@ -82,15 +88,23 @@ def plan(ops, dues):
                 h.append((m, w, i))
                 if ps and len(h) > 150:
                     h[:] = h[-150:]
+    above = [0] * n
     for i in range(n):
-        for j, lat in pred[i].items():
+        for j in sorted(pred[i], reverse=True):
+            if above[i] >> j & 1 and ops[j][4] == ops[j][5]:
+                del pred[i][j]
+            else:
+                above[i] |= above[j] | 1 << j
+    preds = [list(p.items()) for p in pred]
+    for i in range(n):
+        for j, lat in preds[i]:
             succ[j].append((i, lat))
     pr = [0.0] * n
     for i in range(n - 1, -1, -1):
         pr[i] = ops[i][5] + max([lat + pr[k] for k, lat in succ[i]] + [0.0])
 
     def place(key, back):
-        before, after = (succ, [list(p.items()) for p in pred]) if back else ([list(p.items()) for p in pred], succ)
+        before, after = (succ, preds) if back else (preds, succ)
         left, est, start, busy = [len(p) for p in before], [0.0] * n, [0.0] * n, {}
         ready = [i for i in range(n) if not left[i]]
         while ready:
@@ -110,19 +124,46 @@ def plan(ops, dues):
                     ready.append(i)
         return start
 
+    def replay(order, m):
+        done, free = [0.0] * n, {}
+        for i in order:
+            s = max([free.get(ops[i][0], 0.0)] + [done[j] + (WAKES[m] if lat else 0.0) for j, lat in preds[i]])
+            free[ops[i][0]] = s + times[i][0][m]
+            done[i] = s + times[i][1][m]
+        return max(done)
+
     key, best = [0.0] * n, None
     for i in range(n - 1, -1, -1):
         key[i] = min([dues.get(i, 200.0)] + [key[k] - lat - ops[i][5] for k, lat in succ[i]])
-    for _ in range(PASSES):
+    rng = np.random.default_rng(SEED)
+    for it in range(PASSES):
         start = place(key, False)
-        end = max(start[i] + ops[i][5] for i in range(n))
-        if best is None or end < best[0]:
-            best = (end, start)
-        late = place([-start[i] - ops[i][5] for i in range(n)], True)
-        key = [-late[i] - ops[i][4] - (SHORT if ops[i][4] < 0.3 else 0.0) for i in range(n)]
-    PLAN["end"] = best[0]
+        order = sorted(range(n), key=lambda i: (round(start[i], 6), i))
+        ends = [replay(order, m) for m in range(len(WAKES))]
+        score = sum(e * w for e, w in zip(ends, WEIGHT))
+        if best is None or score < best[0]:
+            best = (score, start, order, ends)
+            kept = key
+        if it < 8 or it % 16 == 0:
+            base = start if it < 8 else best[1]
+            late = place([-base[i] - ops[i][5] for i in range(n)], True)
+            key = [-late[i] - ops[i][4] - PULL.get(parts[i][:2], 0.0) for i in range(n)]
+            for i in range(n - 1, -1, -1):
+                key[i] = min([key[i]] + [key[k] - lat - ops[i][5] for k, lat in succ[i]])
+        elif it % 2:
+            part, by = parts[int(rng.integers(n))], float(rng.normal(0.0, SHIFT))
+            key = [kept[i] + (by if parts[i] == part else 0.0) for i in range(n)]
+            for i in range(n - 1, -1, -1) if by < 0 else range(n):
+                if by < 0:
+                    key[i] = min([key[i]] + [key[k] - lat - ops[i][5] for k, lat in succ[i]])
+                else:
+                    key[i] = max([key[i]] + [key[k] + lat + ops[k][5] for k, lat in preds[i]])
+        else:
+            lo, jitter = rng.random() * best[3][0], rng.normal(0.0, JITTER, n)
+            key = [kept[i] + (float(jitter[i]) if lo < best[1][i] < lo + STRETCH else 0.0) for i in range(n)]
+    PLAN["end"] = best[3]
     PLAN["dbg"] = (ops, pr, succ, best[1])
-    return sorted(range(n), key=lambda i: (round(best[1][i], 6), i))
+    return best[2]
 
 
 def route(topo, src, dst):
@@ -148,7 +189,7 @@ def relay_program(g, core, T, topo):
                 rid, pid = topo.addr(dst, core)
                 m = emask(topo, core, dst)
                 g.wait_ge(T.sem["rn%d" % t], 8)
-                g.remote_dma(T.NN[:, t:t + 1], T.RN[:, t:t + 1], T.sem["na%d" % t], T.sem["nl%d" % t], pid, rid, m)
+                g.remote_dma(T.NN[:, 8 * t:8 * t + 2], T.RN[:, 8 * t:8 * t + 2], T.sem["na%d" % t], T.sem["nl%d" % t], pid, rid, m)
                 g.wait_ge(T.sem["ra%d" % t], 8)
                 g.remote_dma(T["C%d" % t][:, 0:JW], T.RL[:, t * JW:(t + 1) * JW], T.sem["arr%d" % t], T.sem["ls%d" % t], pid, rid, m)
     for r in range(N):
@@ -235,10 +276,14 @@ def rank_program(g, core, T, topo):
 
     ops = []
 
-    dues = {}
+    dues, parts, now = {}, [], [-1]
+
+    def step(name):
+        parts.extend([(name, now[0], len(parts))] * (len(ops) - len(parts)))
 
     def due(t, name):
         dues[len(ops) - 1] = RLEN * t + DUE[t][name]
+        step(name)
 
     def run(q, fn, out, ins, cost):
         writes = acc(out)[:1] if isinstance(out, tuple) else out
@@ -263,6 +308,11 @@ def rank_program(g, core, T, topo):
             need(q, None, reads, writes)
             eng[q].dma_start(out, in_).then_inc(T.sem[sem], 16)
             note(tag, reads, writes, sem, 16, dict(known[q]))
+        if sem[:2] == "st":
+            net = ("", tag, 1)
+            ops.append((q, tag, reads, [net], 0.05, 1.8, issue))
+            ops.append(("D", tag + "x", [net], [], dur - 1.8, dur - 1.8, lambda: None))
+            return
         ops.append((q, tag, reads, writes, 0.0 if sem[0] == "l" else 0.05, dur, issue))
 
     def width(x):
@@ -340,7 +390,7 @@ def rank_program(g, core, T, topo):
             g.remote_dma(land[0] if first is None else relay, src[0], T.sem[(arr if first is None else ra) + str(t)], T.sem[ls + str(t)],
                          pid, rid, emask(topo, core, to))
             note("r%s%d" % (ls, t), [src], [], ls + str(t), 8, dict(known["G"]))
-        ops.append(("G", "r%s%d" % (ls, t), [src], [net], 0.3, lat + (0.0 if t else 1.0), issue))
+        ops.append(("G", "r%s%d" % (ls, t), [src], [net], 1.3 if (t, arr) == (0, "na") else 0.3, lat + (0.0 if t else 1.0), issue))
         ops.append(("N", "q%s%d" % (arr, t), [net], [land], 0.0, 0.0 if first is None else lat + (0.0 if t else 1.0),
                     lambda: note("q%s%d" % (arr, t), [], [land], arr + str(t), 8, {})))
 
@@ -359,8 +409,8 @@ def rank_program(g, core, T, topo):
     sel(a("BO"), a("RX"), [[16, 8], [0, 16]], A_.is_ge, 0.0, 15, -1)
     sel(a("TS"), a("BO"), [[1, 128]], A_.is_ge, 0.0, -1, -1)
     sel(a("ID"), a("ONE", 0, 128), [[-1, 128]], A_.is_equal, 0.0, 0, 1)
-    sel(a("PM", 0, 256), a("ONE", 0, 256, p=16), [[0, 16], [1, 16]], A_.is_equal, 0.0, 0, -1)
-    copy(a("PMF"), a("PM", 0, 128))
+    sel(a("PM"), a("ONE", 0, 128, p=16), KP, A_.is_equal, 0.0, 0, -1)
+    copy(a("PMF"), a("PM"))
     for name, c in (("NI", -1.0), ("I4", 4096.0), ("NI4", -4096.0)):
         ts(a(name), a("ID"), c, A_.mult)
     ts(a("NTS"), a("TS"), -1.0, A_.mult)
@@ -381,6 +431,9 @@ def rank_program(g, core, T, topo):
     fill(a("ROW", 0, 256), 8.0 + 87 * 32)
     fill(a("ROW", 256, Q), 4096.0)
     fill(a("ROW", 256 + Q, 16), 0.0)
+    fill(a("ROW", 416, 128), -4164.0)
+    fill(a("ROW", 320, Q), -6.5 / 8)
+    fill(a("ROW", 320 + Q, Q), -9.5 / 8)
 
     fill(a("SN"), 2 * V + OFF)
 
@@ -404,13 +457,10 @@ def rank_program(g, core, T, topo):
                 mm(a("B6", 256 + 128 * c, 128), a("ID"), a(m), j == 0, j == 2)
         act(a("MH", 256 * (t - 1), 256), a("B6", 256, 256), F_.Identity)
 
-    def lists(t, x, off):
+    def lists(t):
         fa, fd = a("FL", 0, Q), a("FL", Q, Q)
-        ts(fa, x, off + 0.5, A_.is_lt)
-        ts(fd, x, off + 3.5, A_.is_gt)
         scan(a("PRE", 0, Q), a("ONE", 0, Q), fa, 0.0, A_.mult, A_.subtract)
         scan(a("PRE", Q, Q), fa, fd, 0.0, A_.add, A_.add)
-        ts(a("XS"), x, -off, A_.add, 0.0, A_.max)
         mm(a("B6", 0, Q), a("NI4"), fa, False, False)
         mm(a("B6", Q, Q), a("I4"), fa, False, False)
         mm(a("B6", Q, Q), a("I4"), fd, False, False)
@@ -437,6 +487,7 @@ def rank_program(g, core, T, topo):
         ts(a("OF"), a("LN", K, LF), 0.25 - OFF, A_.add)
         if t < RO - 1:
             sentinels(t)
+        step("offsets")
         scan(a("PRE", 2 * Q, Q), a("ONE", 0, Q), fd, 0.0, A_.mult, A_.add)
         mm(a("B7", 0, Q + 1), a("ONE", 0, 128, p=1), a("ROW", 256, Q + 1), True, False)
         mm(a("B7", 0, Q), a("NI4"), fd, False, False)
@@ -474,12 +525,16 @@ def rank_program(g, core, T, topo):
     consts_of_lists(0)
     for p in range(16):
         ts(a("C0", JW + p, Q, 16), a("CI", Q * p, Q), OFF, A_.add)
-    lists(0, a("FR"), 0.0)
+    ts(a("FL", 0, Q), a("FR"), 0.5, A_.is_lt)
+    ts(a("FL", Q, Q), a("FR"), 3.5, A_.is_gt)
+    ts(a("XS"), a("FR"), 0.125, A_.mult)
+    lists(0)
     for lo, n in ((0, XH), (XH, V - XH)):
         ts(a("W", XB + V + lo, n), a("W", XB + lo, n), -1.0, A_.mult, 63.0, A_.add)
     ts(a("TH"), a("TI"), 64.0, A_.add)
     ts(a("TT"), a("TI"), 64.0, A_.add)
     ts(a("NT1"), a("TT"), -1.0, A_.mult, 65.0, A_.add)
+    step("first")
     fill(a("W", 0, XB), 0.0)
     fill(a("SEGM"), 1.0)
     fill(a("SEGM", 0, 64, 16), 0.0)
@@ -492,27 +547,31 @@ def rank_program(g, core, T, topo):
     fill(a("CUM", 0, 16), 0.0)
     fill(a("O32"), 1.0 / 32)
     fill(a("ALT"), 32.0)
-    fill(a("ALT", 0, 16, 2), 0.0)
-    for name, c in (("NK", -1.0 / 1024), ("I128", 1.0 / 128), ("NQ", -0.25), ("N2K", -2048.0), ("HI", 0.5), ("NHI", -0.5)):
+    fill(a("ALT", 0, 8, 2), 0.0)
+    for name, c in (("PK", 1.0 / 1024), ("NQ", -0.25), ("N2K", -2048.0), ("HI", 0.5), ("NHI", -0.5)):
         ts(a(name), a("ID"), c, A_.mult)
     ts(a("NBO"), a("BO"), -1.0, A_.mult)
     ts(a("I2K"), a("BO", 0, 16, 8), 2048.0, A_.mult)
     ts(a("NIN"), a("BO", 0, 8, 16), -1.0, A_.mult)
-    P16 = [[0, 16], [1, 16]]
-    sel(a("PN"), a("ONE", 0, 256, p=16), P16, A_.is_ge, 0.0, 0, -1)
-    sel(a("CT0"), a("PN"), P16, A_.not_equal, 1024.0, 0, -1)
-    sel(a("PM", 256, 256), a("CT0"), P16, A_.not_equal, 0.0, -15, -16)
-    mm(a("B0"), a("PM", 0, 128), a("PM"), True, True)
+    step("fill")
+    P16 = [[1, 16]]
+    sel(a("PN", 0, 16), a("ONE", 0, 16, p=16), P16, A_.is_ge, 0.0, 0, -1)
+    sel(a("PN", 16, 16), a("PN", 0, 16), P16, A_.not_equal, 1024.0, 0, -1)
+    sel(a("PN", 32, 16), a("PN", 16, 16), P16, A_.not_equal, 2.0 ** -13, -15, 0)
+    sel(a("PN", 48, 16), a("PN", 32, 16), P16, A_.not_equal, 0.125, -30, 1)
+    mms([(a("B0", 128 * j, 128), a("PM"), a("PM"), True, True) for j in range(2)]
+        + [(a("B0", 256 + 16 * j, 16), a("PM"), a("PN", 48, 16), True, True) for j in range(16)])
     act(a("DC"), a("B0"), F_.Identity)
-    ts(a("MZ"), a("NK"), a("DC", 0, 1), A_.mult)
-    iota(a("PN"), [[0, 256]], 2048, 0)
+    step("mask")
+    iota(a("PN", 64, XB), [[0, XB]], 2048, 0)
     for j in range(J):
-        sel(a("CT0"), a("PN"), [[0, 16 // J], [-100, J], [-1, 16]], A_.is_ge, 8192.0, 100 * j, 1)
-        sel(a("CT", 256 * j, 256), a("CT0"), [[0, 16 // J], [100, J], [1, 16]], A_.not_equal, -2048.0, -100 * j, -1)
-        sel(a("BTM"), a("ONE", 0, 128), [[-XB, 8 // J], [0, XB]], A_.is_ge, 0.0, -16 * j, 1)
-        sel(a("BJ", 128 * j, 128), a("BTM"), [[XB, 8 // J], [0, XB]], A_.is_ge, 0.0, 16 * j + 15, -1)
+        sel(a("PN", 64 + XB * (j + 1), XB), a("PN", 64, XB), [[-100, J], [-1, 16]], A_.is_ge, 8192.0, 100 * j, 1)
+        sel(a("CT", XB * j, XB), a("PN", 64 + XB * (j + 1), XB), [[100, J], [1, 16]], A_.not_equal, -2048.0, -100 * j, -1)
+        sel(a("LH", 128 * j, 128), a("ONE", 0, 128), [[-XB, 8 // J], [0, XB]], A_.is_ge, 0.0, -16 * j, 1)
+        sel(a("BJ", 128 * j, 128), a("LH", 128 * j, 128), [[XB, 8 // J], [0, XB]], A_.is_ge, 0.0, 16 * j + 15, -1)
+    step("pairs")
     fill(a("SEJ"), 1.0)
-    fill(a("SEJ", 0, 512 // XB, XB), 0.0)
+    fill(a("SEJ", 0, 256 // XB, XB), 0.0)
     iota(a("TB", 0, Q), [[16, Q]], JW + 1, 1)
     iota(a("TB", Q, Q), [[1, 16], [256, 3]], JW + 1, 16)
     iota(a("TB", 2 * Q, 8), [[16, 8]], JW - 255, 1)
@@ -521,11 +580,12 @@ def rank_program(g, core, T, topo):
     mm(a("B1", 0, 132), a("PMF"), a("TB"), True, True)
     act(a("JC"), a("B1", 0, 132), F_.Identity)
     copy(a("LT"), a("JC", 108, 24))
-    iota(a("LQI"), [[2, 16]], 1, 0)
+    iota(a("LQI"), [[2, 8]], 1, 0)
     copy(a("L2"), a("LQI"))
     sel(a("MA"), a("TS"), [[-1, 128]], A_.not_equal, -255.0, 0, 1)
     sel(a("GT"), a("BO"), [[-1, 128]], A_.is_ge, 0.0, 0, 1)
     sel(a("MB"), a("GT"), [[-1, 128]], A_.not_equal, 256.0, 0, 1)
+    step("joint")
     ts(a("EE", 0, 128), a("ID"), 2.0, A_.mult)
     ts(a("EE", 128, 128), a("ID"), -64.0, A_.mult)
     fill(a("EE", 256, 128), 0.0)
@@ -538,9 +598,12 @@ def rank_program(g, core, T, topo):
     for t in range(RO):
         C, last = "C%d" % t, t == RO - 1
         SG = a("YW", 0, LA)
+        step("dead")
+        now[0] = t
         if not last:
             cyclic(t + 1)
             consts_of_lists(t + 1)
+            step("cyclic")
         for frozen, who in ((False, GA[t]), (True, GF[t])):
             lo = 0
             for q, n in who:
@@ -566,23 +629,25 @@ def rank_program(g, core, T, topo):
             scan(a("M", lo, 16 * CH), a("SEGM"), a("S", lo, 16 * CH), 0.0, A_.mult, A_.max)
             ts(a("FA", CH * c, CH), a("M", lo + 15, CH, 16), a("TT"), A_.is_lt, EPS, A_.max)
             tt(a("S", lo, CH, 16), a("FA", CH * c, CH), a("M", lo, CH, 16), A_.mult)
+            step("rows")
             scan(a("Z", lo, 16 * CH), a("RST"), a("S", lo, 16 * CH), 1.0, A_.mult, A_.min)
+            step("mask")
         for h, m0, n in KB:
             mms([(a("B%d" % h, k, 16, 16, p=n, p0=m0), a("Z", 16 * (128 * h + m0) + k, n, 16), a("I2K"), False, k == 15 and m0 + n == 128)
                  for k in range(16)])
+        step("sums")
         mm(a("B4", 0, LA), a("BO"), a("FA"), True, True)
         act(SG, a("B4", 0, LA), F_.Sign, -3.5, 1.0, a("SGA"))
         due(t, "viol")
-        mm(a("B3", 256, 128), a("ID"), a("DC", 0, 128), True, False)
-        mm(a("B3", 256, 128), a("ID"), a("YW", 0, 128, 2), False, False)
-        mm(a("B3", 256, 128), a("ID"), a("YW", 1, 128, 2), False, True)
-        ts(a("BTM"), a("B3", 256, 128), 2.5, A_.is_gt)
+        mm(a("B3", 256, 128), a("ONE", 0, 128, p=1), a("ROW", 416, 128), True, False)
+        mm(a("B3", 256, 128), a("I4"), a("DC", 0, 128), False, False)
+        mms([(a("B3", 128, 128), a("BO"), a("FA", 0, 128, 2), False, False), (a("B3", 256, 128), a("BO"), a("FA", 1, 128, 2), False, True)])
+        ts(a("BT"), a("B3", 128, 128), 4.0, A_.min, -16.0, A_.mult)
+        tt(a("BTM"), a("B3", 256, 128), a("BT"), A_.is_ge)
         scan(a("CUM", 16, 128), a("ONE", 0, 128), a("BTM"), 0.0, A_.mult, A_.add)
-        mm(a("B3", 392, 1), a("BO"), a("CUM", 143, 1), True, True)
+        send(t, a("CUM", 142, 2), a("NN", 8 * t, 2), T.RN[:, 8 * t:8 * t + 2], "na", "rn", "nl", HOPN)
         mm(a("B3", 384, 8), a("MA"), a("CUM", 31, 8, 16), True, False)
         mm(a("B3", 384, 8), a("MB"), a("CUM", 15, 8, 16), False, True)
-        copy(a("NS", t, 1), a("B3", 392, 1))
-        send(t, a("NS", t, 1), a("NN", t, 1), T.RN[:, t:t + 1], "na", "rn", "nl", HOPN)
         tt(a("JL"), a("B3", 384, 8), a("JC", 2 * Q, 8), A_.min)
         ts(a("JLU"), a("JL"), 255.0, A_.add)
         for k0 in range(0, 16, 4):
@@ -594,37 +659,38 @@ def rank_program(g, core, T, topo):
         tt(ind(a("JB"), a("JLU")), a("PJ"), a("LXM"), A_.add)
         due(t, "send")
         send(t, a("JB", 0, JW), a(C, 0, JW), T.RL[:, t * JW:(t + 1) * JW], "arr", "ra", "ls", HOPJ)
-        for h in range(2):
-            scan(a("R", 256 * h, 256), a("SEGM", 0, 256), a("B%d" % h, 0, 256), 0.0, A_.mult, A_.max)
-        due(t, "keys")
-        ts(a("KR"), a("R", 15, 32, 16), MAGIC, A_.add, MAGIC, A_.subtract)
-        tt(a("DD"), a("R", 15, 32, 16), a("KR"), A_.subtract)
-        scan(a("VC"), a("ALT"), a("DD"), 0.0, A_.mult, A_.add)
-        tt(a("HD", 256, 16, 16), a("KR", 0, 16, 2), a("KR", 1, 16, 2), A_.subtract)
-        tt(a("VM"), ind(a("VC"), a("L2")), DM, A_.mult)
-        copy(a("HD", 0, 16, 16), a("VC", 1, 16, 2))
-        scan(a("VB"), a("SEGM", 0, 512), a("HD"), 0.0, A_.mult, A_.add)
-        for h in range(2):
-            mm(a("B0", 256 + 8 * h, 8), a("VM", 128 * h, 128), a("BO", 0, 8, 16), True, True)
         nb = 8 // J
-        mms([(a("B0", 272 + 2 * nb * j + nb * h, nb), a("VM", 128 * h, 128), a("BO", 16 * j, nb, XB), True, True) for j in range(J) for h in range(2)])
-        for i, bank in enumerate(("B4", "B1")[:J // 2]):
-            mm(a(bank), a("PM", 0, 128), a("CT", 512 * i, 512), True, False)
-            mms([(a(bank, 256 * j, 256), a("N2K"), SG, False, False) for j in range(2)])
-            mms([(a(bank, 256 * j + 128 * h, 128), a("VM", 128 * h, 128), a("BJ", 128 * (2 * i + j), 128), False, False) for j in range(2) for h in range(2)])
-            mms([(a(bank, 256 * j + 128 * h, 128), a("VB", 128 * h, 128), a("NI"), False, j + h == 2) for j in range(2) for h in range(2)])
-            ts(a("EE", 512 * i, 512), a(bank), 0.0, A_.is_equal, -4096.0, A_.mult)
-            scan(a("ES", 512 * i, 512), a("SEJ"), a("EE", 512 * i, 512), 0.0, A_.mult, A_.add)
-        mm(a("B3", 0, 256), a("ONE", 0, 128, p=1), a("ROW", 0, 256), True, False)
-        for h in range(2):
-            mm(a("B3", 128 * h, 128), a("VB", 256 + 128 * h, 128), a("NQ"), False, h == 1)
-        ts(a("GL"), a("B0", 256, 16), 1023.5 + XB, A_.add, V + XB - 1.0, A_.min)
-        tt(a("W1"), a("B0", 272, 16), a("ES", XB - 1, 16, XB), A_.add)
-        for j in range(J):
-            ts(a("SL", j, 2 * nb, J), a("W1", 2 * nb * j, 2 * nb), 1023.5 + XB, A_.add, a("JC", 104 + j, 1), A_.max)
-        tt(a("FSG"), a("B3", 0, 256), a("FA"), A_.mult)
-        tt(a("XN"), ind(a("W", 0, XB + V), a("GL")), a("FSG"), A_.add)
-        ts(a("XC"), a("XN"), 0.0, A_.max, 63.0, A_.min)
+        for h in (1, 0):
+            key, same, vm = "B%d" % h, "B4" if h else "B7", a("VM", 128 * h, 128)
+            scan(a("R", 256 * h, 256), a("SEGM", 0, 256), a(key, 0, 256), 0.0, A_.mult, A_.max)
+            due(t, "keys")
+            ends = a("R", 256 * h + 15, 16, 16)
+            ts(a("KR", 16 * h, 16), ends, MAGIC, A_.add, MAGIC, A_.subtract)
+            tt(a("DD", 16 * h, 16), ends, a("KR", 16 * h, 16), A_.subtract)
+            scan(a("VC", 16 * h, 16), a("ALT"), a("DD", 16 * h, 16), 0.0, A_.mult, A_.add)
+            tt(a("HD", 256 * h + 128, 8, 16), a("KR", 16 * h, 8, 2), a("KR", 16 * h + 1, 8, 2), A_.subtract)
+            copy(a("HD", 256 * h, 8, 16), a("VC", 16 * h + 1, 8, 2))
+            tt(vm, ind(a("VC", 16 * h, 16), a("L2")), a("DC", 0, 128), A_.mult)
+            scan(a("VB", 256 * h, 256), a("SEGM", 0, 256), a("HD", 256 * h, 256), 0.0, A_.mult, A_.add)
+            step("chosen")
+            mms([(a(key, 256, 8), vm, a("BO", 0, 8, 16), True, True)]
+                + [(a(key, 264 + nb * j, nb), vm, a("BO", 16 * j, nb, XB), True, True) for j in range(J)])
+            mms([(a(same, 256 + XB * b, XB), a("PM"), a("CT", XB * (b // nb), XB), b == 0, False) for b in range(8)])
+            mms([(a(same, 256 + 128 * j, 128), a("N2K"), a("YW", 128 * h, 128), False, False) for j in range(J)])
+            mms([(a(same, 256 + 128 * j, 128), vm, a("BJ", 128 * j, 128), False, False) for j in range(J)])
+            mms([(a(same, 256 + 128 * j, 128), a("VB", 256 * h, 128), a("NI"), False, j == J - 1) for j in range(J)])
+            mms([(a(key, 384, 128), a("ONE", 0, 128, p=1), a("ROW", 0, 128), True, False), (a(key, 384, 128), a("VB", 256 * h + 128, 128), a("NQ"), False, True)])
+            ts(a("GL", 8 * h, 8), a(key, 256, 8), 1023.5 + XB, A_.add, V + XB - 1.0, A_.min)
+            tt(a("FSG", 128 * h, 128), a(key, 384, 128), a("FA", 128 * h, 128), A_.mult)
+            tt(a("XN", 128 * h, 128), ind(a("W", 0, XB + V), a("GL", 8 * h, 8)), a("FSG", 128 * h, 128), A_.add)
+            ts(a("XC", 128 * h, 128), a("XN", 128 * h, 128), 0.0, A_.max, 63.0, A_.min)
+            step("new%d" % h)
+            ts(a("EE", 256 * h, 256), a(same, 256, 256), 0.0, A_.is_equal, -4096.0, A_.mult)
+            scan(a("ES", 256 * h, 256), a("SEJ"), a("EE", 256 * h, 256), 0.0, A_.mult, A_.add)
+            tt(a("W1", 8 * h, 8), a(key, 264, 8), a("ES", 256 * h + XB - 1, 8, XB), A_.add)
+            for j in range(J):
+                ts(a("SL", 8 * h + j, nb, J), a("W1", 8 * h + nb * j, nb), 1023.5 + XB, A_.add, a("JC", 104 + j, 1), A_.max)
+            step("lowest%d" % h)
         for b in range(2 * nb - 1, -1, -1):
             copy(ind(a("W", 0, XB + V), a("SL", J * b, J)), a("XC", XB * b, XB))
             if b == 2 * nb - 1:
@@ -632,9 +698,12 @@ def rank_program(g, core, T, topo):
         if not last:
             negate(t + 1)
         else:
-            dma("Y", T.yx[:], T.W[:, XB:XB + V], "st0", [a("W", XB, V)], [], 4.5)
-        for c in range(NF):
-            mms([(a("B5", CH * c, CH), a("ID"), a("S2", 16 * CH * c + k, CH, 16), k == 0, k == 15) for k in range(16)])
+            dma("Y", T.yx[:], T.W[:, XB:XB + V], "st0", [a("W", XB, V)], [], 3.7)
+        step("moves")
+        lo = 0
+        for n in FB:
+            mms([(a("B5", lo, n), a("ID"), a("S2", 16 * lo + k, n, 16), k == 0, k == 15) for k in range(16)])
+            lo += n
         act(a("FA2"), a("B5", 0, LF), F_.Relu, 1.0, -1.0)
         mm(a("B5", LF, LF), a("BO"), a("FA2"), True, True)
         act(a("YW", K, LF), a("B5", LF, LF), F_.Sign, -3.5)
@@ -645,29 +714,38 @@ def rank_program(g, core, T, topo):
             ts(a("AI", 1, 1), a("AI", 0, 1), 3, A_.bitwise_and)
             tt(a("TT"), a("TH"), a("AI", 1, 1), A_.add)
             ts(a("NT1"), a("TT"), -1.0, A_.mult, 65.0, A_.add)
-        ts(a("NT"), a("DR"), a("NN", t, 1), A_.is_gt, 1024.0, A_.mult)
+        step("count")
+        come = a("B2", 300, 1)
+        mm(come, a("BO"), a("NN", 8 * t + 1, 1), True, True)
+        ts(a("NT"), a("DR"), come, A_.is_gt, 1024.0, A_.mult)
         if last:
-            ts(a("NTN"), a("DRN"), a("NN", t, 1), A_.is_gt, 1024.0, A_.mult)
+            ts(a("NTN"), a("DRN"), come, A_.is_gt, 1024.0, A_.mult)
         mm(a("B2", 320, Q), a("ID"), a("DRN" if last else "DR"), True, False)
         mm(a("B2", 320, Q), a("ID"), a("NTN" if last else "NT"), False, True)
         tt(a("IXF"), a("B2", 320, Q), a("JC", Q if last else 0, Q), A_.min)
         ts(a("IX"), a("IXF"), -1.0, A_.add)
         act(a("C%d" % (t + 1), 0 if last else JW, K), ind(a(C), a("IX")), F_.Identity, -OFF if last else 0.0)
+        step("come")
         act(a("FW"), ind(a("YW"), a("PL")), F_.Identity, 3.0, 2.0)
         for j in range(3):
             scan(a("FWS", 256 * j, 256), a("FW", 256 * j, 256), CWM, 0.0, A_.max, A_.mult)
-        X1 = a("B5", 2 * LF, Q)
-        mm(X1, a("ID"), a("XS"), True, False)
-        mm(X1, a("I128"), a("NT"), False, False)
-        mm(X1, a("MZ"), a("FWS", 14, Q, 16), False, False)
-        mm(X1, a("NK"), a("FWS", 15, Q, 16), False, True)
+        y = a("FWS", 15, Q, 16)
+        mm(a("B5", 384, 2 * Q), a("ONE", 0, 128, p=1), a("ROW", 320, 2 * Q), True, False)
+        mms([(a("B5", 384 + Q * j, Q), a("ID"), a("XS"), False, False) for j in range(2)])
+        mms([(a("B5", 384 + Q * j, Q), a("PK"), a("NT"), False, j == 1) for j in range(2)])
         if not last:
-            lists(t + 1, X1, 6.0)
-    dma("S", T.yc[:], T.C3[:], "st1", [a("C3")], [], 4.0)
-    ts(a("YF"), a("B5", 2 * LF, Q), -6.0, A_.add, 0.0, A_.max)
+            tt(a("FL", 0, Q), a("B5", 384, Q), y, A_.is_lt)
+            tt(a("FL", Q, Q), a("B5", 384 + Q, Q), y, A_.is_gt)
+        tt(a("X1"), a("B5", 384, Q), y, A_.subtract)
+        ts(a("XS"), a("X1"), 1.0 / 16, A_.add, 0.0, A_.max)
+        if not last:
+            lists(t + 1)
+    dma("S", T.yc[:], T.C3[:], "st1", [a("C3")], [], 3.3)
+    ts(a("YF"), a("XS"), 8.0, A_.mult)
     dma("Y", T.yf[:], T.YF[:], "st2", [a("YF")], [], 2.2)
     if "order" not in PLAN:
-        PLAN["order"] = plan(ops, dues)
+        step("end")
+        PLAN["order"] = plan(ops, dues, parts)
     for i in PLAN["order"]:
         ops[i][6]()
     for q in cnt:

@@ -4,63 +4,70 @@ from concourse.mybir import dt, AluOpType, AxisListType, ActivationFunctionType
 A_, F_ = AluOpType, ActivationFunctionType
 N, V, K, LA, LF, RO, AS, FS = 8, 2048, 768, 256, 192, 3, 170, 255
 Q = K // 16
-J = 2
+J = 4
 XB = 16 * J
-SB = XB + 2 * V
-WW = SB + 16
+SB = 2 * V
+DU = SB + 16
+WW = DU + 2 * XB
 LW = 2 * K + 880
 JW = 128
-CW = JW + K
+CW = 2 * JW + K
 OFF = 64.0
+NW = 10
 CH = 64
 NA, NF = LA // CH, LF // CH
-EPS, BIGM, MAGIC = 2.0 ** -60, 2.0 ** 70, 1.5 * 2.0 ** 29
+MAGIC = 1.5 * 2.0 ** 23
+UN = 2.0 ** -10
 H = "float16"
 
 B, F, U, I = "bfloat16", "float32", "uint16", "int32"
 SHAPES = {
-    B: {"W": WW, "S": 16 * LA, "M": 16 * LA, "Z": 16 * LA, "S2": 16 * LF, "YW": LW, "ONE": 512, "BO": 128, "NBO": 128, "TS": 128,
-        "NTS": 128, "ID": 128, "NI": 128, "I4": 128, "NI4": 128, "PK": 128, "NQ": 128, "N2K": 128, "HI": 128, "NHI": 128,
-        "X1": Q, "BT": 128, "NN": 8 * RO, "RN": 8 * RO, "MA": 128, "MB": 128, "DC": 512, "SEGM": 1024, "RST": 1024, "I2K": 16, "NIN": 8, "RA": 512,
-        "RX": 128, "RY": 128, "MH": 512, "SE": 512, "MX": 512, "FL": 2 * Q, "PRE": 3 * Q, "XS": Q, "DR": Q, "DRN": Q, "NT": Q,
-        "NTN": Q, "LH": 384, "FW": K, "FWS": K, "FA": LA, "FA2": LF, "HB": LA, "BTM": 128, "CUM": 144, "GT": 128, "EE": 256 * J, "ES": 256 * J, "SEJ": 256, "BJ": 128 * J,
-        "XN": 256, "XC": 256},
-    H: {"CZ": LA, "HD": 512, "VB": 512, "VM": 256, "FSG": 256},
-    F: {"C0": CW, "C1": CW, "C2": CW, "C3": K, "LN": LW, "TH": 1, "TT": 1, "NT1": 1, "O32": 128, "JC": 132, "P3": 3 * Q, "P4": 3 * Q,
-        "RS3": 3 * Q, "ALT": 16, "R": 512, "KR": 32, "DD": 32, "VC": 32, "W1": 16, "DEO": 128, "LXM": 128, "PJ": 128, "JB": 256,
-        "JL": 8, "IXF": Q, "SGA": 1, "YF": Q, "RL": RO * JW, "SIL": 16},
-    U: {"OA": LA, "OF": LF, "PL": Q, "IX": Q, "L2": 8, "LT": 24, "GL": 16, "SL": 32, "JLU": 8},
-    I: {"CI": K, "FR": Q, "TI": 1, "AI": 2, "LQI": 8},
+    B: {"W": WW, "S": 16 * LA, "M": 16 * LA, "S2": 16 * LF, "M2": 512, "YW": LW, "ONE": 512, "BO": 128, "NBO": 128, "TS": 128,
+        "NTS": 128, "ID": 128, "NI": 128, "I4": 128, "NI4": 128, "N2K": 128, "P1K": 128, "HI": 128, "NHI": 128, "I5": 128, "I75": 128,
+        "B75": 128, "BT": 128, "MA": 128, "MB": 128, "DM": 256, "SEGA": 1024, "RST": 2048,
+        "I2K": 16, "NIN": 8, "CN": 128, "RX": 128, "RY": 128, "MH": 512, "SE": 512, "MX": 512, "FL": 3 * Q, "PRE": 2 * Q, "X4": Q,
+        "DR": Q, "DRN": Q, "NT": Q, "LH": 384, "FW": K, "SG": LA, "BTM": 128, "CUM": 144, "GT": 128, "EE": 256 * J,
+        "BJ": 128 * J, "TJ": 128 * J, "B64": 128, "TRI": 128, "XN": 256, "XV": 512, "EP": 144, "NV": 16, "LL": Q, "BI": 4, "NB": 48},
+    H: {"CZ": LA, "Z": 16 * LA, "VM": 512},
+    F: {"C0": CW, "C1": CW, "C2": CW, "C3": K, "LN": LW, "TH": 2, "TT": 2, "O32": 128, "JC": 148, "P3": 3 * Q, "P4": 3 * Q,
+        "RS3": 3 * Q, "R": 512, "VF": 16, "SF": 32, "CJ": J, "TE": Q, "DEO": 128, "PJ": 128, "JB": 128,
+        "JL": 16, "NN": 16 * RO, "RN": 16 * RO, "AR": RO * JW, "IXF": Q, "SGA": 1, "YF": Q, "RL": RO * JW, "NS": 16},
+    U: {"OA": LA, "OF": LF, "PL": Q, "IX": Q, "L2": 16, "LT": 24, "GL": 16, "SL": 32, "JLU": 8},
+    I: {"CI": K, "FR": Q, "TI": 1, "AI": 2, "LQI": 16, "RI": 32, "RA": 32},
 }
 SCRATCH = {n: ("sbuf", [128, w], d) for d, tab in SHAPES.items() for n, w in tab.items()}
-SCRATCH.update({"PM": ("sbuf", [16, 128], B), "PN": ("sbuf", [16, 64 + XB * (J + 1)], B), "CT": ("sbuf", [16, XB * J], B),
-                "PMF": ("sbuf", [16, 128], F), "TB": ("sbuf", [16, 132], F), "CU": ("sbuf", [16, 108], F), "CV": ("sbuf", [16, 8], F),
-                "KC": ("sbuf", [1, 256], H), "SN": ("sbuf", [128, LA], F), "ROW": ("sbuf", [1, 544], H)})
+SCRATCH.update({"PM": ("sbuf", [16, 128], B), "PMF": ("sbuf", [16, 128], F), "TB": ("sbuf", [16, 148], F), "CU": ("sbuf", [16, 108], F),
+                "CV": ("sbuf", [16, 8], F), "KC": ("sbuf", [1, 512], B), "KR": ("sbuf", [1, 512], F), "SN": ("sbuf", [128, LA], F),
+                "ROW": ("sbuf", [1, 384], H)})
 for _i in range(8):
     SCRATCH["B%d" % _i] = ("psum", [128, 512], F)
-SEMAPHORES = ["sV", "sS", "sP", "sG"] + ["ld%d" % i for i in range(5)] + ["st%d" % i for i in range(3)] + ["sn%d" % i for i in range(4)] \
+SEMAPHORES = ["sV", "sS", "sP", "sG"] + ["ld%d" % i for i in range(6)] + ["st%d" % i for i in range(4)] + ["sn%d" % i for i in range(4)] \
+    + ["cp%d" % i for i in range(1, 10)] \
     + [s + str(i) for s in ("arr", "ls", "ra", "na", "nl", "rn") for i in range(RO)]
 
 
 CYC, PEC = np.array([0.00083, 0.0012, 0.00083]), np.array([0.00045, 0.0006, 0.0008])
 GAT, SCA, WAKES, WEIGHT = np.array([1.5, 1.9, 1.5]), np.array([3.5, 5.0, 3.5]), [0.22, 0.22, 0.18], [1.0, 0.35, 0.3]
-PASSES, SEED, JITTER, HOPN, HOPJ = 800, 1, 0.8, 2.0, 2.6
-PLAN, RLEN, STRETCH, SHIFT = {}, 18.0, 2.0, 2.0
-PULL = {("send", 2): 2.0}
+HOPN, HOPJ, ONCE = np.array([1.5, 2.4, 1.5]), np.array([1.9, 3.0, 1.9]), np.array([0.6, 1.2, 0.6])
+LOAD = np.array([0.85, 1.1, 0.65])
+PASSES, SEED, JITTER, SWAPS, HEAT, DRIFT, MARK = 300, 3, 0.8, 40000, 0.05, 0.4, 0.3
+PLAN, RLEN, STRETCH, SHIFT = {}, 15.0, 2.0, 2.0
+PULL = {("send", 2): 2.0, ("come", 2): 2.0, ("joint", 2): 2.0}
 INORDER = "P"
 WAR = "P"
-XH = 1024
-FB = (64, 64, 64)
-D0 = {"A0": 0.0, "A1": 0.0, "A2": 1.6, "A3": 3.2, "F0": 3.1, "F1": 4.8, "F2": 6.7, "lit": 1.7, "viol": 6.3, "send": 9.0, "keys": 9.5,
-      "wake": 9.5, "lanes": 13.0, "moves": 14.0, "out": 15.0}
+XH = 1536
+OAS = ((192, 64), (128, 64), (0, 128))
+YCS = ((0, Q // 2), (Q // 2, Q // 2))
+XS = [(0, 1), (1, 1), (2, 1)]
+FB = [(80, 80), (80, 80), (64, 64, 64)]
+D0 = {"A3": 0.0, "A2": 0.0, "A1": 1.6, "A0": 3.2, "F0": 3.1, "F1": 4.8, "F2": 6.7, "lit": 1.7, "viol": 6.3, "send": 6.5, "joint": 5.0,
+      "keys": 7.5, "wake": 8.5, "lanes": 12.0, "moves": 12.0}
 DUE = [dict(D0), dict(D0), dict(D0)]
-GA = [(("S", 64), ("V", 64), ("S", 64), ("V", 32), ("S", 32))] * RO
-GF = [(("S", 64), ("S", 64), ("S", 64))] * RO
-NEGV = [V, 1408, 1408]
-KB = ((0, 0, 128), (1, 0, 128))
+GA = [(("S", 64), ("V", 64), ("S", 64), ("V", 48), ("S", 16))] * RO
+GF = [(("S", 80), ("S", 80), ("S", 32))] * 2 + [(("S", 64), ("S", 64), ("S", 64))]
 
 
-def plan(ops, dues, parts):
+def plan(ops, dues, parts, marks, loads):
     n = len(ops)
     times = [[(np.zeros(len(WAKES)) + x).tolist() for x in o[4:6]] for o in ops]
     ops = [o[:4] + (times[i][0][0], times[i][1][0], o[6]) for i, o in enumerate(ops)]
@@ -99,19 +106,19 @@ def plan(ops, dues, parts):
     for i in range(n):
         for j, lat in preds[i]:
             succ[j].append((i, lat))
-    pr = [0.0] * n
-    for i in range(n - 1, -1, -1):
-        pr[i] = ops[i][5] + max([lat + pr[k] for k, lat in succ[i]] + [0.0])
 
     def place(key, back):
         before, after = (succ, preds) if back else (preds, succ)
         left, est, start, busy = [len(p) for p in before], [0.0] * n, [0.0] * n, {}
         ready = [i for i in range(n) if not left[i]]
         while ready:
-            k = min(ready, key=lambda i: (key[i], i))
+            k = min(ready, key=lambda i: key[i])
             ready.remove(k)
             occ, dur = ops[k][4], ops[k][5]
-            s, lst, at = est[k] + (dur - occ if back else 0.0), busy.setdefault(ops[k][0], []), 0
+            s, lst = est[k] + (dur - occ if back else 0.0), busy.setdefault(ops[k][0], [])
+            at = len(lst)
+            while at and lst[at - 1][1] > s:
+                at -= 1
             while at < len(lst) and lst[at][0] < s + occ - 1e-9:
                 s = max(s, lst[at][1])
                 at += 1
@@ -161,9 +168,80 @@ def plan(ops, dues, parts):
         else:
             lo, jitter = rng.random() * best[3][0], rng.normal(0.0, JITTER, n)
             key = [kept[i] + (float(jitter[i]) if lo < best[1][i] < lo + STRETCH else 0.0) for i in range(n)]
-    PLAN["end"] = best[3]
-    PLAN["dbg"] = (ops, pr, succ, best[1])
-    return best[2]
+
+    def timed(order, lo, old):
+        last = {}
+        for i in order[:lo]:
+            last[queue[i]] = i
+        res = []
+        for m in range(len(WAKES)):
+            left, done, by = [list(x) for x in old[m][1:]]
+            prev, w, occ, dur = dict(last), WAKES[m], occs[m], durs[m]
+            for i in order[lo:]:
+                b = prev.get(queue[i], -1)
+                s = left[b] if b >= 0 else 0.0
+                for j, lat in preds[i]:
+                    x = done[j] + w if lat else done[j]
+                    if x > s:
+                        s, b = x, j
+                by[i], prev[queue[i]], left[i], done[i] = b, i, s + occ[i], s + dur[i]
+            res.append((max(done), left, done, by))
+        return sum(w * (r[0] + MARK * sum(max(r[2][i] for i in m) for m in marks)) for r, w in zip(res, WEIGHT)), res
+
+    queue = [o[0] for o in ops]
+    occs, durs = [[[times[i][x][m] for i in range(n)] for m in range(len(WAKES))] for x in range(2)]
+    order = best[2]
+    score, res = timed(order, 0, [(0.0, [0.0] * n, [0.0] * n, [-1] * n)] * len(WAKES))
+    top = (score, order, res)
+    for it in range(SWAPS):
+        if rng.random() < DRIFT:
+            a = b = int(rng.integers(n - 1))
+            while b < n - 1 and (b == a or queue[order[b]] != queue[order[a]]):
+                b += 1
+            u, v = order[a], order[b]
+            if queue[u] != queue[v] or above[v] >> u & 1:
+                continue
+        else:
+            end, _, done, by = res[int(rng.integers(len(WAKES)))]
+            m = int(rng.integers(len(marks) + 1))
+            i, held = max(marks[m], key=lambda x: done[x]) if m < len(marks) else done.index(end), []
+            while by[i] >= 0:
+                if queue[by[i]] == queue[i] and not above[i] >> by[i] & 1:
+                    held.append((by[i], i))
+                i = by[i]
+            if not held:
+                continue
+            u, v = held[int(rng.integers(len(held)))]
+            a, b = order.index(u), order.index(v)
+        far = int(rng.geometric(0.5))
+        if rng.random() < 0.5:
+            while far > 1 and a > 0:
+                a -= 1
+                if queue[order[a]] == queue[v]:
+                    if above[v] >> order[a] & 1:
+                        a += 1
+                        break
+                    far -= 1
+            mid = order[a:b]
+            new = order[:a] + [x for x in mid if above[v] >> x & 1] + [v] + [x for x in mid if not above[v] >> x & 1] + order[b + 1:]
+        else:
+            while far > 1 and b < n - 1:
+                b += 1
+                if queue[order[b]] == queue[u]:
+                    if above[order[b]] >> u & 1:
+                        b -= 1
+                        break
+                    far -= 1
+            mid = order[a + 1:b + 1]
+            new = order[:a] + [x for x in mid if not above[x] >> u & 1] + [u] + [x for x in mid if above[x] >> u & 1] + order[b + 1:]
+        s2, r2 = timed(new, a, res)
+        if s2 < score + HEAT * (1 - it / SWAPS) * rng.exponential():
+            order, score, res = new, s2, r2
+            if score < top[0]:
+                top = (score, order, res)
+    PLAN["end"] = [r[0] for r in top[2]]
+    PLAN["dbg"] = (ops, None, succ, [top[2][0][2][i] - durs[0][i] for i in range(n)])
+    return list(range(loads)) + [i for i in top[1] if i >= loads]
 
 
 def route(topo, src, dst):
@@ -173,30 +251,27 @@ def route(topo, src, dst):
     return sorted(c, key=lambda r: (topo.die(r) != topo.die(src), r))[0]
 
 
-def emask(topo, src, dst):
-    m = 0
-    for e in topo.engines(src, dst)[:8]:
-        m |= 1 << e
-    return m
+def writer(topo, src, t, cores):
+    dst = cores[(cores.index(src) + 1 + t % 3) % N]
+    return route(topo, src, dst) or src
 
 
 def relay_program(g, core, T, topo):
-    for r in range(N):
-        src = T.cores[r]
-        for t in range(RO):
-            dst = T.cores[(r + 1 + t % 3) % N]
-            if route(topo, src, dst) == core:
-                rid, pid = topo.addr(dst, core)
-                m = emask(topo, core, dst)
-                g.wait_ge(T.sem["rn%d" % t], 8)
-                g.remote_dma(T.NN[:, 8 * t:8 * t + 2], T.RN[:, 8 * t:8 * t + 2], T.sem["na%d" % t], T.sem["nl%d" % t], pid, rid, m)
-                g.wait_ge(T.sem["ra%d" % t], 8)
-                g.remote_dma(T["C%d" % t][:, 0:JW], T.RL[:, t * JW:(t + 1) * JW], T.sem["arr%d" % t], T.sem["ls%d" % t], pid, rid, m)
-    for r in range(N):
-        for t in range(RO):
-            if route(topo, T.cores[r], T.cores[(r + 1 + t % 3) % N]) == core:
-                g.wait_ge(T.sem["nl%d" % t], 8)
-                g.wait_ge(T.sem["ls%d" % t], 8)
+    mine = [(T.cores[r], T.cores[(r + 1 + t % 3) % N], t) for r in range(N) for t in range(RO)]
+    mine = [x for x in mine if route(topo, x[0], x[1]) == core]
+    for src, dst, t in mine:
+        rid, pid = topo.addr(dst, core)
+        m, e = topo.mask(core, dst), len(topo.engines(src, core))
+        for big in sorted((True, False), key=lambda x: PLAN.get(("arr" if x else "na", t), 0)):
+            if big:
+                g.wait_ge(T.sem["ra%d" % t], e)
+                g.remote_dma(T.AR[:, t * JW:(t + 1) * JW], T.RL[:, t * JW:(t + 1) * JW], T.sem["arr%d" % t], T.sem["ls%d" % t], pid, rid, m)
+            else:
+                g.wait_ge(T.sem["rn%d" % t], e)
+                g.remote_dma(T.NN[:, 16 * t:16 * t + NW], T.RN[:, 16 * t:16 * t + NW], T.sem["na%d" % t], T.sem["nl%d" % t], pid, rid, m)
+    for src, dst, t in mine:
+        g.wait_ge(T.sem["nl%d" % t], len(topo.engines(core, dst)))
+        g.wait_ge(T.sem["ls%d" % t], len(topo.engines(core, dst)))
 
 
 def rank_program(g, core, T, topo):
@@ -210,6 +285,7 @@ def rank_program(g, core, T, topo):
     hist = {}
     bits = {}
     serial = [0]
+    final = {}
 
     def cols(lo, n, step):
         k = (lo, n, step)
@@ -276,7 +352,7 @@ def rank_program(g, core, T, topo):
 
     ops = []
 
-    dues, parts, now = {}, [], [-1]
+    dues, parts, now, marks = {}, [], [-1], [[] for _ in range(RO)]
 
     def step(name):
         parts.extend([(name, now[0], len(parts))] * (len(ops) - len(parts)))
@@ -303,6 +379,7 @@ def rank_program(g, core, T, topo):
     def dma(q, out, in_, sem, reads, writes, dur=2.5):
         serial[0] += 1
         tag = "d%d" % serial[0]
+        final[sem] = 16
 
         def issue():
             need(q, None, reads, writes)
@@ -324,7 +401,7 @@ def rank_program(g, core, T, topo):
                 return 0.05 + GAT * CYC * 16 * width(x[2])
         if isinstance(out[1], tuple):
             return 0.05 + SCA * CYC * 16 * width(out[2])
-        two = all(SCRATCH[x[1]][2] in (B, U, "float16") for x in [out] + ins)
+        two = all(SCRATCH[x[1]][2] in (B, U, H) for x in [out] + ins)
         return CYC * max(64, width(out) * (per if per == 2 or not two else 0.5))
 
     def ap(x):
@@ -350,27 +427,28 @@ def rank_program(g, core, T, topo):
     def fill(out, c):
         run("V", lambda: g.vector.memset(ap(out), c), out, [], cost(out, [], 1))
 
-    def act(out, x, func, bias=0.0, scale=1.0, accum=None):
+    def act(out, x, func, bias=0.0, scale=1.0):
         ins = [x] + ([bias] if isinstance(bias, tuple) else [])
         if isinstance(out[1], tuple):
             run("S", lambda: g.scalar.activation(ap(out), ap(x), func), out, ins, cost(out, [x], 1))
-        elif accum is None:
+        else:
             c = cost(out, [x], 2) if isinstance(x[1], tuple) else CYC * max(64, width(out)) + (1.3 if func == F_.Silu else 0.0)
             run("S", lambda: g.scalar.activation(ap(out), ap(x), func, bias=ap(bias), scale=scale), out, ins, c)
-        else:
-            run("S", lambda: g.scalar.activation(ap(out), ap(x), func, bias=ap(bias), scale=scale, accum_out=ap(accum)), [out, accum], ins,
-                CYC * width(out))
 
-    def mm(out, l, r, start, stop):
-        c = PEC * max(min(64, width(l)), width(r)) * (4 if SCRATCH[l[1]][2] == F else 1)
-        run("P", lambda: g.tensor.matmul(ap(out), ap(l), ap(r), start, stop), out, [l, r], c)
+    def times(out, x, c):
+        ins = [x] + ([c] if isinstance(c, tuple) else [])
+        run("S", lambda: g.scalar.activation(ap(out), ap(x), F_.Identity, scale=ap(c)), out, ins, CYC * max(64, width(out)))
 
     def mms(calls):
         def fn():
             for out, l, r, start, stop in calls:
                 last = g.tensor.matmul(ap(out), ap(l), ap(r), start, stop)
             return last
-        run("P", fn, [c[0] for c in calls], [x for c in calls for x in c[1:3]], sum(PEC * max(min(64, width(c[1])), width(c[2])) for c in calls))
+        run("P", fn, [c[0] for c in calls], [x for c in calls for x in c[1:3]],
+            sum(PEC * max(min(64, width(c[1])), width(c[2])) * (4 if SCRATCH[c[1][1]][2] == F else 1) for c in calls))
+
+    def mm(out, l, r, start, stop):
+        mms([(out, l, r, start, stop)])
 
     def iota(out, pat, base, cm):
         run("G", lambda: g.iota(ap(out), pat, base, cm, allow_small_or_imprecise_dtypes=True), out, [], 0.13 + 2 * CYC * width(out))
@@ -382,35 +460,40 @@ def rank_program(g, core, T, topo):
         dst = T.cores[(rank + 1 + t % 3) % N]
         first = route(topo, core, dst)
         to = dst if first is None else first
-        net = ("", "net" + arr, 1)
+        net, once = ("", "net" + arr, 1), ONCE if (t, arr) == (0, "arr") else 0.0
+        final[ls + str(t)] = len(topo.engines(core, to))
+        final[arr + str(t)] = len(topo.engines(writer(topo, T.cores[(rank - 1 - t % 3) % N], t, T.cores), core))
 
         def issue():
             need("G", None, [src], [])
+            PLAN.setdefault((arr, t), len(PLAN))
             rid, pid = topo.addr(to, core)
             g.remote_dma(land[0] if first is None else relay, src[0], T.sem[(arr if first is None else ra) + str(t)], T.sem[ls + str(t)],
-                         pid, rid, emask(topo, core, to))
-            note("r%s%d" % (ls, t), [src], [], ls + str(t), 8, dict(known["G"]))
-        ops.append(("G", "r%s%d" % (ls, t), [src], [net], 1.3 if (t, arr) == (0, "na") else 0.3, lat + (0.0 if t else 1.0), issue))
-        ops.append(("N", "q%s%d" % (arr, t), [net], [land], 0.0, 0.0 if first is None else lat + (0.0 if t else 1.0),
-                    lambda: note("q%s%d" % (arr, t), [], [land], arr + str(t), 8, {})))
+                         pid, rid, topo.mask(core, to))
+            note("r%s%d" % (ls, t), [src], [], ls + str(t), final[ls + str(t)], dict(known["G"]))
+        ops.append(("G", "r%s%d" % (ls, t), [src], [net], 0.3 + once, lat + once, issue))
+        ops.append(("N", "q%s%d" % (arr, t), [net], [land], 0.0, 0.0 if first is None else lat + once,
+                    lambda: note("q%s%d" % (arr, t), [], [land], arr + str(t), final[arr + str(t)], {})))
 
-    dma("Y", T.FR[:], T.fr[:], "ld0", [], [a("FR")], 2.2)
-    dma("Y", T.CI[:], T.cl[:], "ld2", [], [a("CI")], 4.5)
-    dma("Y", T.W[:, XB:XB + XH], T.xv[:, 0:XH], "ld3", [], [a("W", XB, XH)], 6.0)
-    dma("Y", T.W[:, XB + XH:XB + V], T.xv[:, XH:V], "ld4", [], [a("W", XB + XH, V - XH)], 7.5)
-    dma("Y", T.TI[:], T.th[:], "ld1", [], [a("TI")], 7.5)
-    fill(a("SIL"), 100.0)
-    act(a("W", SB, 16), a("SIL"), F_.Silu)
+    dma("Y", T.FR[:], T.fr[:], "ld0", [], [a("FR")], 2.2 * LOAD)
+    dma("Y", T.TI[:], T.th[:], "ld1", [], [a("TI")], 2.4 * LOAD)
+    dma("Y", T.CI[:, 0:K // 2], T.cl[:, 0:K // 2], "ld5", [], [a("CI", 0, K // 2)], 3.4 * LOAD)
+    dma("Y", T.CI[:, K // 2:K], T.cl[:, K // 2:K], "ld2", [], [a("CI", K // 2)], 4.5 * LOAD)
+    dma("Y", T.W[:, 0:XH], T.xv[:, 0:XH], "ld3", [], [a("W", 0, XH)], 6.8 * LOAD)
+    dma("Y", T.W[:, XH:V], T.xv[:, XH:V], "ld4", [], [a("W", XH, V - XH)], 7.5 * LOAD)
+    loads, loaded = len(ops), a("W", XH, V - XH)
+    fill(a("NS"), 63.0)
+    act(a("W", SB, 16), a("NS"), F_.Silu)
 
     GP, KP = [[-16, 8], [0, 16]], [[0, 8], [1, 16]]
-    DM, CWM = a("DC", 0, 256), a("DC", 256, 256)
+    BO8, ONE1 = a("BO", 0, 8, 16), a("ONE", 0, 128, p=1)
     fill(a("ONE"), 1.0)
     sel(a("RX"), a("ONE", 0, 128), GP, A_.is_ge, 0.0, 0, 1)
     sel(a("BO"), a("RX"), [[16, 8], [0, 16]], A_.is_ge, 0.0, 15, -1)
-    sel(a("TS"), a("BO"), [[1, 128]], A_.is_ge, 0.0, -1, -1)
+    sel(a("TS"), a("RX"), [[1, 128]], A_.is_ge, 0.0, -1, -1)
     sel(a("ID"), a("ONE", 0, 128), [[-1, 128]], A_.is_equal, 0.0, 0, 1)
     sel(a("PM"), a("ONE", 0, 128, p=16), KP, A_.is_equal, 0.0, 0, -1)
-    copy(a("PMF"), a("PM"))
+    times(a("PMF"), a("PM"), 1.0)
     for name, c in (("NI", -1.0), ("I4", 4096.0), ("NI4", -4096.0)):
         ts(a(name), a("ID"), c, A_.mult)
     ts(a("NTS"), a("TS"), -1.0, A_.mult)
@@ -428,14 +511,12 @@ def rank_program(g, core, T, topo):
     iota(a("P3", 0, Q, 3), [[16, Q]], 2 * K, 1)
     fill(a("RS3"), 0.0)
     fill(a("RS3", 0, Q, 3), 1e6)
-    fill(a("ROW", 0, 256), 8.0 + 87 * 32)
-    fill(a("ROW", 256, Q), 4096.0)
-    fill(a("ROW", 256 + Q, 16), 0.0)
-    fill(a("ROW", 416, 128), -4164.0)
-    fill(a("ROW", 320, Q), -6.5 / 8)
-    fill(a("ROW", 320 + Q, Q), -9.5 / 8)
-
-    fill(a("SN"), 2 * V + OFF)
+    fill(a("ROW", 0, Q), 4096.0)
+    fill(a("ROW", Q, 16), 0.0)
+    fill(a("ROW", 64, 128), -4640.0)
+    fill(a("ROW", 192, Q), 4608.0)
+    fill(a("ROW", 256, 128), V + OFF)
+    times(a("SN"), a("ONE", 0, LA), 2 * V + OFF)
 
     def sentinels(t):
         dma("Y", T.LN[:, 0:LA], T.SN[:], "sn%d" % (2 * t), [a("SN")], [a("LN", 0, LA)])
@@ -449,20 +530,20 @@ def rank_program(g, core, T, topo):
     def cyclic(t):
         for c in range(2):
             p0, i = starts[t][c][0], 128 * (2 * (t - 1) + c)
-            sel(a("RX"), a("BO"), [[16, 8], [0, 16]], A_.is_ge, 0.0, p0 - 1, -1)
-            sel(a("RY"), a("NBO"), [[0, 8], [-1, 16]], A_.is_ge, 0.0, p0 - 1, 0)
+            rx, ry = (a("FW", 2 * i, 128), a("FW", 2 * i + 128, 128)) if 2 * i < K else (a("RX"), a("RY"))
+            sel(rx, a("BO"), [[16, 8], [0, 16]], A_.is_ge, 0.0, p0 - 1, -1)
+            sel(ry, a("NBO"), [[0, 8], [-1, 16]], A_.is_ge, 0.0, p0 - 1, 0)
             sel(a("SE", i, 128), a("BO"), GP, A_.is_equal, 0.0, -p0, 1)
             sel(a("MX", i, 128), a("NBO"), KP, A_.is_equal, 0.0, -p0, 0)
-            for j, m in enumerate(("NTS", "RX", "RY")):
-                mm(a("B6", 256 + 128 * c, 128), a("ID"), a(m), j == 0, j == 2)
+            mms([(a("B6", 256 + 128 * c, 128), a("ID"), m, j == 0, j == 2) for j, m in enumerate((a("NTS"), rx, ry))])
         act(a("MH", 256 * (t - 1), 256), a("B6", 256, 256), F_.Identity)
 
     def lists(t):
-        fa, fd = a("FL", 0, Q), a("FL", Q, Q)
+        fa, fb, fd = a("FL", 0, Q), a("FL", 2 * Q if t else 0, Q), a("FL", Q, Q)
+        scan(a("PRE", Q, Q), fb, fd, 0.0, A_.add, A_.add)
         scan(a("PRE", 0, Q), a("ONE", 0, Q), fa, 0.0, A_.mult, A_.subtract)
-        scan(a("PRE", Q, Q), fa, fd, 0.0, A_.add, A_.add)
         mm(a("B6", 0, Q), a("NI4"), fa, False, False)
-        mm(a("B6", Q, Q), a("I4"), fa, False, False)
+        mm(a("B6", Q, Q), a("I4"), fb, False, False)
         mm(a("B6", Q, Q), a("I4"), fd, False, False)
         for c in range(2):
             q0, i, b = starts[t][c][1], 128 * (2 * (t - 1) + c), 2 * Q + 4 * t + 2 * c
@@ -478,284 +559,296 @@ def rank_program(g, core, T, topo):
                 ts(a("P3", 1 + c, q0, 3), a("B6", Q * c, q0), a("B6", b, 1), A_.add, a("B6", b + 1, 1), A_.add)
         scan(a("P4"), a("RS3"), a("P3"), 0.0, A_.add, A_.min)
         copy(a("PL"), a("P4", 2, Q, 3))
-        act(ind(a("LN"), a("PL")), a("C%d" % t, JW, K), F_.Silu)
+        act(ind(a("LN"), a("PL")), a("C%d" % t, 2 * JW, K), F_.Silu)
         if t:
+            marks[t - 1].append(len(ops) - 1)
             due(t - 1, "lanes")
         else:
             dues[len(ops) - 1] = -4.0
-        ts(a("OA"), a("LN", 0, LA), 0.25 - OFF, A_.add)
+        for lo, n in OAS:
+            ts(a("OA", lo, n), a("LN", lo, n), 0.25 - OFF, A_.add)
         ts(a("OF"), a("LN", K, LF), 0.25 - OFF, A_.add)
         if t < RO - 1:
             sentinels(t)
         step("offsets")
-        scan(a("PRE", 2 * Q, Q), a("ONE", 0, Q), fd, 0.0, A_.mult, A_.add)
-        mm(a("B7", 0, Q + 1), a("ONE", 0, 128, p=1), a("ROW", 256, Q + 1), True, False)
-        mm(a("B7", 0, Q), a("NI4"), fd, False, False)
-        mm(a("B7", 0, Q), a("ID"), a("PRE", 2 * Q, Q), False, False)
-        mm(a("B7", Q, 1), a("TS"), a("PRE", 3 * Q - 1, 1), False, True)
-        ts(a("DR"), a("B7", 0, Q), a("B7", Q, 1), A_.add, 256.0, A_.min)
+        dr = a("B6", 128, Q)
+        mms([(a("B6", 128, Q + 1), ONE1, a("ROW", 0, Q + 1), True, False), (dr, a("NI4"), fd, False, False)]
+            + ([(dr, a("NI4"), fb, False, False), (dr, a("I4"), fa, False, False)] if t else []))
+        mms([(dr, a("ID"), a("PRE", Q * c, Q), False, False) for c in range(2)]
+            + [(a("B6", 128 + Q, 1), a("TS"), a("PRE", Q * c + Q - 1, 1), False, c == 1) for c in range(2)])
+        ts(a("DR"), dr, a("B6", 128 + Q, 1), A_.add, 1024.0, A_.min)
         if t == RO - 1:
             for j in range(3):
                 tt(a("LH", 128 * j, 128), ind(a("DR"), a("LT", 8 * j, 8)), a("BO"), A_.mult)
-                mm(a("B7", 64 + j, 16, 3), a("LH", 128 * j, 128), a("DC", 0, 16), True, True)
-            copy(a("DRN"), a("B7", 64, Q))
+                mm(a("B6", 192 + j, 16, 3), a("LH", 128 * j, 128), a("DM", 0, 16), True, True)
+            copy(a("DRN"), a("B6", 192, Q))
 
-    def gather(q, lo, n, frozen):
-        w = ind(a("W", XB, WW - XB), a("OF" if frozen else "OA", lo, n))
+    def gather(q, lo, n, frozen, th):
+        w = ind(a("W", 0, DU), a("OF" if frozen else "OA", lo, n))
         out = a("S2" if frozen else "S", 16 * lo, 16 * n)
         if frozen:
             if q == "V":
-                ts(out, w, 64.0, A_.add, a("TT"), A_.is_ge)
+                ts(out, w, a(th, 1, 1), A_.add, 0.0, A_.max)
             else:
-                act(out, w, F_.Relu, a("NT1"))
+                act(out, w, F_.Relu, a(th, 1, 1))
         elif q == "V":
-            ts(out, w, 64.0, A_.add)
+            ts(out, w, UN, A_.mult)
         else:
-            act(out, w, F_.Identity, 64.0)
+            act(out, w, F_.Identity, 0.0, UN)
 
-    def negate(t):
-        n = NEGV[t]
-        if n:
-            ts(a("W", XB + V, n), a("W", XB, n), -1.0, A_.mult, 63.0, A_.add)
-        if n < V:
-            act(a("W", XB + V + n, V - n), a("W", XB + n, V - n), F_.Identity, 63.0, -1.0)
-
-    fill(a("LN", 0, LA), 2 * V + OFF)
-    fill(a("LN", K, LF), 2 * V + OFF)
+    times(a("LN", 0, LA), a("ONE", 0, LA), 2 * V + OFF)
+    times(a("LN", K, LF), a("ONE", 0, LF), 2 * V + OFF)
     consts_of_lists(0)
     for p in range(16):
-        ts(a("C0", JW + p, Q, 16), a("CI", Q * p, Q), OFF, A_.add)
+        ts(a("C0", 2 * JW + p, Q, 16), a("CI", Q * p, Q), OFF, A_.add)
     ts(a("FL", 0, Q), a("FR"), 0.5, A_.is_lt)
     ts(a("FL", Q, Q), a("FR"), 3.5, A_.is_gt)
-    ts(a("XS"), a("FR"), 0.125, A_.mult)
+    ts(a("X4"), a("FR"), 512.0, A_.mult)
     lists(0)
     for lo, n in ((0, XH), (XH, V - XH)):
-        ts(a("W", XB + V + lo, n), a("W", XB + lo, n), -1.0, A_.mult, 63.0, A_.add)
-    ts(a("TH"), a("TI"), 64.0, A_.add)
-    ts(a("TT"), a("TI"), 64.0, A_.add)
-    ts(a("NT1"), a("TT"), -1.0, A_.mult, 65.0, A_.add)
+        ts(a("W", V + lo, n), a("W", lo, n), -1.0, A_.mult, 63.0, A_.add)
+    ts(a("TH", 0, 1), a("TI"), UN, A_.mult)
+    ts(a("TH", 1, 1), a("TI"), -1.0, A_.mult, 1.0, A_.add)
     step("first")
-    fill(a("W", 0, XB), 0.0)
-    fill(a("SEGM"), 1.0)
-    fill(a("SEGM", 0, 64, 16), 0.0)
-    fill(a("RST"), 2.0)
-    fill(a("RST", 0, 64, 16), BIGM)
-    for lo in range(0, LW, 1024):
-        act(a("YW", lo, min(1024, LW - lo)), a("RST", 0, min(1024, LW - lo)), F_.Identity, -0.5, 0.0)
-    fill(a("JB"), 0.0)
-    fill(a("HD"), 0.0)
+    fill(a("SEGA"), 0.0)
+    fill(a("SEGA", 0, 64, 16), -2.0 ** 30)
+    fill(a("RST", 0, 512), 64 * UN)
+    fill(a("RST", 15, 32, 16), 1152 * UN)
+    times(a("YW", LA, 512), a("ONE"), 1.625)
+    for i in range(1, 4):
+        dma("Y", T.RST[:, 512 * i:512 * (i + 1)], T.RST[:, 0:512], "cp%d" % i, [a("RST", 0, 512), loaded], [a("RST", 512 * i, 512)], 2.0)
+    for i, lo in enumerate(range(K + LF, LW, 512)):
+        n = min(512, LW - lo)
+        dma("Y", T.YW[:, lo:lo + n], T.YW[:, LA:LA + n], "cp%d" % (4 + i), [a("YW", LA, n), loaded], [a("YW", lo, n)], 2.0)
+    for t in range(RO):
+        dma("Y", T["C%d" % t][:, 0:2 * JW], T.SN[:], "cp%d" % (7 + t), [a("SN"), loaded], [a("C%d" % t, 0, 2 * JW)], 2.0)
     fill(a("CUM", 0, 16), 0.0)
-    fill(a("O32"), 1.0 / 32)
-    fill(a("ALT"), 32.0)
-    fill(a("ALT", 0, 8, 2), 0.0)
-    for name, c in (("PK", 1.0 / 1024), ("NQ", -0.25), ("N2K", -2048.0), ("HI", 0.5), ("NHI", -0.5)):
-        ts(a(name), a("ID"), c, A_.mult)
-    ts(a("NBO"), a("BO"), -1.0, A_.mult)
-    ts(a("I2K"), a("BO", 0, 16, 8), 2048.0, A_.mult)
-    ts(a("NIN"), a("BO", 0, 8, 16), -1.0, A_.mult)
+    times(a("O32"), a("ONE", 0, 128), -1.0 / 4096)
+    for name, c in (("N2K", -2048.0), ("P1K", 1024.0), ("HI", 0.5), ("NHI", -0.5), ("I5", 512.0), ("I75", 1.75)):
+        times(a(name), a("ID"), c)
+    times(a("NBO"), a("BO"), -1.0)
+    times(a("B75"), a("BO"), 1.75)
+    for i in range(2):
+        ts(a("I2K", 8 * i, 8), BO8, 2.0 ** 25, A_.mult)
+    ts(a("NIN"), BO8, -1.0, A_.mult)
+    fill(a("EP"), 0.0)
+    ts(a("EP", 15, 8, 16), BO8, -256.0, A_.mult)
     step("fill")
-    P16 = [[1, 16]]
-    sel(a("PN", 0, 16), a("ONE", 0, 16, p=16), P16, A_.is_ge, 0.0, 0, -1)
-    sel(a("PN", 16, 16), a("PN", 0, 16), P16, A_.not_equal, 1024.0, 0, -1)
-    sel(a("PN", 32, 16), a("PN", 16, 16), P16, A_.not_equal, 2.0 ** -13, -15, 0)
-    sel(a("PN", 48, 16), a("PN", 32, 16), P16, A_.not_equal, 0.125, -30, 1)
-    mms([(a("B0", 128 * j, 128), a("PM"), a("PM"), True, True) for j in range(2)]
-        + [(a("B0", 256 + 16 * j, 16), a("PM"), a("PN", 48, 16), True, True) for j in range(16)])
-    act(a("DC"), a("B0"), F_.Identity)
+    mms([(a("B0", 128 * j, 128), a("PM"), a("PM"), True, True) for j in range(2)])
+    act(a("DM"), a("B0", 0, 256), F_.Identity)
     step("mask")
-    iota(a("PN", 64, XB), [[0, XB]], 2048, 0)
+    fill(a("B64"), 0.0)
+    fill(a("BI"), 0.0)
+    for i in range(2):
+        fill(a("B64", 64 * i, 64, p=64, p0=64 * i), 16384.0)
+        fill(a("BI", 2 * i, 2, p=64, p0=64 * i), 8192.0)
+    sel(a("XV", 256, 128), a("B64"), [[1, 128]], A_.is_gt, 0.0, 0, -1)
+    sel(a("TRI"), a("XV", 256, 128), [[1, 128]], A_.not_equal, 4096.0, 0, -1)
+    tt(a("CJ"), a("BO", 0, J, 16), a("BO", 64, J, 16), A_.add)
     for j in range(J):
-        sel(a("PN", 64 + XB * (j + 1), XB), a("PN", 64, XB), [[-100, J], [-1, 16]], A_.is_ge, 8192.0, 100 * j, 1)
-        sel(a("CT", XB * j, XB), a("PN", 64 + XB * (j + 1), XB), [[100, J], [1, 16]], A_.not_equal, -2048.0, -100 * j, -1)
-        sel(a("LH", 128 * j, 128), a("ONE", 0, 128), [[-XB, 8 // J], [0, XB]], A_.is_ge, 0.0, -16 * j, 1)
-        sel(a("BJ", 128 * j, 128), a("LH", 128 * j, 128), [[XB, 8 // J], [0, XB]], A_.is_ge, 0.0, 16 * j + 15, -1)
+        ts(a("BJ", 128 * j, 128), a("B64"), a("CJ", j, 1), A_.mult, 1.0 / 16384, A_.mult)
+        times(a("TJ", 128 * j, 128), a("TRI"), a("CJ", j, 1))
+    fill(a("NB", 32, 16), 0.0)
+    for lo, n, b, sign in ((0, 4, 0, -2.0), (4, 8, 0, 2.0), (12, 4, 4, -2.0)):
+        times(a("NB", lo, n), a("BO", 16 * b, n, 16), 1.0)
+        times(a("NB", 16 + lo, n), a("BO", 16 * b, n, 16), sign)
+        if sign < 0:
+            times(a("NB", 32 + lo, n), a("BO", 16 * b, n, 16), float(V))
     step("pairs")
-    fill(a("SEJ"), 1.0)
-    fill(a("SEJ", 0, 256 // XB, XB), 0.0)
-    iota(a("TB", 0, Q), [[16, Q]], JW + 1, 1)
-    iota(a("TB", Q, Q), [[1, 16], [256, 3]], JW + 1, 16)
+    iota(a("TB", 0, Q), [[16, Q]], 2 * JW - 1023, 1)
+    iota(a("TB", Q, Q), [[1, 16], [256, 3]], 2 * JW - 1023, 16)
     iota(a("TB", 2 * Q, 8), [[16, 8]], JW - 255, 1)
-    iota(a("TB", 104, 4), [[16, 4]], 0, 1)
+    iota(a("TB", 104, 4), [[0, 4]], 1000, 0)
     iota(a("TB", 108, 24), [[16, 3], [0, 8]], 0, 1)
-    mm(a("B1", 0, 132), a("PMF"), a("TB"), True, True)
-    act(a("JC"), a("B1", 0, 132), F_.Identity)
+    iota(a("TB", 132, 16), [[0, 2], [16, 8]], DU, 1)
+    mm(a("B1", 0, 148), a("PMF"), a("TB"), True, True)
+    act(a("JC"), a("B1", 0, 148), F_.Identity)
     copy(a("LT"), a("JC", 108, 24))
-    iota(a("LQI"), [[2, 8]], 1, 0)
+    iota(a("LQI"), [[1, 16]], 0, 0)
     copy(a("L2"), a("LQI"))
     sel(a("MA"), a("TS"), [[-1, 128]], A_.not_equal, -255.0, 0, 1)
     sel(a("GT"), a("BO"), [[-1, 128]], A_.is_ge, 0.0, 0, 1)
     sel(a("MB"), a("GT"), [[-1, 128]], A_.not_equal, 256.0, 0, 1)
     step("joint")
-    ts(a("EE", 0, 128), a("ID"), 2.0, A_.mult)
-    ts(a("EE", 128, 128), a("ID"), -64.0, A_.mult)
-    fill(a("EE", 256, 128), 0.0)
-    mms([(a("B2", 256 * i + 16 * j, 16), a("EE", 128 * (j % 2), 128) if i else a("ID") if j % 2 else a("EE", 256, 128),
-          a("ID", 16 * (j // 2), 16), True, True) for i in range(2) for j in range(16)])
-    act(a("RA"), a("B2"), F_.Identity)
-    iota(a("R", 0, 256, p=1), [[0, 8], [-1281, 2], [-256, 16]], 3266, 0)
-    ts(a("KC"), a("R", 0, 256, p=1), 0.5, A_.mult)
+    iota(a("XV", 0, 128), KP, -16, 0)
+    times(a("XV", 128, 128), a("BO"), 2.0 ** 18)
+    tt(a("CN"), a("XV", 0, 128), a("XV", 128, 128), A_.mult)
+    iota(a("KR", 0, 256), [[0, 16], [-2, 16]], 29, 0)
+    iota(a("KR", 15, 16, 16), [[0, 16]], -35, 0)
+    iota(a("KR", 256, 256), [[-1, 2], [0, 8], [-1, 16]], 16, 0)
+    times(a("KC", 0, 256), a("KR", 0, 256), 2.0 ** 24)
+    times(a("KC", 256, 256), a("KR", 256, 256), 2.0 ** 11)
 
     for t in range(RO):
-        C, last = "C%d" % t, t == RO - 1
-        SG = a("YW", 0, LA)
+        C, last, th = "C%d" % t, t == RO - 1, "TT" if t else "TH"
         step("dead")
         now[0] = t
         if not last:
-            cyclic(t + 1)
+            for u in range(1, RO) if t == 0 else ():
+                cyclic(u)
             consts_of_lists(t + 1)
             step("cyclic")
-        for frozen, who in ((False, GA[t]), (True, GF[t])):
-            lo = 0
-            for q, n in who:
-                gather(q, lo, n, frozen)
-                due(t, "AF"[frozen] + str(lo // CH))
-                lo += n
+        lo = LA
+        for q, n in GA[t]:
+            lo -= n
+            gather(q, lo, n, False, th)
+            due(t, "A" + str(lo // CH))
+        for q, n in GF[t]:
+            gather(q, lo, n, True, th)
+            due(t, "F" + str(lo // CH))
+            lo += n
         ts(a("CZ"), a("OA"), -float(V), A_.add)
         due(t, "lit")
-        ts(a("HB"), a("OA"), 1.0 / 64, A_.mult, 128.0 - 63.0 / 128, A_.add)
+        ts(a("SG"), a("OA"), V - 0.5, A_.is_gt)
         due(t, "lit")
-        for j, l in enumerate(("NHI", "HI")):
-            mm(a("B7", 256 + 128 * j, 128), a(l), a("CZ", 0, 128, 2), True, False)
-            mm(a("B7", 256 + 128 * j, 128), a("HI"), a("CZ", 1, 128, 2), False, True)
-        act(a("DEO"), a("B7", 256, 128), F_.Identity)
-        act(a("LXM"), a("B7", 384, 128), F_.Identity, V + OFF)
-        for h in range(2):
-            key = a("B%d" % h, 0, 256)
-            mm(key, a("ONE", 0, 128, p=1), a("KC"), True, False)
-            mm(key, a("CZ", 128 * h, 128), a("RA", 0, 256), False, False)
-            mm(key, a("HB", 128 * h, 128), a("RA", 256, 256), False, False)
-        for c in range(NA):
-            lo = 16 * CH * c
-            scan(a("M", lo, 16 * CH), a("SEGM"), a("S", lo, 16 * CH), 0.0, A_.mult, A_.max)
-            ts(a("FA", CH * c, CH), a("M", lo + 15, CH, 16), a("TT"), A_.is_lt, EPS, A_.max)
-            tt(a("S", lo, CH, 16), a("FA", CH * c, CH), a("M", lo, CH, 16), A_.mult)
+        mms([(a("B5", 192, 128), a(l), a("CZ", j, 128, 2), j == 0, j == 1) for j, l in enumerate(("NHI", "HI"))])
+        act(a("DEO"), a("B5", 192, 128), F_.Identity)
+        mms([(a("B2", 256, 128), ONE1, a("ROW", 256, 128), True, False)]
+            + [(a("B2", 256, 128), a("HI"), a("CZ", j, 128, 2), False, j == 1) for j in range(2)])
+        for h in (1, 0):
+            key = "B%d" % h
+            mms([(a(key, 0, 256), ONE1, a("KC", 256 * i, 256), i == 0, False) for i in range(2)])
+            mms([(a(key, 128 * i, 128), a("SG", 128 * h, 128), a(m), False, False) for i, m in enumerate(("N2K", "P1K"))])
+            mms([(a("B4" if h else "B7", j, 128, J), a("TJ", 128 * j, 128), a("DM", 0, 128), j == 0, False) for j in range(J)])
+        for c in range(NA - 1, -1, -1):
+            lo, rs = 16 * CH * c, 16 * CH * (c % 2)
+            scan(a("M", lo, 16 * CH), a("SEGA"), a("S", lo, 16 * CH), 0.0, A_.add, A_.max)
+            ts(a("RST", rs, CH, 16), a("M", lo + 15, CH, 16), a(th, 0, 1), A_.is_lt, 960 * UN, A_.subtract)
+            if c % 2 == 0:
+                ts(a("YW", CH * c, 128), a("M", lo + 15, 128, 16), a(th, 0, 1), A_.is_lt, 8.0, A_.mult)
+                mms([(a("B%d" % (c // 2), 128 * i, 128), a("YW", CH * c, 128), a("CN"), False, False) for i in range(2)])
             step("rows")
-            scan(a("Z", lo, 16 * CH), a("RST"), a("S", lo, 16 * CH), 1.0, A_.mult, A_.min)
+            scan(a("Z", lo, 16 * CH), a("S", lo, 16 * CH), a("RST", rs, 16 * CH), 1.0, A_.min, A_.add)
             step("mask")
-        for h, m0, n in KB:
-            mms([(a("B%d" % h, k, 16, 16, p=n, p0=m0), a("Z", 16 * (128 * h + m0) + k, n, 16), a("I2K"), False, k == 15 and m0 + n == 128)
-                 for k in range(16)])
+        for h in (1, 0):
+            mms([(a("B%d" % h, k, 16, 16), a("Z", 16 * 128 * h + k, 128, 16), a("I2K"), False, False) for k in range(16)]
+                + [(a("B%d" % h, 0, 128), a("CZ", 128 * h, 128), a("ID"), False, True)])
         step("sums")
-        mm(a("B4", 0, LA), a("BO"), a("FA"), True, True)
-        act(SG, a("B4", 0, LA), F_.Sign, -3.5, 1.0, a("SGA"))
+        mm(a("B3", 256, 128), ONE1, a("ROW", 64, 128), True, False)
+        mm(a("B3", 256, 128), a("I4"), a("DM", 0, 128), False, False)
+        mms([(a("B3", 128, 128), a("BO"), a("YW", 0, 128, 2), False, False), (a("B3", 256, 128), a("BO"), a("YW", 1, 128, 2), False, False)]
+            + [(a("B3", 8 * h, 8), a("YW", 128 * h, 128), BO8, False, h == 1) for h in range(2)])
+        ts(a("BT"), a("B3", 128, 128), 32.0, A_.min, -16.0, A_.mult)
         due(t, "viol")
-        mm(a("B3", 256, 128), a("ONE", 0, 128, p=1), a("ROW", 416, 128), True, False)
-        mm(a("B3", 256, 128), a("I4"), a("DC", 0, 128), False, False)
-        mms([(a("B3", 128, 128), a("BO"), a("FA", 0, 128, 2), False, False), (a("B3", 256, 128), a("BO"), a("FA", 1, 128, 2), False, True)])
-        ts(a("BT"), a("B3", 128, 128), 4.0, A_.min, -16.0, A_.mult)
         tt(a("BTM"), a("B3", 256, 128), a("BT"), A_.is_ge)
+        ts(a("NV"), a("B3", 0, 16), 28.0, A_.is_lt, 4096.0, A_.mult)
         scan(a("CUM", 16, 128), a("ONE", 0, 128), a("BTM"), 0.0, A_.mult, A_.add)
-        send(t, a("CUM", 142, 2), a("NN", 8 * t, 2), T.RN[:, 8 * t:8 * t + 2], "na", "rn", "nl", HOPN)
-        mm(a("B3", 384, 8), a("MA"), a("CUM", 31, 8, 16), True, False)
-        mm(a("B3", 384, 8), a("MB"), a("CUM", 15, 8, 16), False, True)
-        tt(a("JL"), a("B3", 384, 8), a("JC", 2 * Q, 8), A_.min)
-        ts(a("JLU"), a("JL"), 255.0, A_.add)
+        mms([(a("B3", 384, 8), a("MA"), a("CUM", 31, 8, 16), True, False), (a("B3", 384, 8), a("MB"), a("CUM", 15, 8, 16), False, False),
+             (a("B3", 392, 1), a("NBO"), a("CUM", 143, 1), False, False), (a("B3", 393, 1), a("B75"), a("CUM", 143, 1), False, True)])
+        tt(a("JL", 0, NW), a("B3", 384, NW), a("JC", 2 * Q, NW), A_.min)
+        due(t, "send")
         for k0 in range(0, 16, 4):
-            mms([(a("B2", k, 8, 16), a("S" if k else "M", 16 * (1 - h) + k, 128, 32), a("NIN") if h else a("BO", 0, 8, 16), h == 0, h == 1)
+            mms([(a("B2", k, 8, 16), a("S", 16 * (1 - h) + k, 128, 32), a("NIN") if h else BO8, h == 0, h == 1)
                  for k in range(15 - k0, 11 - k0, -1) for h in range(2)])
-        act(a("GT"), a("B2", 0, 128), F_.Sign, -0.5)
+        act(a("GT"), a("B2", 0, 128), F_.Sign, -0.5, 1.0 / UN)
         mm(a("B2", 128, 128), a("GT"), a("ID"), True, True)
         tt(a("PJ"), a("B2", 128, 128), a("DEO"), A_.mult)
-        tt(ind(a("JB"), a("JLU")), a("PJ"), a("LXM"), A_.add)
-        due(t, "send")
-        send(t, a("JB", 0, JW), a(C, 0, JW), T.RL[:, t * JW:(t + 1) * JW], "arr", "ra", "ls", HOPJ)
-        nb = 8 // J
+        tt(a("JB"), a("B2", 256, 128), a("PJ"), A_.add)
+        due(t, "joint")
+        send(t, a("JB"), a("AR", t * JW, JW), T.RL[:, t * JW:(t + 1) * JW], "arr", "ra", "ls", HOPJ)
+        send(t, a("JL", 0, NW), a("NN", 16 * t, NW), T.RN[:, 16 * t:16 * t + NW], "na", "rn", "nl", HOPN)
         for h in (1, 0):
-            key, same, vm = "B%d" % h, "B4" if h else "B7", a("VM", 128 * h, 128)
-            scan(a("R", 256 * h, 256), a("SEGM", 0, 256), a(key, 0, 256), 0.0, A_.mult, A_.max)
+            key, same, vm, sm = "B%d" % h, "B4" if h else "B7", a("VM", 256 * h, 128), a("VM", 256 * h + 128, 128)
+            scan(a("R", 256 * h, 256), a("SEGA", 0, 256), a(key, 0, 256), 0.0, A_.add, A_.max)
             due(t, "keys")
-            ends = a("R", 256 * h + 15, 16, 16)
-            ts(a("KR", 16 * h, 16), ends, MAGIC, A_.add, MAGIC, A_.subtract)
-            tt(a("DD", 16 * h, 16), ends, a("KR", 16 * h, 16), A_.subtract)
-            scan(a("VC", 16 * h, 16), a("ALT"), a("DD", 16 * h, 16), 0.0, A_.mult, A_.add)
-            tt(a("HD", 256 * h + 128, 8, 16), a("KR", 16 * h, 8, 2), a("KR", 16 * h + 1, 8, 2), A_.subtract)
-            copy(a("HD", 256 * h, 8, 16), a("VC", 16 * h + 1, 8, 2))
-            tt(vm, ind(a("VC", 16 * h, 16), a("L2")), a("DC", 0, 128), A_.mult)
-            scan(a("VB", 256 * h, 256), a("SEGM", 0, 256), a("HD", 256 * h, 256), 0.0, A_.mult, A_.add)
+            copy(a("RI", 16 * h, 16), a("R", 256 * h + 15, 16, 16))
+            ts(a("RA", 16 * h, 16), a("RI", 16 * h, 16), V - 1, A_.bitwise_and)
+            tt(a("VM", 256 * h, 256), ind(a("RA", 16 * h, 16), a("L2")), a("DM"), A_.mult)
+            tt(a("VF", 8 * h, 8), a("RA", 16 * h, 8), a("NV", 8 * h, 8), A_.add)
             step("chosen")
-            mms([(a(key, 256, 8), vm, a("BO", 0, 8, 16), True, True)]
-                + [(a(key, 264 + nb * j, nb), vm, a("BO", 16 * j, nb, XB), True, True) for j in range(J)])
-            mms([(a(same, 256 + XB * b, XB), a("PM"), a("CT", XB * (b // nb), XB), b == 0, False) for b in range(8)])
-            mms([(a(same, 256 + 128 * j, 128), a("N2K"), a("YW", 128 * h, 128), False, False) for j in range(J)])
-            mms([(a(same, 256 + 128 * j, 128), vm, a("BJ", 128 * j, 128), False, False) for j in range(J)])
-            mms([(a(same, 256 + 128 * j, 128), a("VB", 256 * h, 128), a("NI"), False, j == J - 1) for j in range(J)])
-            mms([(a(key, 384, 128), a("ONE", 0, 128, p=1), a("ROW", 0, 128), True, False), (a(key, 384, 128), a("VB", 256 * h + 128, 128), a("NQ"), False, True)])
-            ts(a("GL", 8 * h, 8), a(key, 256, 8), 1023.5 + XB, A_.add, V + XB - 1.0, A_.min)
-            tt(a("FSG", 128 * h, 128), a(key, 384, 128), a("FA", 128 * h, 128), A_.mult)
-            tt(a("XN", 128 * h, 128), ind(a("W", 0, XB + V), a("GL", 8 * h, 8)), a("FSG", 128 * h, 128), A_.add)
-            ts(a("XC", 128 * h, 128), a("XN", 128 * h, 128), 0.0, A_.max, 63.0, A_.min)
+            mms([(a(same, j, 128, J), a("BJ", 128 * j, 128), vm, False, j == J - 1) for j in range(J)])
+            mms([(a(key, 256, 8), vm, BO8, True, False), (a(key, 256, 8), sm, a("NB", 20, 8), False, True)])
+            copy(a("GL", 8 * h, 8), a(key, 256, 8))
+            mms([(a(key, 272, 16), a("DM", 0, 128), a("NB", 32, 16), True, False), (a(key, 272, 16), vm, a("NB", 0, 16), False, False),
+                 (a(key, 272, 16), sm, a("NB", 16, 16), False, False)])
+            new, other = [a("XV", 256 * h + XB + XB * b, XB) for b in range(2)], [a("XV", 256 * h + 3 * XB * b, XB) for b in range(2)]
+            if (t, h) in XS:
+                act(a("XN", 128 * h, 128), ind(a("W", 0, DU), a("GL", 8 * h, 8)), F_.Identity)
+                mms([(a("B3", 128 * h, 128), a("ID"), a(m, 128 * h, 128), m == "YW", m == "XN") for m in ("YW", "XN")])
+                for b in range(2):
+                    act(other[b], a("B3", 128 * h + XB * b, XB), F_.Relu, 63.0, -1.0)
+                for b in range(2):
+                    act(new[b], other[b], F_.Identity, 63.0, -1.0)
+            else:
+                tt(a("XN", 128 * h, 128), ind(a("W", 0, DU), a("GL", 8 * h, 8)), a("YW", 128 * h, 128), A_.add)
+                ts(a("XV", 256 * h + XB, 128), a("XN", 128 * h, 128), 63.0, A_.min)
+                for b in range(2):
+                    ts(other[b], new[b], -1.0, A_.mult, 63.0, A_.add)
             step("new%d" % h)
-            ts(a("EE", 256 * h, 256), a(same, 256, 256), 0.0, A_.is_equal, -4096.0, A_.mult)
-            scan(a("ES", 256 * h, 256), a("SEJ"), a("EE", 256 * h, 256), 0.0, A_.mult, A_.add)
-            tt(a("W1", 8 * h, 8), a(key, 264, 8), a("ES", 256 * h + XB - 1, 8, XB), A_.add)
-            for j in range(J):
-                ts(a("SL", 8 * h + j, nb, J), a("W1", 8 * h + nb * j, nb), 1023.5 + XB, A_.add, a("JC", 104 + j, 1), A_.max)
+            for i in range(8):
+                ts(a("EE", 512 * h + XB * i, XB), a(same, XB * i, XB), a("VF", 8 * h + i, 1), A_.is_equal)
+            mms([(a(key, 272 + j, 4, J), a("EE", 512 * h + j, 128, J), a("BI"), False, j == J - 1) for j in range(J)])
+            tt(a("SF", 16 * h, 16), a(key, 272, 16), a("JC", 132, 16), A_.min)
+            copy(a("SL", 16 * h, 16), a("SF", 16 * h, 16))
             step("lowest%d" % h)
-        for b in range(2 * nb - 1, -1, -1):
-            copy(ind(a("W", 0, XB + V), a("SL", J * b, J)), a("XC", XB * b, XB))
-            if b == 2 * nb - 1:
+        for b in range(LA // XB - 1, -1, -1):
+            copy(ind(a("W"), a("SL", 2 * J * b, 2 * J)), a("XV", 2 * XB * b, 2 * XB))
+            if b == LA // XB - 1:
                 due(t, "moves")
-        if not last:
-            negate(t + 1)
-        else:
-            dma("Y", T.yx[:], T.W[:, XB:XB + V], "st0", [a("W", XB, V)], [], 3.7)
+        marks[t].append(len(ops) - 1)
+        if last:
+            dma("Y", T.yx[:], T.W[:, 0:V], "st0", [a("W", 0, V)], [], 3.7)
         step("moves")
         lo = 0
-        for n in FB:
+        for n in FB[t]:
             mms([(a("B5", lo, n), a("ID"), a("S2", 16 * lo + k, n, 16), k == 0, k == 15) for k in range(16)])
             lo += n
-        act(a("FA2"), a("B5", 0, LF), F_.Relu, 1.0, -1.0)
-        mm(a("B5", LF, LF), a("BO"), a("FA2"), True, True)
-        act(a("YW", K, LF), a("B5", LF, LF), F_.Sign, -3.5)
+        act(a("YW", K, lo), a("B5", 0, lo), F_.Relu, 8.0, -8.0)
         due(t, "wake")
+        if lo < LF:
+            scan(a("M2", 0, 16 * (LF - lo)), a("SEGA", 0, 16 * (LF - lo)), a("S2", 16 * lo), 0.0, A_.add, A_.max)
+            ts(a("YW", K + lo, LF - lo), a("M2", 15, LF - lo, 16), 0.5, A_.is_lt, 8.0, A_.mult)
+            due(t, "wake")
         if not last:
-            mm(a("B2", 256, 1), a("O32"), a("SGA"), True, True)
-            copy(a("AI", 0, 1), a("B2", 256, 1))
+            run("S", lambda: g.scalar.activation(T.NS[:], T.NV[:], F_.Identity, accum_out=T.SGA[:]), [a("SGA"), a("NS")], [a("NV")], 90 * CYC)
+            mm(a("B2", 500, 1), a("O32"), a("SGA"), True, True)
+            copy(a("AI", 0, 1), a("B2", 500, 1))
             ts(a("AI", 1, 1), a("AI", 0, 1), 3, A_.bitwise_and)
-            tt(a("TT"), a("TH"), a("AI", 1, 1), A_.add)
-            ts(a("NT1"), a("TT"), -1.0, A_.mult, 65.0, A_.add)
+            ts(a("TT", 0, 1), a("AI", 1, 1), UN, A_.mult, a("TH", 0, 1), A_.add)
+            ts(a("TT", 1, 1), a("AI", 1, 1), -1.0, A_.mult, a("TH", 1, 1), A_.add)
         step("count")
-        come = a("B2", 300, 1)
-        mm(come, a("BO"), a("NN", 8 * t + 1, 1), True, True)
-        ts(a("NT"), a("DR"), come, A_.is_gt, 1024.0, A_.mult)
+        ts(a("JLU"), a("NN", 16 * t, 8), 255.0, A_.add)
         if last:
-            ts(a("NTN"), a("DRN"), come, A_.is_gt, 1024.0, A_.mult)
-        mm(a("B2", 320, Q), a("ID"), a("DRN" if last else "DR"), True, False)
-        mm(a("B2", 320, Q), a("ID"), a("NTN" if last else "NT"), False, True)
-        tt(a("IXF"), a("B2", 320, Q), a("JC", Q if last else 0, Q), A_.min)
-        ts(a("IX"), a("IXF"), -1.0, A_.add)
-        act(a("C%d" % (t + 1), 0 if last else JW, K), ind(a(C), a("IX")), F_.Identity, -OFF if last else 0.0)
+            act(a(C, 2 * JW, K), a(C, 2 * JW, K), F_.Identity, MAGIC)
+            ts(ind(a(C, 0, 2 * JW), a("JLU")), a("AR", t * JW, JW), 1.0, A_.mult, MAGIC, A_.add)
+        else:
+            act(ind(a(C, 0, 2 * JW), a("JLU")), a("AR", t * JW, JW), F_.Silu)
+        act(a("NT"), a("DRN" if last else "DR"), F_.Sign, a("NN", 16 * t + 8, 1), 1.0 - UN)
+        mm(a("B2", 384, Q), a("ID"), a("DRN" if last else "DR"), True, False)
+        mm(a("B2", 384, Q), a("P1K"), a("NT"), False, True)
+        tt(a("IXF"), a("B2", 384, Q), a("JC", Q if last else 0, Q), A_.min)
+        ts(a("IX"), a("IXF"), 1023.0, A_.add)
+        if last:
+            for i, (lo, n) in enumerate(YCS):
+                act(a("C3", 16 * lo, 16 * n), ind(a(C), a("IX", lo, n)), F_.Identity, -MAGIC - OFF)
+                dma("Y", T.yc[:, 16 * lo:16 * (lo + n)], T.C3[:, 16 * lo:16 * (lo + n)], "st%d" % (2 + i), [a("C3", 16 * lo, 16 * n)], [], 1.8 + 1.5 * n / Q)
+        else:
+            act(a("C%d" % (t + 1), 2 * JW, K), ind(a(C), a("IX")), F_.Identity)
         step("come")
-        act(a("FW"), ind(a("YW"), a("PL")), F_.Identity, 3.0, 2.0)
-        for j in range(3):
-            scan(a("FWS", 256 * j, 256), a("FW", 256 * j, 256), CWM, 0.0, A_.max, A_.mult)
-        y = a("FWS", 15, Q, 16)
-        mm(a("B5", 384, 2 * Q), a("ONE", 0, 128, p=1), a("ROW", 320, 2 * Q), True, False)
-        mms([(a("B5", 384 + Q * j, Q), a("ID"), a("XS"), False, False) for j in range(2)])
-        mms([(a("B5", 384 + Q * j, Q), a("PK"), a("NT"), False, j == 1) for j in range(2)])
+        act(a("FW"), ind(a("YW"), a("PL")), F_.Identity)
+        y = a("B5", 448, Q)
+        mms([(y, ONE1, a("ROW", 192, Q), True, False), (y, a("ID"), a("X4"), False, False), (y, a("I75"), a("DR"), False, False)])
+        mms([(y, a("EP", 15 - p, 128), a("FW", p, Q, 16), False, p == 15) for p in range(16)])
         if not last:
-            tt(a("FL", 0, Q), a("B5", 384, Q), y, A_.is_lt)
-            tt(a("FL", Q, Q), a("B5", 384 + Q, Q), y, A_.is_gt)
-        tt(a("X1"), a("B5", 384, Q), y, A_.subtract)
-        ts(a("XS"), a("X1"), 1.0 / 16, A_.add, 0.0, A_.max)
-        if not last:
+            act(a("TE"), a("X4"), F_.Identity, 19968.0, -12.0)
+            ts(a("FL", 2 * Q, Q), y, 0.0, A_.is_le)
+            tt(a("FL", Q, Q), y, a("TE"), A_.is_gt)
+        ts(a("FL", 0, Q), y, a("NN", 16 * t + 9, 1), A_.is_le)
+        tt(a("LL"), y, a("X4"), A_.is_gt)
+        x4 = a("B2", 440, Q)
+        mms([(x4, a("ID"), a("X4"), True, False), (x4, a("I5"), a("LL"), False, False), (x4, a("NI4"), a("FL", 0, Q), False, True)])
+        if last:
+            act(a("YF"), x4, F_.Relu, 0.0, 1.0 / 512)
+        else:
+            act(a("X4"), x4, F_.Relu)
             lists(t + 1)
-    dma("S", T.yc[:], T.C3[:], "st1", [a("C3")], [], 3.3)
-    ts(a("YF"), a("XS"), 8.0, A_.mult)
-    dma("Y", T.yf[:], T.YF[:], "st2", [a("YF")], [], 2.2)
+    dma("Y", T.yf[:], T.YF[:], "st1", [a("YF")], [], 2.2)
     if "order" not in PLAN:
         step("end")
-        PLAN["order"] = plan(ops, dues, parts)
+        PLAN["order"] = plan(ops, dues, parts, marks, loads)
     for i in PLAN["order"]:
         ops[i][6]()
     for q in cnt:
         g.wait_ge(T.sem["s" + q], cnt[q])
-    for i in range(5):
-        g.wait_ge(T.sem["ld%d" % i], 16)
-    for i in range(3):
-        g.wait_ge(T.sem["st%d" % i], 16)
-    for i in range(4):
-        g.wait_ge(T.sem["sn%d" % i], 16)
-    for t in range(RO):
-        for s in ("ls", "arr", "nl", "na"):
-            g.wait_ge(T.sem[s + str(t)], 8)
+    for s in final:
+        g.wait_ge(T.sem[s], final[s])

@@ -9,7 +9,7 @@ XB = 16 * J
 SB = 2 * V
 DU = SB + 16
 WW = DU + 2 * XB
-LW = 2 * K + 880
+LW = 4 * K
 JW = 128
 CW = 2 * JW + K
 OFF = 64.0
@@ -24,33 +24,35 @@ B, F, U, I = "bfloat16", "float32", "uint16", "int32"
 SHAPES = {
     B: {"W": WW, "S": 16 * LA, "M": 16 * LA, "S2": 16 * LF, "M2": 512, "YW": LW, "ONE": 512, "BO": 128, "NBO": 128, "TS": 128,
         "NTS": 128, "ID": 128, "NI": 128, "I4": 128, "NI4": 128, "N2K": 128, "P1K": 128, "HI": 128, "NHI": 128, "I5": 128, "I75": 128,
-        "B75": 128, "BT": 128, "MA": 128, "MB": 128, "DM": 256, "SEGA": 1024, "RST": 2048,
+        "NQ": 128, "N15": 128, "B75": 128, "BT": 128, "MA": 128, "MB": 128, "DM": 256, "SEGA": 1024, "RST": 16 * LA,
         "I2K": 16, "NIN": 8, "CN": 128, "RX": 128, "RY": 128, "MH": 512, "SE": 512, "MX": 512, "FL": 3 * Q, "PRE": 2 * Q, "X4": Q,
-        "DR": Q, "DRN": Q, "NT": Q, "LH": 384, "FW": K, "SG": LA, "BTM": 128, "CUM": 144, "GT": 128, "EE": 256 * J,
+        "DR": 64, "TR": 64, "IDS": 320, "QR": Q, "DRN": Q, "NT": Q, "FW": K, "SG": LA, "BTM": 128, "CUM": 144, "GT": 128, "EE": 256 * J,
         "BJ": 128 * J, "TJ": 128 * J, "B64": 128, "TRI": 128, "XN": 256, "XV": 512, "EP": 144, "NV": 16, "LL": Q, "BI": 4, "NB": 48},
-    H: {"CZ": LA, "Z": 16 * LA, "VM": 512},
-    F: {"C0": CW, "C1": CW, "C2": CW, "C3": K, "LN": LW, "TH": 2, "TT": 2, "O32": 128, "JC": 148, "P3": 3 * Q, "P4": 3 * Q,
-        "RS3": 3 * Q, "R": 512, "VF": 16, "SF": 32, "CJ": J, "TE": Q, "DEO": 128, "PJ": 128, "JB": 128,
-        "JL": 16, "NN": 16 * RO, "RN": 16 * RO, "AR": RO * JW, "IXF": Q, "SGA": 1, "YF": Q, "RL": RO * JW, "NS": 16},
-    U: {"OA": LA, "OF": LF, "PL": Q, "IX": Q, "L2": 16, "LT": 24, "GL": 16, "SL": 32, "JLU": 8},
-    I: {"CI": K, "FR": Q, "TI": 1, "AI": 2, "LQI": 16, "RI": 32, "RA": 32},
+    H: {"CZ": LA, "Z": 16 * LA, "VM": 512, "POS": 2 * Q, "FP": Q},
+    F: {"C0": CW, "C1": CW, "C2": CW, "C3": K, "LN": LW, "TH": 2, "TT": 2, "O32": 128, "JC": 172, "P3": 3 * Q, "PX": 2 * Q,
+        "VF": 16, "CJ": J + 2, "TE": Q, "DEO": 128, "PJ": 128, "JB": 128,
+        "JL": 16, "NN": 16 * RO, "RN": 16 * RO, "AR": RO * JW, "SGA": 1, "YF": Q, "RL": RO * JW, "NS": 16},
+    U: {"OA": LA, "OF": LF, "PL": Q, "IX": Q, "L2": 16, "GL": 16, "SL": 32, "JLU": 8},
+    I: {"CI": K, "FR": Q, "TI": 1, "AI": 2, "LQI": 16, "R": 512, "RA": 32},
 }
 SCRATCH = {n: ("sbuf", [128, w], d) for d, tab in SHAPES.items() for n, w in tab.items()}
-SCRATCH.update({"PM": ("sbuf", [16, 128], B), "PMF": ("sbuf", [16, 128], F), "TB": ("sbuf", [16, 148], F), "CU": ("sbuf", [16, 108], F),
-                "CV": ("sbuf", [16, 8], F), "KC": ("sbuf", [1, 512], B), "KR": ("sbuf", [1, 512], F), "SN": ("sbuf", [128, LA], F),
-                "ROW": ("sbuf", [1, 384], H)})
+SCRATCH.update({"PM": ("sbuf", [16, 128], B), "PMF": ("sbuf", [16, 128], F), "TB": ("sbuf", [16, 172], F),
+                "KC": ("sbuf", [1, 512], B), "KR": ("sbuf", [1, 512], F), "SN": ("sbuf", [128, LA], F),
+                "ROW": ("sbuf", [1, 576], H)})
 for _i in range(8):
     SCRATCH["B%d" % _i] = ("psum", [128, 512], F)
-SEMAPHORES = ["sV", "sS", "sP", "sG"] + ["ld%d" % i for i in range(6)] + ["st%d" % i for i in range(4)] + ["sn%d" % i for i in range(4)] \
-    + ["cp%d" % i for i in range(1, 10)] \
+SEMAPHORES = ["sV", "sS", "sP", "sG"] + ["ld%d" % i for i in range(8)] + ["st%d" % i for i in range(4)] + ["sn%d" % i for i in range(4)] \
+    + ["cp%d" % i for i in range(16)] \
     + [s + str(i) for s in ("arr", "ls", "ra", "na", "nl", "rn") for i in range(RO)]
 
 
 CYC, PEC = np.array([0.00083, 0.0012, 0.00083]), np.array([0.00045, 0.0006, 0.0008])
 GAT, SCA, WAKES, WEIGHT = np.array([1.5, 1.9, 1.5]), np.array([3.5, 5.0, 3.5]), [0.22, 0.22, 0.18], [1.0, 0.35, 0.3]
-HOPN, HOPJ, ONCE = np.array([1.5, 2.4, 1.5]), np.array([1.9, 3.0, 1.9]), np.array([0.6, 1.2, 0.6])
-LOAD = np.array([0.85, 1.1, 0.65])
-PASSES, SEED, JITTER, SWAPS, HEAT, DRIFT, MARK = 300, 3, 0.8, 40000, 0.05, 0.4, 0.3
+HOPN, HOPJ, ONCE = np.array([1.5, 2.2, 2.2]), np.array([1.9, 2.8, 2.8]), np.array([0.6, 1.2, 1.4])
+LOAD, STORE = np.array([0.7, 1.0, 0.6]), np.array([0.8, 1.0, 0.7])
+PASSES, SEED, JITTER, SWAPS, HEAT, DRIFT, MARK, POOL, CUT = 150, 21, 0.8, 8000, 0.08, 0.4, 0.3, 4, 20
+ONV = ("TJ", "IDS", "KC", "JC", "MH", "NB", "I5", "I75")
+CIS = ((0, 7, 3.3), (7, 7, 4.25), (14, 2, 4.55))
 PLAN, RLEN, STRETCH, SHIFT = {}, 15.0, 2.0, 2.0
 PULL = {("send", 2): 2.0, ("come", 2): 2.0, ("joint", 2): 2.0}
 INORDER = "P"
@@ -58,16 +60,35 @@ WAR = "P"
 XH = 1536
 OAS = ((192, 64), (128, 64), (0, 128))
 YCS = ((0, Q // 2), (Q // 2, Q // 2))
-XS = [(0, 1), (1, 1), (2, 1)]
-FB = [(80, 80), (80, 80), (64, 64, 64)]
+CV = (Q // 2, 0)
+FK = 8
+GS = ()
+XS = [(0, 1), (1, 1)]
+FB = [(64, 96), (64, 96), (64, 64, 64)]
 D0 = {"A3": 0.0, "A2": 0.0, "A1": 1.6, "A0": 3.2, "F0": 3.1, "F1": 4.8, "F2": 6.7, "lit": 1.7, "viol": 6.3, "send": 6.5, "joint": 5.0,
       "keys": 7.5, "wake": 8.5, "lanes": 12.0, "moves": 12.0}
 DUE = [dict(D0), dict(D0), dict(D0)]
-GA = [(("S", 64), ("V", 64), ("S", 64), ("V", 48), ("S", 16))] * RO
-GF = [(("S", 80), ("S", 80), ("S", 32))] * 2 + [(("S", 64), ("S", 64), ("S", 64))]
+GA = [(("S", 64), ("V", 64), ("S", 64), ("V", n), ("S", 64 - n))[:4 + (n < 64)] for n in (48, 64, 32)]
+GF = [(("S", 64), ("S", 48), ("S", 48), ("S", 32))] * 2 + [(("S", 64), ("S", 64), ("S", 64))]
 
 
-def plan(ops, dues, parts, marks, loads):
+def search(ops, dues, parts, marks, loads):
+    pool = [plan(ops, dues, parts, marks, SEED + 100 * i, None, SWAPS, HEAT) for i in range(POOL)]
+    timed, pool = pool[0][1], [x[0] for x in pool]
+    for cut in list(range(CUT, len(ops), CUT)) * 2:
+        for x in list(pool):
+            head = set(x[1][:cut])
+            for y in list(pool):
+                new = x[1][:cut] + [i for i in y[1] if i not in head]
+                score, res = timed(new, cut, x[2])
+                if score < min(x[0], y[0]) - 1e-9:
+                    pool.remove(max(pool, key=lambda z: z[0]))
+                    pool.append((score, new, res))
+    order = plan(ops, dues, parts, marks, SEED + 1, min(pool, key=lambda z: z[0])[1], 2 * SWAPS, HEAT / 3)[0][1]
+    return list(range(loads)) + [i for i in order if i >= loads]
+
+
+def plan(ops, dues, parts, marks, seed, given, swaps, heat):
     n = len(ops)
     times = [[(np.zeros(len(WAKES)) + x).tolist() for x in o[4:6]] for o in ops]
     ops = [o[:4] + (times[i][0][0], times[i][1][0], o[6]) for i, o in enumerate(ops)]
@@ -142,8 +163,8 @@ def plan(ops, dues, parts, marks, loads):
     key, best = [0.0] * n, None
     for i in range(n - 1, -1, -1):
         key[i] = min([dues.get(i, 200.0)] + [key[k] - lat - ops[i][5] for k, lat in succ[i]])
-    rng = np.random.default_rng(SEED)
-    for it in range(PASSES):
+    rng = np.random.default_rng(seed)
+    for it in range(0 if given else PASSES):
         start = place(key, False)
         order = sorted(range(n), key=lambda i: (round(start[i], 6), i))
         ends = [replay(order, m) for m in range(len(WAKES))]
@@ -190,10 +211,10 @@ def plan(ops, dues, parts, marks, loads):
 
     queue = [o[0] for o in ops]
     occs, durs = [[[times[i][x][m] for i in range(n)] for m in range(len(WAKES))] for x in range(2)]
-    order = best[2]
+    order = given or best[2]
     score, res = timed(order, 0, [(0.0, [0.0] * n, [0.0] * n, [-1] * n)] * len(WAKES))
     top = (score, order, res)
-    for it in range(SWAPS):
+    for it in range(swaps):
         if rng.random() < DRIFT:
             a = b = int(rng.integers(n - 1))
             while b < n - 1 and (b == a or queue[order[b]] != queue[order[a]]):
@@ -235,13 +256,13 @@ def plan(ops, dues, parts, marks, loads):
             mid = order[a + 1:b + 1]
             new = order[:a] + [x for x in mid if not above[x] >> u & 1] + [u] + [x for x in mid if above[x] >> u & 1] + order[b + 1:]
         s2, r2 = timed(new, a, res)
-        if s2 < score + HEAT * (1 - it / SWAPS) * rng.exponential():
+        if s2 < score + heat * (1 - it / swaps) * rng.exponential():
             order, score, res = new, s2, r2
             if score < top[0]:
                 top = (score, order, res)
     PLAN["end"] = [r[0] for r in top[2]]
     PLAN["dbg"] = (ops, None, succ, [top[2][0][2][i] - durs[0][i] for i in range(n)])
-    return list(range(loads)) + [i for i in top[1] if i >= loads]
+    return top, timed
 
 
 def route(topo, src, dst):
@@ -387,10 +408,23 @@ def rank_program(g, core, T, topo):
             note(tag, reads, writes, sem, 16, dict(known[q]))
         if sem[:2] == "st":
             net = ("", tag, 1)
-            ops.append((q, tag, reads, [net], 0.05, 1.8, issue))
-            ops.append(("D", tag + "x", [net], [], dur - 1.8, dur - 1.8, lambda: None))
+            ops.append((q, tag, reads, [net], 0.05, 1.8 * STORE, issue))
+            ops.append(("D", tag + "x", [net], [], (dur - 1.8) * STORE, (dur - 1.8) * STORE, lambda: None))
             return
         ops.append((q, tag, reads, writes, 0.0 if sem[0] == "l" else 0.05, dur, issue))
+
+    def copies(pairs, after):
+        net = ("", "copies", 1)
+
+        def issue():
+            need("Y", None, [x[1] for x in pairs] + [after], [x[0] for x in pairs])
+            for i, (out, in_) in enumerate(pairs):
+                g.sync.dma_start(out[0], in_[0]).then_inc(T.sem["cp%d" % i], 16)
+                note("cp%d" % i, [in_], [out], "cp%d" % i, 16, dict(known["Y"]))
+        ops.append(("Y", "copies", [x[1] for x in pairs] + [after], [net], 0.05 * len(pairs), 1.8 * STORE, issue))
+        for i, (out, in_) in enumerate(pairs):
+            final["cp%d" % i] = 16
+            ops.append(("N", "cp%d" % i, [net, in_], [out], 0.0, 0.45 * (i + 1) * STORE, lambda: None))
 
     def width(x):
         return bin(x[2]).count("1")
@@ -436,6 +470,8 @@ def rank_program(g, core, T, topo):
             run("S", lambda: g.scalar.activation(ap(out), ap(x), func, bias=ap(bias), scale=scale), out, ins, c)
 
     def times(out, x, c):
+        if out[1] in ONV:
+            return ts(out, x, c, A_.mult)
         ins = [x] + ([c] if isinstance(c, tuple) else [])
         run("S", lambda: g.scalar.activation(ap(out), ap(x), F_.Identity, scale=ap(c)), out, ins, CYC * max(64, width(out)))
 
@@ -477,8 +513,8 @@ def rank_program(g, core, T, topo):
 
     dma("Y", T.FR[:], T.fr[:], "ld0", [], [a("FR")], 2.2 * LOAD)
     dma("Y", T.TI[:], T.th[:], "ld1", [], [a("TI")], 2.4 * LOAD)
-    dma("Y", T.CI[:, 0:K // 2], T.cl[:, 0:K // 2], "ld5", [], [a("CI", 0, K // 2)], 3.4 * LOAD)
-    dma("Y", T.CI[:, K // 2:K], T.cl[:, K // 2:K], "ld2", [], [a("CI", K // 2)], 4.5 * LOAD)
+    for i, (p, n, at) in enumerate(CIS):
+        dma("Y", T.CI[:, Q * p:Q * (p + n)], T.cl[:, Q * p:Q * (p + n)], "ld%d" % (5 + i), [], [a("CI", Q * p, Q * n)], at * LOAD)
     dma("Y", T.W[:, 0:XH], T.xv[:, 0:XH], "ld3", [], [a("W", 0, XH)], 6.8 * LOAD)
     dma("Y", T.W[:, XH:V], T.xv[:, XH:V], "ld4", [], [a("W", XH, V - XH)], 7.5 * LOAD)
     loads, loaded = len(ops), a("W", XH, V - XH)
@@ -498,21 +534,13 @@ def rank_program(g, core, T, topo):
         ts(a(name), a("ID"), c, A_.mult)
     ts(a("NTS"), a("TS"), -1.0, A_.mult)
     starts = [[divmod(AS * t % K, Q), divmod(FS * t % K, Q)] for t in range(RO)]
-    iota(a("CU", 0, Q), [[0, Q]], 4095, 0)
-    iota(a("CU", Q, Q), [[1, Q]], K, 0)
-    iota(a("CU", 2 * Q, 12), [[0, 12]], 0, 0)
-    iota(a("CV"), [[0, 8]], K, 0)
-    for t in range(RO):
-        p0, q0 = starts[t][1]
-        iota(a("CU", 2 * Q + 4 * t + 2, 1), [[0, 1]], -Q * p0 - q0, Q)
-        if t:
-            sel(a("CV", 2 * t, 1), a("CV", 6, 1), [[0, 1]], A_.is_ge, 0.0, p0 - 1, -1)
-            sel(a("CV", 2 * t + 1, 1), a("CV", 6, 1), [[0, 1]], A_.is_equal, 0.0, p0, -1)
-    iota(a("P3", 0, Q, 3), [[16, Q]], 2 * K, 1)
-    fill(a("RS3"), 0.0)
-    fill(a("RS3", 0, Q, 3), 1e6)
-    fill(a("ROW", 0, Q), 4096.0)
-    fill(a("ROW", Q, 16), 0.0)
+    iota(a("P3", 2 * Q, Q), [[16, Q]], 2 * K, 1)
+    fill(a("ROW", 512, Q), 4096.0 - 2 * K)
+    fill(a("ROW", 0, Q), 1023.0)
+    fill(a("ROW", 384, Q), 2.0 * K)
+    fill(a("ROW", 384 + Q, Q), 4096.0 + K)
+    fill(a("ROW", 384 + 2 * Q, 2, 2), -1.0)
+    fill(a("ROW", 385 + 2 * Q, 2, 2), 0.0)
     fill(a("ROW", 64, 128), -4640.0)
     fill(a("ROW", 192, Q), 4608.0)
     fill(a("ROW", 256, 128), V + OFF)
@@ -521,11 +549,6 @@ def rank_program(g, core, T, topo):
     def sentinels(t):
         dma("Y", T.LN[:, 0:LA], T.SN[:], "sn%d" % (2 * t), [a("SN")], [a("LN", 0, LA)])
         dma("Y", T.LN[:, K:K + LF], T.SN[:, 0:LF], "sn%d" % (2 * t + 1), [a("SN")], [a("LN", K, LF)])
-
-    def consts_of_lists(t):
-        mm(a("B6", 0, 108), a("PMF"), a("CU"), True, False)
-        if t:
-            mm(a("B6", 2 * Q + 4 * t + 2, 2), a("PMF"), a("CV", 2 * t, 2), False, False)
 
     def cyclic(t):
         for c in range(2):
@@ -536,29 +559,36 @@ def rank_program(g, core, T, topo):
             sel(a("SE", i, 128), a("BO"), GP, A_.is_equal, 0.0, -p0, 1)
             sel(a("MX", i, 128), a("NBO"), KP, A_.is_equal, 0.0, -p0, 0)
             mms([(a("B6", 256 + 128 * c, 128), a("ID"), m, j == 0, j == 2) for j, m in enumerate((a("NTS"), rx, ry))])
-        act(a("MH", 256 * (t - 1), 256), a("B6", 256, 256), F_.Identity)
+        times(a("MH", 256 * (t - 1), 256), a("B6", 256, 256), 1.0)
 
     def lists(t):
-        fa, fb, fd = a("FL", 0, Q), a("FL", 2 * Q if t else 0, Q), a("FL", Q, Q)
+        fa, fb, fd = a("FL", 0, Q), a("FL", 2 * Q, Q), a("FL", Q, Q)
+        mm(a("B6", 0, 2 * Q + 4), ONE1, a("ROW", 384, 2 * Q + 4), True, False)
         scan(a("PRE", Q, Q), fb, fd, 0.0, A_.add, A_.add)
         scan(a("PRE", 0, Q), a("ONE", 0, Q), fa, 0.0, A_.mult, A_.subtract)
-        mm(a("B6", 0, Q), a("NI4"), fa, False, False)
+        mm(a("B6", 0, Q), a("N15" if t else "NI4"), fa, False, False)
+        if not t:
+            mm(a("B6", 0, Q), ONE1, a("ROW", 512, Q), False, False)
+        else:
+            tt(a("FP"), fa, a("POS", Q * (t - 1), Q), A_.mult)
+            mm(a("B6", 0, Q), a("ID"), a("POS", Q * (t - 1), Q), False, False)
         mm(a("B6", Q, Q), a("I4"), fb, False, False)
         mm(a("B6", Q, Q), a("I4"), fd, False, False)
-        for c in range(2):
-            q0, i, b = starts[t][c][1], 128 * (2 * (t - 1) + c), 2 * Q + 4 * t + 2 * c
+        for c in (1, 0):
+            q0, i, b = starts[t][c][1], 128 * (2 * (t - 1) + c), 2 * Q + 2 * c
             mm(a("B6", b, 1), a("MH", i, 128) if t else a("NTS"), a("PRE", Q * c + Q - 1, 1), False, False)
             if t:
                 mm(a("B6", b, 1), a("SE", i, 128), a("PRE", Q * c + q0 - 1, 1), False, False)
                 mm(a("B6", b + 1, 1), a("MX", i, 128), a("PRE", Q * c + Q - 1, 1), False, False)
-        mm(a("B6", 0, 2 * Q), a("NI"), a("PRE", 0, 2 * Q), False, True)
+        mms(([(a("B6", 0, Q), a("NI"), a("FP"), False, False)] if t else []) + [(a("B6", 0, 2 * Q), a("NI"), a("PRE", 0, 2 * Q), False, True)])
         for c in range(2):
-            q0, b = starts[t][c][1], 2 * Q + 4 * t + 2 * c
-            ts(a("P3", 3 * q0 + 1 + c, Q - q0, 3), a("B6", Q * c + q0, Q - q0), a("B6", b, 1), A_.add)
+            q0, b = starts[t][c][1], 2 * Q + 2 * c
+            ts(a("P3", Q * c + q0, Q - q0), a("B6", Q * c + q0, Q - q0), a("B6", b, 1), A_.add)
             if q0:
-                ts(a("P3", 1 + c, q0, 3), a("B6", Q * c, q0), a("B6", b, 1), A_.add, a("B6", b + 1, 1), A_.add)
-        scan(a("P4"), a("RS3"), a("P3"), 0.0, A_.add, A_.min)
-        copy(a("PL"), a("P4", 2, Q, 3))
+                ts(a("P3", Q * c, q0), a("B6", Q * c, q0), a("B6", b, 1), A_.add, a("B6", b + 1, 1), A_.add)
+        if not t:
+            tt(a("P3", 0, Q), a("P3", 0, Q), a("P3", 2 * Q, Q), A_.min)
+        tt(a("PL"), a("P3", 0, Q), a("P3", Q, Q), A_.min)
         act(ind(a("LN"), a("PL")), a("C%d" % t, 2 * JW, K), F_.Silu)
         if t:
             marks[t - 1].append(len(ops) - 1)
@@ -572,15 +602,15 @@ def rank_program(g, core, T, topo):
             sentinels(t)
         step("offsets")
         dr = a("B6", 128, Q)
-        mms([(a("B6", 128, Q + 1), ONE1, a("ROW", 0, Q + 1), True, False), (dr, a("NI4"), fd, False, False)]
-            + ([(dr, a("NI4"), fb, False, False), (dr, a("I4"), fa, False, False)] if t else []))
+        mms([(dr, ONE1, a("QR", 0, Q, p=1), True, False), (a("B6", 128 + Q, 1), a("TS"), a("QR", Q - 1, 1), False, False),
+             (dr, a("NI4"), fd, False, False), (dr, a("NI4"), fb, False, False), (dr, a("I4"), fa, False, False)])
         mms([(dr, a("ID"), a("PRE", Q * c, Q), False, False) for c in range(2)]
             + [(a("B6", 128 + Q, 1), a("TS"), a("PRE", Q * c + Q - 1, 1), False, c == 1) for c in range(2)])
-        ts(a("DR"), dr, a("B6", 128 + Q, 1), A_.add, 1024.0, A_.min)
+        ts(a("DR", 0, Q), dr, a("B6", 128 + Q, 1), A_.add, 1024.0, A_.min)
         if t == RO - 1:
-            for j in range(3):
-                tt(a("LH", 128 * j, 128), ind(a("DR"), a("LT", 8 * j, 8)), a("BO"), A_.mult)
-                mm(a("B6", 192 + j, 16, 3), a("LH", 128 * j, 128), a("DM", 0, 16), True, True)
+            run("V", lambda: g.vector.transpose(T.TR[:], T.DR[:]), a("TR"), [a("DR")], 64 * CYC)
+            mms([(a("B6", 192 + e, 16, 3), a("IDS", 160 * (e % 2) + 16 - 16 * (c - e % 2), 128), a("TR", 32 * (e // 2) + 16 * c, 16),
+                  e + c == 0, e + c == 3) for e in range(3) for c in range(2)])
             copy(a("DRN"), a("B6", 192, Q))
 
     def gather(q, lo, n, frozen, th):
@@ -598,11 +628,12 @@ def rank_program(g, core, T, topo):
 
     times(a("LN", 0, LA), a("ONE", 0, LA), 2 * V + OFF)
     times(a("LN", K, LF), a("ONE", 0, LF), 2 * V + OFF)
-    consts_of_lists(0)
     for p in range(16):
         ts(a("C0", 2 * JW + p, Q, 16), a("CI", Q * p, Q), OFF, A_.add)
     ts(a("FL", 0, Q), a("FR"), 0.5, A_.is_lt)
     ts(a("FL", Q, Q), a("FR"), 3.5, A_.is_gt)
+    ts(a("FL", 2 * Q, Q), a("FR"), 0.5, A_.is_lt, 1.0, A_.subtract)
+    iota(a("QR"), [[1, Q]], 1, 0)
     ts(a("X4"), a("FR"), 512.0, A_.mult)
     lists(0)
     for lo, n in ((0, XH), (XH, V - XH)):
@@ -615,16 +646,12 @@ def rank_program(g, core, T, topo):
     fill(a("RST", 0, 512), 64 * UN)
     fill(a("RST", 15, 32, 16), 1152 * UN)
     times(a("YW", LA, 512), a("ONE"), 1.625)
-    for i in range(1, 4):
-        dma("Y", T.RST[:, 512 * i:512 * (i + 1)], T.RST[:, 0:512], "cp%d" % i, [a("RST", 0, 512), loaded], [a("RST", 512 * i, 512)], 2.0)
-    for i, lo in enumerate(range(K + LF, LW, 512)):
-        n = min(512, LW - lo)
-        dma("Y", T.YW[:, lo:lo + n], T.YW[:, LA:LA + n], "cp%d" % (4 + i), [a("YW", LA, n), loaded], [a("YW", lo, n)], 2.0)
-    for t in range(RO):
-        dma("Y", T["C%d" % t][:, 0:2 * JW], T.SN[:], "cp%d" % (7 + t), [a("SN"), loaded], [a("C%d" % t, 0, 2 * JW)], 2.0)
+    copies([(a("RST", 512 * i, 512), a("RST", 0, 512)) for i in range(7, 0, -1)]
+           + [(a("YW", lo, min(512, LW - lo)), a("YW", LA, min(512, LW - lo))) for lo in range(K + LF, LW, 512)]
+           + [(a("C%d" % t, 0, 2 * JW), a("SN")) for t in range(RO)], loaded)
     fill(a("CUM", 0, 16), 0.0)
     times(a("O32"), a("ONE", 0, 128), -1.0 / 4096)
-    for name, c in (("N2K", -2048.0), ("P1K", 1024.0), ("HI", 0.5), ("NHI", -0.5), ("I5", 512.0), ("I75", 1.75)):
+    for name, c in (("N2K", -2048.0), ("P1K", 1024.0), ("HI", 0.5), ("NHI", -0.5), ("I5", 512.0), ("I75", 1.75), ("NQ", -1.0 / 512), ("N15", -2.0 * K)):
         times(a(name), a("ID"), c)
     times(a("NBO"), a("BO"), -1.0)
     times(a("B75"), a("BO"), 1.75)
@@ -644,10 +671,15 @@ def rank_program(g, core, T, topo):
         fill(a("BI", 2 * i, 2, p=64, p0=64 * i), 8192.0)
     sel(a("XV", 256, 128), a("B64"), [[1, 128]], A_.is_gt, 0.0, 0, -1)
     sel(a("TRI"), a("XV", 256, 128), [[1, 128]], A_.not_equal, 4096.0, 0, -1)
-    tt(a("CJ"), a("BO", 0, J, 16), a("BO", 64, J, 16), A_.add)
+    tt(a("CJ", 0, J), a("BO", 0, J, 16), a("BO", 64, J, 16), A_.add)
     for j in range(J):
         ts(a("BJ", 128 * j, 128), a("B64"), a("CJ", j, 1), A_.mult, 1.0 / 16384, A_.mult)
         times(a("TJ", 128 * j, 128), a("TRI"), a("CJ", j, 1))
+    fill(a("DR", Q), 0.0)
+    fill(a("IDS"), 0.0)
+    tt(a("CJ", J, 2), a("CJ", 0, 2), a("CJ", 2, 2), A_.add)
+    for e in range(2):
+        times(a("IDS", 160 * e + 16, 128), a("ID"), a("CJ", J + e, 1))
     fill(a("NB", 32, 16), 0.0)
     for lo, n, b, sign in ((0, 4, 0, -2.0), (4, 8, 0, 2.0), (12, 4, 4, -2.0)):
         times(a("NB", lo, n), a("BO", 16 * b, n, 16), 1.0)
@@ -655,15 +687,18 @@ def rank_program(g, core, T, topo):
         if sign < 0:
             times(a("NB", 32 + lo, n), a("BO", 16 * b, n, 16), float(V))
     step("pairs")
-    iota(a("TB", 0, Q), [[16, Q]], 2 * JW - 1023, 1)
-    iota(a("TB", Q, Q), [[1, 16], [256, 3]], 2 * JW - 1023, 16)
+    iota(a("TB", 0, Q), [[16, Q]], 2 * JW, 1)
+    iota(a("TB", Q, Q), [[1, 16], [256, 3]], 2 * JW, 16)
     iota(a("TB", 2 * Q, 8), [[16, 8]], JW - 255, 1)
     iota(a("TB", 104, 4), [[0, 4]], 1000, 0)
-    iota(a("TB", 108, 24), [[16, 3], [0, 8]], 0, 1)
-    iota(a("TB", 132, 16), [[0, 2], [16, 8]], DU, 1)
-    mm(a("B1", 0, 148), a("PMF"), a("TB"), True, True)
-    act(a("JC"), a("B1", 0, 148), F_.Identity)
-    copy(a("LT"), a("JC", 108, 24))
+    iota(a("TB", 108, 16), [[0, 2], [16, 8]], DU, 1)
+    iota(a("TB", 124, Q), [[1, Q]], 0, Q)
+    mm(a("B1", 0, 172), a("PMF"), a("TB"), True, True)
+    times(a("JC"), a("B1", 0, 172), 1.0)
+    for t in range(1, RO):
+        ts(a("PX", 0, Q), a("JC", 124, Q), AS * t % K - 0.5, A_.is_lt, float(K), A_.mult)
+        ts(a("PX", Q, Q), a("JC", 124, Q), -float(AS * t % K), A_.add)
+        tt(a("POS", Q * (t - 1), Q), a("PX", 0, Q), a("PX", Q, Q), A_.add)
     iota(a("LQI"), [[1, 16]], 0, 0)
     copy(a("L2"), a("LQI"))
     sel(a("MA"), a("TS"), [[-1, 128]], A_.not_equal, -255.0, 0, 1)
@@ -683,11 +718,9 @@ def rank_program(g, core, T, topo):
         C, last, th = "C%d" % t, t == RO - 1, "TT" if t else "TH"
         step("dead")
         now[0] = t
-        if not last:
-            for u in range(1, RO) if t == 0 else ():
-                cyclic(u)
-            consts_of_lists(t + 1)
-            step("cyclic")
+        for u in range(1, RO) if t == 0 else ():
+            cyclic(u)
+        step("cyclic")
         lo = LA
         for q, n in GA[t]:
             lo -= n
@@ -702,7 +735,7 @@ def rank_program(g, core, T, topo):
         ts(a("SG"), a("OA"), V - 0.5, A_.is_gt)
         due(t, "lit")
         mms([(a("B5", 192, 128), a(l), a("CZ", j, 128, 2), j == 0, j == 1) for j, l in enumerate(("NHI", "HI"))])
-        act(a("DEO"), a("B5", 192, 128), F_.Identity)
+        times(a("DEO"), a("B5", 192, 128), 1.0 if t in GS else 2.0)
         mms([(a("B2", 256, 128), ONE1, a("ROW", 256, 128), True, False)]
             + [(a("B2", 256, 128), a("HI"), a("CZ", j, 128, 2), False, j == 1) for j in range(2)])
         for h in (1, 0):
@@ -711,14 +744,16 @@ def rank_program(g, core, T, topo):
             mms([(a(key, 128 * i, 128), a("SG", 128 * h, 128), a(m), False, False) for i, m in enumerate(("N2K", "P1K"))])
             mms([(a("B4" if h else "B7", j, 128, J), a("TJ", 128 * j, 128), a("DM", 0, 128), j == 0, False) for j in range(J)])
         for c in range(NA - 1, -1, -1):
-            lo, rs = 16 * CH * c, 16 * CH * (c % 2)
+            lo = 16 * CH * c
             scan(a("M", lo, 16 * CH), a("SEGA"), a("S", lo, 16 * CH), 0.0, A_.add, A_.max)
-            ts(a("RST", rs, CH, 16), a("M", lo + 15, CH, 16), a(th, 0, 1), A_.is_lt, 960 * UN, A_.subtract)
-            if c % 2 == 0:
-                ts(a("YW", CH * c, 128), a("M", lo + 15, 128, 16), a(th, 0, 1), A_.is_lt, 8.0, A_.mult)
-                mms([(a("B%d" % (c // 2), 128 * i, 128), a("YW", CH * c, 128), a("CN"), False, False) for i in range(2)])
+            if c % 2:
+                continue
+            ts(a("RST", lo, 128, 16), a("M", lo + 15, 128, 16), a(th, 0, 1), A_.is_lt, 960 * UN, A_.subtract)
+            ts(a("YW", CH * c, 128), a("M", lo + 15, 128, 16), a(th, 0, 1), A_.is_lt, 8.0, A_.mult)
+            mms([(a("B%d" % (c // 2), 128 * i, 128), a("YW", CH * c, 128), a("CN"), False, False) for i in range(2)])
             step("rows")
-            scan(a("Z", lo, 16 * CH), a("S", lo, 16 * CH), a("RST", rs, 16 * CH), 1.0, A_.min, A_.add)
+            for lo in (lo + 16 * CH, lo):
+                scan(a("Z", lo, 16 * CH), a("S", lo, 16 * CH), a("RST", lo, 16 * CH), 1.0, A_.min, A_.add)
             step("mask")
         for h in (1, 0):
             mms([(a("B%d" % h, k, 16, 16), a("Z", 16 * 128 * h + k, 128, 16), a("I2K"), False, False) for k in range(16)]
@@ -740,7 +775,10 @@ def rank_program(g, core, T, topo):
         for k0 in range(0, 16, 4):
             mms([(a("B2", k, 8, 16), a("S", 16 * (1 - h) + k, 128, 32), a("NIN") if h else BO8, h == 0, h == 1)
                  for k in range(15 - k0, 11 - k0, -1) for h in range(2)])
-        act(a("GT"), a("B2", 0, 128), F_.Sign, -0.5, 1.0 / UN)
+        if t in GS:
+            act(a("GT"), a("B2", 0, 128), F_.Sign, -0.5, 1.0 / UN)
+        else:
+            ts(a("GT"), a("B2", 0, 128), 0.0, A_.is_gt, 0.5, A_.subtract)
         mm(a("B2", 128, 128), a("GT"), a("ID"), True, True)
         tt(a("PJ"), a("B2", 128, 128), a("DEO"), A_.mult)
         tt(a("JB"), a("B2", 256, 128), a("PJ"), A_.add)
@@ -751,18 +789,28 @@ def rank_program(g, core, T, topo):
             key, same, vm, sm = "B%d" % h, "B4" if h else "B7", a("VM", 256 * h, 128), a("VM", 256 * h + 128, 128)
             scan(a("R", 256 * h, 256), a("SEGA", 0, 256), a(key, 0, 256), 0.0, A_.add, A_.max)
             due(t, "keys")
-            copy(a("RI", 16 * h, 16), a("R", 256 * h + 15, 16, 16))
-            ts(a("RA", 16 * h, 16), a("RI", 16 * h, 16), V - 1, A_.bitwise_and)
-            tt(a("VM", 256 * h, 256), ind(a("RA", 16 * h, 16), a("L2")), a("DM"), A_.mult)
+            ts(a("RA", 16 * h, 16), a("R", 256 * h + 15, 16, 16), V - 1, A_.bitwise_and)
+            if last:
+                tt(vm, ind(a("RA", 16 * h, 16), a("L2", 0, 8)), a("DM", 0, 128), A_.mult)
+                copy(sm, ind(a("RA", 16 * h, 16), a("L2", 8, 8)))
+            else:
+                tt(a("VM", 256 * h, 256), ind(a("RA", 16 * h, 16), a("L2")), a("DM"), A_.mult)
             tt(a("VF", 8 * h, 8), a("RA", 16 * h, 8), a("NV", 8 * h, 8), A_.add)
             step("chosen")
             mms([(a(same, j, 128, J), a("BJ", 128 * j, 128), vm, False, j == J - 1) for j in range(J)])
-            mms([(a(key, 256, 8), vm, BO8, True, False), (a(key, 256, 8), sm, a("NB", 20, 8), False, True)])
+            mms([(a(key, 256, 8), vm, BO8, True, last)] + ([] if last else [(a(key, 256, 8), sm, a("NB", 20, 8), False, True)]))
             copy(a("GL", 8 * h, 8), a(key, 256, 8))
-            mms([(a(key, 272, 16), a("DM", 0, 128), a("NB", 32, 16), True, False), (a(key, 272, 16), vm, a("NB", 0, 16), False, False),
+            ns = 1 if last else 2
+            mms([(a(key, 272, 8), vm, BO8, True, False)] if last else
+                [(a(key, 272, 16), a("DM", 0, 128), a("NB", 32, 16), True, False), (a(key, 272, 16), vm, a("NB", 0, 16), False, False),
                  (a(key, 272, 16), sm, a("NB", 16, 16), False, False)])
             new, other = [a("XV", 256 * h + XB + XB * b, XB) for b in range(2)], [a("XV", 256 * h + 3 * XB * b, XB) for b in range(2)]
-            if (t, h) in XS:
+            if last:
+                mms([(a("B3", 128 * h, 128), ONE1, ONE1, True, False), (a("B3", 128 * h, 128), sm, a("NQ"), False, True)])
+                tt(a("XV", 256 + 128 * h, 128), a("B3", 128 * h, 128), a("YW", 128 * h, 128), A_.mult)
+                tt(a("XN", 128 * h, 128), ind(a("W", 0, DU), a("GL", 8 * h, 8)), a("XV", 256 + 128 * h, 128), A_.add)
+                ts(a("XV", 128 * h, 128), a("XN", 128 * h, 128), 0.0, A_.max, 63.0, A_.min)
+            elif (t, h) in XS:
                 act(a("XN", 128 * h, 128), ind(a("W", 0, DU), a("GL", 8 * h, 8)), F_.Identity)
                 mms([(a("B3", 128 * h, 128), a("ID"), a(m, 128 * h, 128), m == "YW", m == "XN") for m in ("YW", "XN")])
                 for b in range(2):
@@ -777,12 +825,11 @@ def rank_program(g, core, T, topo):
             step("new%d" % h)
             for i in range(8):
                 ts(a("EE", 512 * h + XB * i, XB), a(same, XB * i, XB), a("VF", 8 * h + i, 1), A_.is_equal)
-            mms([(a(key, 272 + j, 4, J), a("EE", 512 * h + j, 128, J), a("BI"), False, j == J - 1) for j in range(J)])
-            tt(a("SF", 16 * h, 16), a(key, 272, 16), a("JC", 132, 16), A_.min)
-            copy(a("SL", 16 * h, 16), a("SF", 16 * h, 16))
+            mms([(a(key, 272 + j, 2 * ns, J), a("EE", 512 * h + j, 128, J), a("BI", 0, 2 * ns, 3 - ns), False, j == J - 1) for j in range(J)])
+            tt(a("SL", 8 * ns * h, 8 * ns), a(key, 272, 8 * ns), a("JC", 108, 8 * ns), A_.min)
             step("lowest%d" % h)
         for b in range(LA // XB - 1, -1, -1):
-            copy(ind(a("W"), a("SL", 2 * J * b, 2 * J)), a("XV", 2 * XB * b, 2 * XB))
+            copy(ind(a("W"), a("SL", ns * J * b, ns * J)), a("XV", ns * XB * b, ns * XB))
             if b == LA // XB - 1:
                 due(t, "moves")
         marks[t].append(len(ops) - 1)
@@ -791,7 +838,8 @@ def rank_program(g, core, T, topo):
         step("moves")
         lo = 0
         for n in FB[t]:
-            mms([(a("B5", lo, n), a("ID"), a("S2", 16 * lo + k, n, 16), k == 0, k == 15) for k in range(16)])
+            for k0 in range(0, 16, FK):
+                mms([(a("B5", lo, n), a("ID"), a("S2", 16 * lo + k, n, 16), k == 0, k == 15) for k in range(k0, k0 + FK)])
             lo += n
         act(a("YW", K, lo), a("B5", 0, lo), F_.Relu, 8.0, -8.0)
         due(t, "wake")
@@ -813,25 +861,26 @@ def rank_program(g, core, T, topo):
             ts(ind(a(C, 0, 2 * JW), a("JLU")), a("AR", t * JW, JW), 1.0, A_.mult, MAGIC, A_.add)
         else:
             act(ind(a(C, 0, 2 * JW), a("JLU")), a("AR", t * JW, JW), F_.Silu)
-        act(a("NT"), a("DRN" if last else "DR"), F_.Sign, a("NN", 16 * t + 8, 1), 1.0 - UN)
-        mm(a("B2", 384, Q), a("ID"), a("DRN" if last else "DR"), True, False)
+        act(a("NT"), a("DRN" if last else "DR", 0, Q), F_.Sign, a("NN", 16 * t + 8, 1), 1.0 - UN)
+        mms([(a("B2", 384, Q), ONE1, a("ROW", 0, Q), True, False), (a("B2", 384, Q), a("ID"), a("DRN" if last else "DR", 0, Q), False, False)])
         mm(a("B2", 384, Q), a("P1K"), a("NT"), False, True)
-        tt(a("IXF"), a("B2", 384, Q), a("JC", Q if last else 0, Q), A_.min)
-        ts(a("IX"), a("IXF"), 1023.0, A_.add)
+        tt(a("IX"), a("B2", 384, Q), a("JC", Q if last else 0, Q), A_.min)
         if last:
             for i, (lo, n) in enumerate(YCS):
                 act(a("C3", 16 * lo, 16 * n), ind(a(C), a("IX", lo, n)), F_.Identity, -MAGIC - OFF)
                 dma("Y", T.yc[:, 16 * lo:16 * (lo + n)], T.C3[:, 16 * lo:16 * (lo + n)], "st%d" % (2 + i), [a("C3", 16 * lo, 16 * n)], [], 1.8 + 1.5 * n / Q)
         else:
-            act(a("C%d" % (t + 1), 2 * JW, K), ind(a(C), a("IX")), F_.Identity)
+            act(a("C%d" % (t + 1), 2 * JW + 16 * CV[t]), ind(a(C), a("IX", CV[t])), F_.Identity)
+            if CV[t]:
+                copy(a("C%d" % (t + 1), 2 * JW, 16 * CV[t]), ind(a(C), a("IX", 0, CV[t])))
         step("come")
         act(a("FW"), ind(a("YW"), a("PL")), F_.Identity)
         y = a("B5", 448, Q)
-        mms([(y, ONE1, a("ROW", 192, Q), True, False), (y, a("ID"), a("X4"), False, False), (y, a("I75"), a("DR"), False, False)])
+        mms([(y, ONE1, a("ROW", 192, Q), True, False), (y, a("ID"), a("X4"), False, False), (y, a("I75"), a("DR", 0, Q), False, False)])
         mms([(y, a("EP", 15 - p, 128), a("FW", p, Q, 16), False, p == 15) for p in range(16)])
         if not last:
             act(a("TE"), a("X4"), F_.Identity, 19968.0, -12.0)
-            ts(a("FL", 2 * Q, Q), y, 0.0, A_.is_le)
+            ts(a("FL", 2 * Q, Q), y, 0.0, A_.is_le, 1.0, A_.subtract)
             tt(a("FL", Q, Q), y, a("TE"), A_.is_gt)
         ts(a("FL", 0, Q), y, a("NN", 16 * t + 9, 1), A_.is_le)
         tt(a("LL"), y, a("X4"), A_.is_gt)
@@ -845,7 +894,7 @@ def rank_program(g, core, T, topo):
     dma("Y", T.yf[:], T.YF[:], "st1", [a("YF")], [], 2.2)
     if "order" not in PLAN:
         step("end")
-        PLAN["order"] = plan(ops, dues, parts, marks, loads)
+        PLAN["order"] = search(ops, dues, parts, marks, loads)
     for i in PLAN["order"]:
         ops[i][6]()
     for q in cnt:

import numpy as np
from concourse.mybir import dt, AluOpType, AxisListType, ActivationFunctionType

A_, F_ = AluOpType, ActivationFunctionType
N, V, K, LA, LF, RO, AS, FS = 8, 2048, 768, 256, 192, 3, 170, 255
Q = K // 16
J = 4
XB = 16 * J
SB = 2 * V
DU = SB + 16
WW = DU + 2 * XB
LW = 4 * K
JW = 128
CW = 2 * JW + K
OFF = 64.0
NW = 10
CH = 64
NA, NF = LA // CH, LF // CH
MAGIC = 1.5 * 2.0 ** 23
UN = 2.0 ** -10
H = "float16"

B, F, U, I = "bfloat16", "float32", "uint16", "int32"
SHAPES = {
    B: {"W": WW, "S": 16 * LA, "M": 16 * LA, "S2": 16 * LF, "M2": 512, "YW": LW, "ONE": 512, "BO": 128, "NBO": 128, "TS": 128,
        "NTS": 128, "ID": 128, "NI": 128, "I4": 128, "NI4": 128, "N2K": 128, "P1K": 128, "HI": 128, "NHI": 128, "I5": 128, "I75": 128,
        "NQ": 128, "N15": 128, "B75": 128, "BT": 128, "MA": 128, "MB": 128, "DM": 256, "SEGA": 1024, "RST": 16 * LA,
        "I2K": 16, "NIN": 8, "CN": 128, "RX": 128, "RY": 128, "MH": 512, "SE": 512, "MX": 512, "FL": 3 * Q, "PRE": 2 * Q, "X4": Q,
        "DR": 64, "TR": 64, "IDS": 320, "QR": Q, "DRN": Q, "NT": Q, "FW": K, "SG": LA, "BTM": 128, "CUM": 144, "GT": 128, "EE": 256 * J,
        "BJ": 128 * J, "TJ": 128 * J, "B64": 128, "TRI": 128, "XN": 256, "XV": 512, "EP": 144, "NV": 16, "LL": Q, "BI": 4, "NB": 48},
    H: {"CZ": LA, "Z": 16 * LA, "VM": 512, "POS": 2 * Q, "FP": Q},
    F: {"C0": CW, "C1": CW, "C2": CW, "C3": K, "LN": LW, "TH": 2, "TT": 2, "O32": 128, "JC": 172, "P3": 3 * Q, "PX": 2 * Q,
        "VF": 16, "CJ": J + 2, "TE": Q, "DEO": 128, "PJ": 128, "JB": 128,
        "JL": 16, "NN": 16 * RO, "RN": 16 * RO, "AR": RO * JW, "SGA": 1, "YF": Q, "RL": RO * JW, "NS": 16},
    U: {"OA": LA, "OF": LF, "PL": Q, "IX": Q, "L2": 16, "GL": 16, "SL": 32, "JLU": 8},
    I: {"CI": K, "FR": Q, "TI": 1, "AI": 2, "LQI": 16, "R": 512, "RA": 32},
}
SCRATCH = {n: ("sbuf", [128, w], d) for d, tab in SHAPES.items() for n, w in tab.items()}
SCRATCH.update({"PM": ("sbuf", [16, 128], B), "PMF": ("sbuf", [16, 128], F), "TB": ("sbuf", [16, 172], F),
                "KC": ("sbuf", [1, 512], B), "KR": ("sbuf", [1, 512], F), "SN": ("sbuf", [128, LA], F),
                "ROW": ("sbuf", [1, 576], H)})
for _i in range(8):
    SCRATCH["B%d" % _i] = ("psum", [128, 512], F)
SEMAPHORES = ["sV", "sS", "sP", "sG"] + ["ld%d" % i for i in range(8)] + ["st%d" % i for i in range(4)] + ["sn%d" % i for i in range(4)] \
    + ["cp%d" % i for i in range(16)] \
    + [s + str(i) for s in ("arr", "ls", "ra", "na", "nl", "rn") for i in range(RO)]


CYC, PEC = np.array([0.00083, 0.0012, 0.00083]), np.array([0.00045, 0.0006, 0.0008])
GAT, SCA, WAKES, WEIGHT = np.array([1.5, 1.9, 1.5]), np.array([3.5, 5.0, 3.5]), [0.22, 0.22, 0.18], [1.0, 0.35, 0.3]
HOPN, HOPJ, ONCE = np.array([1.5, 2.2, 2.2]), np.array([1.9, 2.8, 2.8]), np.array([0.6, 1.2, 1.4])
LOAD, STORE = np.array([0.7, 1.0, 0.6]), np.array([0.8, 1.0, 0.7])
PASSES, SEED, JITTER, SWAPS, HEAT, DRIFT, MARK, POOL, CUT = 150, 21, 0.8, 8000, 0.08, 0.4, 0.3, 4, 20
ONV = ("TJ", "IDS", "KC", "JC", "MH", "NB", "I5", "I75")
CIS = ((0, 7, 3.3), (7, 7, 4.25), (14, 2, 4.55))
PLAN, RLEN, STRETCH, SHIFT = {}, 15.0, 2.0, 2.0
PULL = {("send", 2): 2.0, ("come", 2): 2.0, ("joint", 2): 2.0}
INORDER = "P"
WAR = "P"
XH = 1536
OAS = ((192, 64), (128, 64), (0, 128))
YCS = ((0, Q // 2), (Q // 2, Q // 2))
CV = (Q // 2, 0)
FK = 8
GS = ()
XS = [(0, 1), (1, 1)]
FB = [(64, 96), (64, 96), (64, 64, 64)]
D0 = {"A3": 0.0, "A2": 0.0, "A1": 1.6, "A0": 3.2, "F0": 3.1, "F1": 4.8, "F2": 6.7, "lit": 1.7, "viol": 6.3, "send": 6.5, "joint": 5.0,
      "keys": 7.5, "wake": 8.5, "lanes": 12.0, "moves": 12.0}
DUE = [dict(D0), dict(D0), dict(D0)]
GA = [(("S", 64), ("V", 64), ("S", 64), ("V", n), ("S", 64 - n))[:4 + (n < 64)] for n in (48, 64, 32)]
GF = [(("S", 64), ("S", 48), ("S", 48), ("S", 32))] * 2 + [(("S", 64), ("S", 64), ("S", 64))]


def search(ops, dues, parts, marks, loads):
    pool = [plan(ops, dues, parts, marks, SEED + 100 * i, None, SWAPS, HEAT) for i in range(POOL)]
    timed, pool = pool[0][1], [x[0] for x in pool]
    for cut in list(range(CUT, len(ops), CUT)) * 2:
        for x in list(pool):
            head = set(x[1][:cut])
            for y in list(pool):
                new = x[1][:cut] + [i for i in y[1] if i not in head]
                score, res = timed(new, cut, x[2])
                if score < min(x[0], y[0]) - 1e-9:
                    pool.remove(max(pool, key=lambda z: z[0]))
                    pool.append((score, new, res))
    order = plan(ops, dues, parts, marks, SEED + 1, min(pool, key=lambda z: z[0])[1], 2 * SWAPS, HEAT / 3)[0][1]
    return list(range(loads)) + [i for i in order if i >= loads]


def plan(ops, dues, parts, marks, seed, given, swaps, heat):
    n = len(ops)
    times = [[(np.zeros(len(WAKES)) + x).tolist() for x in o[4:6]] for o in ops]
    ops = [o[:4] + (times[i][0][0], times[i][1][0], o[6]) for i, o in enumerate(ops)]
    WAKE = WAKES[0]
    pred = [dict() for _ in range(n)]
    succ = [[] for _ in range(n)]
    hist = {}
    for i, (q, tag, reads, writes, occ, dur, _) in enumerate(ops):
        for w, lst in ((False, reads), (True, writes)):
            for _a, buf, m in lst:
                ps = buf in SCRATCH and SCRATCH[buf][0] == "psum"
                for em, ew, j in hist.get(buf, []):
                    same = ops[j][1] == tag
                    if j == i or (not (em & m and (w or ew)) and not ps) or (ps and same and q != "P" and not (em & m and (w or ew))):
                        continue
                    lat = 0.0 if same and (q == "P" or (not ew and q in WAR)) else WAKE
                    if pred[i].get(j, -1.0) < lat:
                        pred[i][j] = lat
        for w, lst in ((False, reads), (True, writes)):
            for _a, buf, m in lst:
                h = hist.setdefault(buf, [])
                ps = buf in SCRATCH and SCRATCH[buf][0] == "psum"
                if w and not ps:
                    h[:] = [e for e in h if e[0] & ~m or e[2] == i]
                h.append((m, w, i))
                if ps and len(h) > 150:
                    h[:] = h[-150:]
    above = [0] * n
    for i in range(n):
        for j in sorted(pred[i], reverse=True):
            if above[i] >> j & 1 and ops[j][4] == ops[j][5]:
                del pred[i][j]
            else:
                above[i] |= above[j] | 1 << j
    preds = [list(p.items()) for p in pred]
    for i in range(n):
        for j, lat in preds[i]:
            succ[j].append((i, lat))

    def place(key, back):
        before, after = (succ, preds) if back else (preds, succ)
        left, est, start, busy = [len(p) for p in before], [0.0] * n, [0.0] * n, {}
        ready = [i for i in range(n) if not left[i]]
        while ready:
            k = min(ready, key=lambda i: key[i])
            ready.remove(k)
            occ, dur = ops[k][4], ops[k][5]
            s, lst = est[k] + (dur - occ if back else 0.0), busy.setdefault(ops[k][0], [])
            at = len(lst)
            while at and lst[at - 1][1] > s:
                at -= 1
            while at < len(lst) and lst[at][0] < s + occ - 1e-9:
                s = max(s, lst[at][1])
                at += 1
            lst.insert(at, (s, s + occ))
            start[k] = s
            for i, lat in after[k]:
                est[i] = max(est[i], s + (occ if back else dur) + lat)
                left[i] -= 1
                if not left[i]:
                    ready.append(i)
        return start

    def replay(order, m):
        done, free = [0.0] * n, {}
        for i in order:
            s = max([free.get(ops[i][0], 0.0)] + [done[j] + (WAKES[m] if lat else 0.0) for j, lat in preds[i]])
            free[ops[i][0]] = s + times[i][0][m]
            done[i] = s + times[i][1][m]
        return max(done)

    key, best = [0.0] * n, None
    for i in range(n - 1, -1, -1):
        key[i] = min([dues.get(i, 200.0)] + [key[k] - lat - ops[i][5] for k, lat in succ[i]])
    rng = np.random.default_rng(seed)
    for it in range(0 if given else PASSES):
        start = place(key, False)
        order = sorted(range(n), key=lambda i: (round(start[i], 6), i))
        ends = [replay(order, m) for m in range(len(WAKES))]
        score = sum(e * w for e, w in zip(ends, WEIGHT))
        if best is None or score < best[0]:
            best = (score, start, order, ends)
            kept = key
        if it < 8 or it % 16 == 0:
            base = start if it < 8 else best[1]
            late = place([-base[i] - ops[i][5] for i in range(n)], True)
            key = [-late[i] - ops[i][4] - PULL.get(parts[i][:2], 0.0) for i in range(n)]
            for i in range(n - 1, -1, -1):
                key[i] = min([key[i]] + [key[k] - lat - ops[i][5] for k, lat in succ[i]])
        elif it % 2:
            part, by = parts[int(rng.integers(n))], float(rng.normal(0.0, SHIFT))
            key = [kept[i] + (by if parts[i] == part else 0.0) for i in range(n)]
            for i in range(n - 1, -1, -1) if by < 0 else range(n):
                if by < 0:
                    key[i] = min([key[i]] + [key[k] - lat - ops[i][5] for k, lat in succ[i]])
                else:
                    key[i] = max([key[i]] + [key[k] + lat + ops[k][5] for k, lat in preds[i]])
        else:
            lo, jitter = rng.random() * best[3][0], rng.normal(0.0, JITTER, n)
            key = [kept[i] + (float(jitter[i]) if lo < best[1][i] < lo + STRETCH else 0.0) for i in range(n)]

    def timed(order, lo, old):
        last = {}
        for i in order[:lo]:
            last[queue[i]] = i
        res = []
        for m in range(len(WAKES)):
            left, done, by = [list(x) for x in old[m][1:]]
            prev, w, occ, dur = dict(last), WAKES[m], occs[m], durs[m]
            for i in order[lo:]:
                b = prev.get(queue[i], -1)
                s = left[b] if b >= 0 else 0.0
                for j, lat in preds[i]:
                    x = done[j] + w if lat else done[j]
                    if x > s:
                        s, b = x, j
                by[i], prev[queue[i]], left[i], done[i] = b, i, s + occ[i], s + dur[i]
            res.append((max(done), left, done, by))
        return sum(w * (r[0] + MARK * sum(max(r[2][i] for i in m) for m in marks)) for r, w in zip(res, WEIGHT)), res

    queue = [o[0] for o in ops]
    occs, durs = [[[times[i][x][m] for i in range(n)] for m in range(len(WAKES))] for x in range(2)]
    order = given or best[2]
    score, res = timed(order, 0, [(0.0, [0.0] * n, [0.0] * n, [-1] * n)] * len(WAKES))
    top = (score, order, res)
    for it in range(swaps):
        if rng.random() < DRIFT:
            a = b = int(rng.integers(n - 1))
            while b < n - 1 and (b == a or queue[order[b]] != queue[order[a]]):
                b += 1
            u, v = order[a], order[b]
            if queue[u] != queue[v] or above[v] >> u & 1:
                continue
        else:
            end, _, done, by = res[int(rng.integers(len(WAKES)))]
            m = int(rng.integers(len(marks) + 1))
            i, held = max(marks[m], key=lambda x: done[x]) if m < len(marks) else done.index(end), []
            while by[i] >= 0:
                if queue[by[i]] == queue[i] and not above[i] >> by[i] & 1:
                    held.append((by[i], i))
                i = by[i]
            if not held:
                continue
            u, v = held[int(rng.integers(len(held)))]
            a, b = order.index(u), order.index(v)
        far = int(rng.geometric(0.5))
        if rng.random() < 0.5:
            while far > 1 and a > 0:
                a -= 1
                if queue[order[a]] == queue[v]:
                    if above[v] >> order[a] & 1:
                        a += 1
                        break
                    far -= 1
            mid = order[a:b]
            new = order[:a] + [x for x in mid if above[v] >> x & 1] + [v] + [x for x in mid if not above[v] >> x & 1] + order[b + 1:]
        else:
            while far > 1 and b < n - 1:
                b += 1
                if queue[order[b]] == queue[u]:
                    if above[order[b]] >> u & 1:
                        b -= 1
                        break
                    far -= 1
            mid = order[a + 1:b + 1]
            new = order[:a] + [x for x in mid if not above[x] >> u & 1] + [u] + [x for x in mid if above[x] >> u & 1] + order[b + 1:]
        s2, r2 = timed(new, a, res)
        if s2 < score + heat * (1 - it / swaps) * rng.exponential():
            order, score, res = new, s2, r2
            if score < top[0]:
                top = (score, order, res)
    PLAN["end"] = [r[0] for r in top[2]]
    PLAN["dbg"] = (ops, None, succ, [top[2][0][2][i] - durs[0][i] for i in range(n)])
    return top, timed


def route(topo, src, dst):
    if topo.may_write(src, dst):
        return None
    c = [r for r in topo.cores_of(src) if r != src and topo.may_write(r, dst)]
    return sorted(c, key=lambda r: (topo.die(r) != topo.die(src), r))[0]


def writer(topo, src, t, cores):
    dst = cores[(cores.index(src) + 1 + t % 3) % N]
    return route(topo, src, dst) or src


def relay_program(g, core, T, topo):
    mine = [(T.cores[r], T.cores[(r + 1 + t % 3) % N], t) for r in range(N) for t in range(RO)]
    mine = [x for x in mine if route(topo, x[0], x[1]) == core]
    for src, dst, t in mine:
        rid, pid = topo.addr(dst, core)
        m, e = topo.mask(core, dst), len(topo.engines(src, core))
        for big in sorted((True, False), key=lambda x: PLAN.get(("arr" if x else "na", t), 0)):
            if big:
                g.wait_ge(T.sem["ra%d" % t], e)
                g.remote_dma(T.AR[:, t * JW:(t + 1) * JW], T.RL[:, t * JW:(t + 1) * JW], T.sem["arr%d" % t], T.sem["ls%d" % t], pid, rid, m)
            else:
                g.wait_ge(T.sem["rn%d" % t], e)
                g.remote_dma(T.NN[:, 16 * t:16 * t + NW], T.RN[:, 16 * t:16 * t + NW], T.sem["na%d" % t], T.sem["nl%d" % t], pid, rid, m)
    for src, dst, t in mine:
        g.wait_ge(T.sem["nl%d" % t], len(topo.engines(core, dst)))
        g.wait_ge(T.sem["ls%d" % t], len(topo.engines(core, dst)))


def rank_program(g, core, T, topo):
    rank = T.rank_of(core)
    if rank is None:
        relay_program(g, core, T, topo)
        return
    eng = {"V": g.vector, "S": g.scalar, "P": g.tensor, "G": g, "Y": g.sync}
    cnt = {"V": 0, "S": 0, "P": 0, "G": 0}
    known = {q: {} for q in eng}
    hist = {}
    bits = {}
    serial = [0]
    final = {}

    def cols(lo, n, step):
        k = (lo, n, step)
        if k not in bits:
            m = 0
            for i in range(n):
                m |= 1 << (lo + i * step)
            bits[k] = m
        return bits[k]

    def a(buf, lo=0, n=None, step=1, p=None, p0=0):
        if n is None:
            n = T[buf].shape[1] - lo
        p = T[buf].shape[0] if p is None else p
        return (T[buf][p0:p0 + p, lo:lo + (n - 1) * step + 1:step] if step > 1 else T[buf][p0:p0 + p, lo:lo + n], buf, cols(lo, n, step))

    def ind(w, o):
        return (w[0].indirect(o[0]), w, o)

    def acc(x):
        return [x] if len(x) == 3 and isinstance(x[1], str) else [x[1], x[2]]

    def psum(buf):
        return buf in SCRATCH and SCRATCH[buf][0] == "psum"

    def need(q, tag, reads, writes):
        want = {}
        for w, lst in ((False, reads), (True, writes)):
            for _, buf, m in lst:
                ps = psum(buf)
                for (em, ew, eq, sem, val, snap) in hist.get(buf, []):
                    hit = em & m
                    if ps and eq != tag:
                        pass
                    elif not hit or not (w or ew):
                        continue
                    elif eq == tag and ((not ew and q in WAR) or (w and q in INORDER)):
                        continue
                    if known[q].get(sem, 0) >= val:
                        continue
                    if sem not in want or want[sem][0] < val:
                        want[sem] = (val, snap)
        for sem in list(want):
            val = want[sem][0]
            if any(o != sem and want[o][1].get(sem, 0) >= val for o in want):
                del want[sem]
        for sem in want:
            val, snap = want[sem]
            eng[q].wait_ge(T.sem[sem], val)
            for k, x in snap.items():
                if known[q].get(k, 0) < x:
                    known[q][k] = x
            known[q][sem] = max(known[q].get(sem, 0), val)

    def note(tag, reads, writes, sem, val, snap):
        for _, buf, m in writes:
            h = hist.setdefault(buf, [])
            h[:] = [e for e in h if e[0] & ~m] if not psum(buf) else [e for e in h if e[2] != tag or e[0] & ~m]
            h.append((m, True, tag, sem, val, snap))
        for _, buf, m in reads:
            h = hist.setdefault(buf, [])
            h[:] = [e for e in h if e[1] or e[2] != tag or e[0] & ~m]
            h.append((m, False, tag, sem, val, snap))

    ops = []

    dues, parts, now, marks = {}, [], [-1], [[] for _ in range(RO)]

    def step(name):
        parts.extend([(name, now[0], len(parts))] * (len(ops) - len(parts)))

    def due(t, name):
        dues[len(ops) - 1] = RLEN * t + DUE[t][name]
        step(name)

    def run(q, fn, out, ins, cost):
        writes = acc(out)[:1] if isinstance(out, tuple) else out
        reads = acc(out)[1:] if isinstance(out, tuple) else []
        for x in ins:
            reads = reads + acc(x)

        def issue():
            need(q, q, reads, writes)
            cnt[q] += 1
            fn().then_inc(T.sem["s" + q], 1)
            snap = dict(known[q])
            snap["s" + q] = cnt[q]
            note(q, reads, writes, "s" + q, cnt[q], snap)
        ops.append((q, q, reads, writes, cost, cost, issue))

    def dma(q, out, in_, sem, reads, writes, dur=2.5):
        serial[0] += 1
        tag = "d%d" % serial[0]
        final[sem] = 16

        def issue():
            need(q, None, reads, writes)
            eng[q].dma_start(out, in_).then_inc(T.sem[sem], 16)
            note(tag, reads, writes, sem, 16, dict(known[q]))
        if sem[:2] == "st":
            net = ("", tag, 1)
            ops.append((q, tag, reads, [net], 0.05, 1.8 * STORE, issue))
            ops.append(("D", tag + "x", [net], [], (dur - 1.8) * STORE, (dur - 1.8) * STORE, lambda: None))
            return
        ops.append((q, tag, reads, writes, 0.0 if sem[0] == "l" else 0.05, dur, issue))

    def copies(pairs, after):
        net = ("", "copies", 1)

        def issue():
            need("Y", None, [x[1] for x in pairs] + [after], [x[0] for x in pairs])
            for i, (out, in_) in enumerate(pairs):
                g.sync.dma_start(out[0], in_[0]).then_inc(T.sem["cp%d" % i], 16)
                note("cp%d" % i, [in_], [out], "cp%d" % i, 16, dict(known["Y"]))
        ops.append(("Y", "copies", [x[1] for x in pairs] + [after], [net], 0.05 * len(pairs), 1.8 * STORE, issue))
        for i, (out, in_) in enumerate(pairs):
            final["cp%d" % i] = 16
            ops.append(("N", "cp%d" % i, [net, in_], [out], 0.0, 0.45 * (i + 1) * STORE, lambda: None))

    def width(x):
        return bin(x[2]).count("1")

    def cost(out, ins, per):
        for x in ins:
            if isinstance(x[1], tuple):
                return 0.05 + GAT * CYC * 16 * width(x[2])
        if isinstance(out[1], tuple):
            return 0.05 + SCA * CYC * 16 * width(out[2])
        two = all(SCRATCH[x[1]][2] in (B, U, H) for x in [out] + ins)
        return CYC * max(64, width(out) * (per if per == 2 or not two else 0.5))

    def ap(x):
        return x[0] if isinstance(x, tuple) else x

    def copy(out, in_):
        run("V", lambda: g.vector.tensor_copy(ap(out), ap(in_)), out, [in_], cost(out, [in_], 1))

    def tt(out, x, y, op):
        ps = any(isinstance(z[1], str) and psum(z[1]) for z in (x, y))
        run("V", lambda: g.vector.tensor_tensor(ap(out), ap(x), ap(y), op), out, [x, y], cost(out, [x, y], 1 if ps else 2))

    def ts(out, x, s1, op0, s2=None, op1=None):
        ins = [x] + [s for s in (s1, s2) if isinstance(s, tuple)]
        if op1 is None:
            run("V", lambda: g.vector.tensor_scalar(ap(out), ap(x), ap(s1), None, op0), out, ins, cost(out, [x], 1))
        else:
            run("V", lambda: g.vector.tensor_scalar(ap(out), ap(x), ap(s1), ap(s2), op0, op1), out, ins, cost(out, [x], 1))

    def scan(out, d0, d1, ini, op0, op1):
        run("V", lambda: g.vector.tensor_tensor_scan(ap(out), ap(d0), ap(d1), ini, op0, op1), out, [d0, d1], cost(out, [d0, d1], 1))

    def fill(out, c):
        run("V", lambda: g.vector.memset(ap(out), c), out, [], cost(out, [], 1))

    def act(out, x, func, bias=0.0, scale=1.0):
        ins = [x] + ([bias] if isinstance(bias, tuple) else [])
        if isinstance(out[1], tuple):
            run("S", lambda: g.scalar.activation(ap(out), ap(x), func), out, ins, cost(out, [x], 1))
        else:
            c = cost(out, [x], 2) if isinstance(x[1], tuple) else CYC * max(64, width(out)) + (1.3 if func == F_.Silu else 0.0)
            run("S", lambda: g.scalar.activation(ap(out), ap(x), func, bias=ap(bias), scale=scale), out, ins, c)

    def times(out, x, c):
        if out[1] in ONV:
            return ts(out, x, c, A_.mult)
        ins = [x] + ([c] if isinstance(c, tuple) else [])
        run("S", lambda: g.scalar.activation(ap(out), ap(x), F_.Identity, scale=ap(c)), out, ins, CYC * max(64, width(out)))

    def mms(calls):
        def fn():
            for out, l, r, start, stop in calls:
                last = g.tensor.matmul(ap(out), ap(l), ap(r), start, stop)
            return last
        run("P", fn, [c[0] for c in calls], [x for c in calls for x in c[1:3]],
            sum(PEC * max(min(64, width(c[1])), width(c[2])) * (4 if SCRATCH[c[1][1]][2] == F else 1) for c in calls))

    def mm(out, l, r, start, stop):
        mms([(out, l, r, start, stop)])

    def iota(out, pat, base, cm):
        run("G", lambda: g.iota(ap(out), pat, base, cm, allow_small_or_imprecise_dtypes=True), out, [], 0.13 + 2 * CYC * width(out))

    def sel(out, x, pat, op, fl, base, cm):
        run("G", lambda: g.affine_select(ap(out), ap(x), pat, op, fl, base, cm), out, [x], 0.17 + 2 * CYC * width(out))

    def send(t, src, land, relay, arr, ra, ls, lat):
        dst = T.cores[(rank + 1 + t % 3) % N]
        first = route(topo, core, dst)
        to = dst if first is None else first
        net, once = ("", "net" + arr, 1), ONCE if (t, arr) == (0, "arr") else 0.0
        final[ls + str(t)] = len(topo.engines(core, to))
        final[arr + str(t)] = len(topo.engines(writer(topo, T.cores[(rank - 1 - t % 3) % N], t, T.cores), core))

        def issue():
            need("G", None, [src], [])
            PLAN.setdefault((arr, t), len(PLAN))
            rid, pid = topo.addr(to, core)
            g.remote_dma(land[0] if first is None else relay, src[0], T.sem[(arr if first is None else ra) + str(t)], T.sem[ls + str(t)],
                         pid, rid, topo.mask(core, to))
            note("r%s%d" % (ls, t), [src], [], ls + str(t), final[ls + str(t)], dict(known["G"]))
        ops.append(("G", "r%s%d" % (ls, t), [src], [net], 0.3 + once, lat + once, issue))
        ops.append(("N", "q%s%d" % (arr, t), [net], [land], 0.0, 0.0 if first is None else lat + once,
                    lambda: note("q%s%d" % (arr, t), [], [land], arr + str(t), final[arr + str(t)], {})))

    dma("Y", T.FR[:], T.fr[:], "ld0", [], [a("FR")], 2.2 * LOAD)
    dma("Y", T.TI[:], T.th[:], "ld1", [], [a("TI")], 2.4 * LOAD)
    for i, (p, n, at) in enumerate(CIS):
        dma("Y", T.CI[:, Q * p:Q * (p + n)], T.cl[:, Q * p:Q * (p + n)], "ld%d" % (5 + i), [], [a("CI", Q * p, Q * n)], at * LOAD)
    dma("Y", T.W[:, 0:XH], T.xv[:, 0:XH], "ld3", [], [a("W", 0, XH)], 6.8 * LOAD)
    dma("Y", T.W[:, XH:V], T.xv[:, XH:V], "ld4", [], [a("W", XH, V - XH)], 7.5 * LOAD)
    loads, loaded = len(ops), a("W", XH, V - XH)
    fill(a("NS"), 63.0)
    act(a("W", SB, 16), a("NS"), F_.Silu)

    GP, KP = [[-16, 8], [0, 16]], [[0, 8], [1, 16]]
    BO8, ONE1 = a("BO", 0, 8, 16), a("ONE", 0, 128, p=1)
    fill(a("ONE"), 1.0)
    sel(a("RX"), a("ONE", 0, 128), GP, A_.is_ge, 0.0, 0, 1)
    sel(a("BO"), a("RX"), [[16, 8], [0, 16]], A_.is_ge, 0.0, 15, -1)
    sel(a("TS"), a("RX"), [[1, 128]], A_.is_ge, 0.0, -1, -1)
    sel(a("ID"), a("ONE", 0, 128), [[-1, 128]], A_.is_equal, 0.0, 0, 1)
    sel(a("PM"), a("ONE", 0, 128, p=16), KP, A_.is_equal, 0.0, 0, -1)
    times(a("PMF"), a("PM"), 1.0)
    for name, c in (("NI", -1.0), ("I4", 4096.0), ("NI4", -4096.0)):
        ts(a(name), a("ID"), c, A_.mult)
    ts(a("NTS"), a("TS"), -1.0, A_.mult)
    starts = [[divmod(AS * t % K, Q), divmod(FS * t % K, Q)] for t in range(RO)]
    iota(a("P3", 2 * Q, Q), [[16, Q]], 2 * K, 1)
    fill(a("ROW", 512, Q), 4096.0 - 2 * K)
    fill(a("ROW", 0, Q), 1023.0)
    fill(a("ROW", 384, Q), 2.0 * K)
    fill(a("ROW", 384 + Q, Q), 4096.0 + K)
    fill(a("ROW", 384 + 2 * Q, 2, 2), -1.0)
    fill(a("ROW", 385 + 2 * Q, 2, 2), 0.0)
    fill(a("ROW", 64, 128), -4640.0)
    fill(a("ROW", 192, Q), 4608.0)
    fill(a("ROW", 256, 128), V + OFF)
    times(a("SN"), a("ONE", 0, LA), 2 * V + OFF)

    def sentinels(t):
        dma("Y", T.LN[:, 0:LA], T.SN[:], "sn%d" % (2 * t), [a("SN")], [a("LN", 0, LA)])
        dma("Y", T.LN[:, K:K + LF], T.SN[:, 0:LF], "sn%d" % (2 * t + 1), [a("SN")], [a("LN", K, LF)])

    def cyclic(t):
        for c in range(2):
            p0, i = starts[t][c][0], 128 * (2 * (t - 1) + c)
            rx, ry = (a("FW", 2 * i, 128), a("FW", 2 * i + 128, 128)) if 2 * i < K else (a("RX"), a("RY"))
            sel(rx, a("BO"), [[16, 8], [0, 16]], A_.is_ge, 0.0, p0 - 1, -1)
            sel(ry, a("NBO"), [[0, 8], [-1, 16]], A_.is_ge, 0.0, p0 - 1, 0)
            sel(a("SE", i, 128), a("BO"), GP, A_.is_equal, 0.0, -p0, 1)
            sel(a("MX", i, 128), a("NBO"), KP, A_.is_equal, 0.0, -p0, 0)
            mms([(a("B6", 256 + 128 * c, 128), a("ID"), m, j == 0, j == 2) for j, m in enumerate((a("NTS"), rx, ry))])
        times(a("MH", 256 * (t - 1), 256), a("B6", 256, 256), 1.0)

    def lists(t):
        fa, fb, fd = a("FL", 0, Q), a("FL", 2 * Q, Q), a("FL", Q, Q)
        mm(a("B6", 0, 2 * Q + 4), ONE1, a("ROW", 384, 2 * Q + 4), True, False)
        scan(a("PRE", Q, Q), fb, fd, 0.0, A_.add, A_.add)
        scan(a("PRE", 0, Q), a("ONE", 0, Q), fa, 0.0, A_.mult, A_.subtract)
        mm(a("B6", 0, Q), a("N15" if t else "NI4"), fa, False, False)
        if not t:
            mm(a("B6", 0, Q), ONE1, a("ROW", 512, Q), False, False)
        else:
            tt(a("FP"), fa, a("POS", Q * (t - 1), Q), A_.mult)
            mm(a("B6", 0, Q), a("ID"), a("POS", Q * (t - 1), Q), False, False)
        mm(a("B6", Q, Q), a("I4"), fb, False, False)
        mm(a("B6", Q, Q), a("I4"), fd, False, False)
        for c in (1, 0):
            q0, i, b = starts[t][c][1], 128 * (2 * (t - 1) + c), 2 * Q + 2 * c
            mm(a("B6", b, 1), a("MH", i, 128) if t else a("NTS"), a("PRE", Q * c + Q - 1, 1), False, False)
            if t:
                mm(a("B6", b, 1), a("SE", i, 128), a("PRE", Q * c + q0 - 1, 1), False, False)
                mm(a("B6", b + 1, 1), a("MX", i, 128), a("PRE", Q * c + Q - 1, 1), False, False)
        mms(([(a("B6", 0, Q), a("NI"), a("FP"), False, False)] if t else []) + [(a("B6", 0, 2 * Q), a("NI"), a("PRE", 0, 2 * Q), False, True)])
        for c in range(2):
            q0, b = starts[t][c][1], 2 * Q + 2 * c
            ts(a("P3", Q * c + q0, Q - q0), a("B6", Q * c + q0, Q - q0), a("B6", b, 1), A_.add)
            if q0:
                ts(a("P3", Q * c, q0), a("B6", Q * c, q0), a("B6", b, 1), A_.add, a("B6", b + 1, 1), A_.add)
        if not t:
            tt(a("P3", 0, Q), a("P3", 0, Q), a("P3", 2 * Q, Q), A_.min)
        tt(a("PL"), a("P3", 0, Q), a("P3", Q, Q), A_.min)
        act(ind(a("LN"), a("PL")), a("C%d" % t, 2 * JW, K), F_.Silu)
        if t:
            marks[t - 1].append(len(ops) - 1)
            due(t - 1, "lanes")
        else:
            dues[len(ops) - 1] = -4.0
        for lo, n in OAS:
            ts(a("OA", lo, n), a("LN", lo, n), 0.25 - OFF, A_.add)
        ts(a("OF"), a("LN", K, LF), 0.25 - OFF, A_.add)
        if t < RO - 1:
            sentinels(t)
        step("offsets")
        dr = a("B6", 128, Q)
        mms([(dr, ONE1, a("QR", 0, Q, p=1), True, False), (a("B6", 128 + Q, 1), a("TS"), a("QR", Q - 1, 1), False, False),
             (dr, a("NI4"), fd, False, False), (dr, a("NI4"), fb, False, False), (dr, a("I4"), fa, False, False)])
        mms([(dr, a("ID"), a("PRE", Q * c, Q), False, False) for c in range(2)]
            + [(a("B6", 128 + Q, 1), a("TS"), a("PRE", Q * c + Q - 1, 1), False, c == 1) for c in range(2)])
        ts(a("DR", 0, Q), dr, a("B6", 128 + Q, 1), A_.add, 1024.0, A_.min)
        if t == RO - 1:
            run("V", lambda: g.vector.transpose(T.TR[:], T.DR[:]), a("TR"), [a("DR")], 64 * CYC)
            mms([(a("B6", 192 + e, 16, 3), a("IDS", 160 * (e % 2) + 16 - 16 * (c - e % 2), 128), a("TR", 32 * (e // 2) + 16 * c, 16),
                  e + c == 0, e + c == 3) for e in range(3) for c in range(2)])
            copy(a("DRN"), a("B6", 192, Q))

    def gather(q, lo, n, frozen, th):
        w = ind(a("W", 0, DU), a("OF" if frozen else "OA", lo, n))
        out = a("S2" if frozen else "S", 16 * lo, 16 * n)
        if frozen:
            if q == "V":
                ts(out, w, a(th, 1, 1), A_.add, 0.0, A_.max)
            else:
                act(out, w, F_.Relu, a(th, 1, 1))
        elif q == "V":
            ts(out, w, UN, A_.mult)
        else:
            act(out, w, F_.Identity, 0.0, UN)

    times(a("LN", 0, LA), a("ONE", 0, LA), 2 * V + OFF)
    times(a("LN", K, LF), a("ONE", 0, LF), 2 * V + OFF)
    for p in range(16):
        ts(a("C0", 2 * JW + p, Q, 16), a("CI", Q * p, Q), OFF, A_.add)
    ts(a("FL", 0, Q), a("FR"), 0.5, A_.is_lt)
    ts(a("FL", Q, Q), a("FR"), 3.5, A_.is_gt)
    ts(a("FL", 2 * Q, Q), a("FR"), 0.5, A_.is_lt, 1.0, A_.subtract)
    iota(a("QR"), [[1, Q]], 1, 0)
    ts(a("X4"), a("FR"), 512.0, A_.mult)
    lists(0)
    for lo, n in ((0, XH), (XH, V - XH)):
        ts(a("W", V + lo, n), a("W", lo, n), -1.0, A_.mult, 63.0, A_.add)
    ts(a("TH", 0, 1), a("TI"), UN, A_.mult)
    ts(a("TH", 1, 1), a("TI"), -1.0, A_.mult, 1.0, A_.add)
    step("first")
    fill(a("SEGA"), 0.0)
    fill(a("SEGA", 0, 64, 16), -2.0 ** 30)
    fill(a("RST", 0, 512), 64 * UN)
    fill(a("RST", 15, 32, 16), 1152 * UN)
    times(a("YW", LA, 512), a("ONE"), 1.625)
    copies([(a("RST", 512 * i, 512), a("RST", 0, 512)) for i in range(7, 0, -1)]
           + [(a("YW", lo, min(512, LW - lo)), a("YW", LA, min(512, LW - lo))) for lo in range(K + LF, LW, 512)]
           + [(a("C%d" % t, 0, 2 * JW), a("SN")) for t in range(RO)], loaded)
    fill(a("CUM", 0, 16), 0.0)
    times(a("O32"), a("ONE", 0, 128), -1.0 / 4096)
    for name, c in (("N2K", -2048.0), ("P1K", 1024.0), ("HI", 0.5), ("NHI", -0.5), ("I5", 512.0), ("I75", 1.75), ("NQ", -1.0 / 512), ("N15", -2.0 * K)):
        times(a(name), a("ID"), c)
    times(a("NBO"), a("BO"), -1.0)
    times(a("B75"), a("BO"), 1.75)
    for i in range(2):
        ts(a("I2K", 8 * i, 8), BO8, 2.0 ** 25, A_.mult)
    ts(a("NIN"), BO8, -1.0, A_.mult)
    fill(a("EP"), 0.0)
    ts(a("EP", 15, 8, 16), BO8, -256.0, A_.mult)
    step("fill")
    mms([(a("B0", 128 * j, 128), a("PM"), a("PM"), True, True) for j in range(2)])
    act(a("DM"), a("B0", 0, 256), F_.Identity)
    step("mask")
    fill(a("B64"), 0.0)
    fill(a("BI"), 0.0)
    for i in range(2):
        fill(a("B64", 64 * i, 64, p=64, p0=64 * i), 16384.0)
        fill(a("BI", 2 * i, 2, p=64, p0=64 * i), 8192.0)
    sel(a("XV", 256, 128), a("B64"), [[1, 128]], A_.is_gt, 0.0, 0, -1)
    sel(a("TRI"), a("XV", 256, 128), [[1, 128]], A_.not_equal, 4096.0, 0, -1)
    tt(a("CJ", 0, J), a("BO", 0, J, 16), a("BO", 64, J, 16), A_.add)
    for j in range(J):
        ts(a("BJ", 128 * j, 128), a("B64"), a("CJ", j, 1), A_.mult, 1.0 / 16384, A_.mult)
        times(a("TJ", 128 * j, 128), a("TRI"), a("CJ", j, 1))
    fill(a("DR", Q), 0.0)
    fill(a("IDS"), 0.0)
    tt(a("CJ", J, 2), a("CJ", 0, 2), a("CJ", 2, 2), A_.add)
    for e in range(2):
        times(a("IDS", 160 * e + 16, 128), a("ID"), a("CJ", J + e, 1))
    fill(a("NB", 32, 16), 0.0)
    for lo, n, b, sign in ((0, 4, 0, -2.0), (4, 8, 0, 2.0), (12, 4, 4, -2.0)):
        times(a("NB", lo, n), a("BO", 16 * b, n, 16), 1.0)
        times(a("NB", 16 + lo, n), a("BO", 16 * b, n, 16), sign)
        if sign < 0:
            times(a("NB", 32 + lo, n), a("BO", 16 * b, n, 16), float(V))
    step("pairs")
    iota(a("TB", 0, Q), [[16, Q]], 2 * JW, 1)
    iota(a("TB", Q, Q), [[1, 16], [256, 3]], 2 * JW, 16)
    iota(a("TB", 2 * Q, 8), [[16, 8]], JW - 255, 1)
    iota(a("TB", 104, 4), [[0, 4]], 1000, 0)
    iota(a("TB", 108, 16), [[0, 2], [16, 8]], DU, 1)
    iota(a("TB", 124, Q), [[1, Q]], 0, Q)
    mm(a("B1", 0, 172), a("PMF"), a("TB"), True, True)
    times(a("JC"), a("B1", 0, 172), 1.0)
    for t in range(1, RO):
        ts(a("PX", 0, Q), a("JC", 124, Q), AS * t % K - 0.5, A_.is_lt, float(K), A_.mult)
        ts(a("PX", Q, Q), a("JC", 124, Q), -float(AS * t % K), A_.add)
        tt(a("POS", Q * (t - 1), Q), a("PX", 0, Q), a("PX", Q, Q), A_.add)
    iota(a("LQI"), [[1, 16]], 0, 0)
    copy(a("L2"), a("LQI"))
    sel(a("MA"), a("TS"), [[-1, 128]], A_.not_equal, -255.0, 0, 1)
    sel(a("GT"), a("BO"), [[-1, 128]], A_.is_ge, 0.0, 0, 1)
    sel(a("MB"), a("GT"), [[-1, 128]], A_.not_equal, 256.0, 0, 1)
    step("joint")
    iota(a("XV", 0, 128), KP, -16, 0)
    times(a("XV", 128, 128), a("BO"), 2.0 ** 18)
    tt(a("CN"), a("XV", 0, 128), a("XV", 128, 128), A_.mult)
    iota(a("KR", 0, 256), [[0, 16], [-2, 16]], 29, 0)
    iota(a("KR", 15, 16, 16), [[0, 16]], -35, 0)
    iota(a("KR", 256, 256), [[-1, 2], [0, 8], [-1, 16]], 16, 0)
    times(a("KC", 0, 256), a("KR", 0, 256), 2.0 ** 24)
    times(a("KC", 256, 256), a("KR", 256, 256), 2.0 ** 11)

    for t in range(RO):
        C, last, th = "C%d" % t, t == RO - 1, "TT" if t else "TH"
        step("dead")
        now[0] = t
        for u in range(1, RO) if t == 0 else ():
            cyclic(u)
        step("cyclic")
        lo = LA
        for q, n in GA[t]:
            lo -= n
            gather(q, lo, n, False, th)
            due(t, "A" + str(lo // CH))
        for q, n in GF[t]:
            gather(q, lo, n, True, th)
            due(t, "F" + str(lo // CH))
            lo += n
        ts(a("CZ"), a("OA"), -float(V), A_.add)
        due(t, "lit")
        ts(a("SG"), a("OA"), V - 0.5, A_.is_gt)
        due(t, "lit")
        mms([(a("B5", 192, 128), a(l), a("CZ", j, 128, 2), j == 0, j == 1) for j, l in enumerate(("NHI", "HI"))])
        times(a("DEO"), a("B5", 192, 128), 1.0 if t in GS else 2.0)
        mms([(a("B2", 256, 128), ONE1, a("ROW", 256, 128), True, False)]
            + [(a("B2", 256, 128), a("HI"), a("CZ", j, 128, 2), False, j == 1) for j in range(2)])
        for h in (1, 0):
            key = "B%d" % h
            mms([(a(key, 0, 256), ONE1, a("KC", 256 * i, 256), i == 0, False) for i in range(2)])
            mms([(a(key, 128 * i, 128), a("SG", 128 * h, 128), a(m), False, False) for i, m in enumerate(("N2K", "P1K"))])
            mms([(a("B4" if h else "B7", j, 128, J), a("TJ", 128 * j, 128), a("DM", 0, 128), j == 0, False) for j in range(J)])
        for c in range(NA - 1, -1, -1):
            lo = 16 * CH * c
            scan(a("M", lo, 16 * CH), a("SEGA"), a("S", lo, 16 * CH), 0.0, A_.add, A_.max)
            if c % 2:
                continue
            ts(a("RST", lo, 128, 16), a("M", lo + 15, 128, 16), a(th, 0, 1), A_.is_lt, 960 * UN, A_.subtract)
            ts(a("YW", CH * c, 128), a("M", lo + 15, 128, 16), a(th, 0, 1), A_.is_lt, 8.0, A_.mult)
            mms([(a("B%d" % (c // 2), 128 * i, 128), a("YW", CH * c, 128), a("CN"), False, False) for i in range(2)])
            step("rows")
            for lo in (lo + 16 * CH, lo):
                scan(a("Z", lo, 16 * CH), a("S", lo, 16 * CH), a("RST", lo, 16 * CH), 1.0, A_.min, A_.add)
            step("mask")
        for h in (1, 0):
            mms([(a("B%d" % h, k, 16, 16), a("Z", 16 * 128 * h + k, 128, 16), a("I2K"), False, False) for k in range(16)]
                + [(a("B%d" % h, 0, 128), a("CZ", 128 * h, 128), a("ID"), False, True)])
        step("sums")
        mm(a("B3", 256, 128), ONE1, a("ROW", 64, 128), True, False)
        mm(a("B3", 256, 128), a("I4"), a("DM", 0, 128), False, False)
        mms([(a("B3", 128, 128), a("BO"), a("YW", 0, 128, 2), False, False), (a("B3", 256, 128), a("BO"), a("YW", 1, 128, 2), False, False)]
            + [(a("B3", 8 * h, 8), a("YW", 128 * h, 128), BO8, False, h == 1) for h in range(2)])
        ts(a("BT"), a("B3", 128, 128), 32.0, A_.min, -16.0, A_.mult)
        due(t, "viol")
        tt(a("BTM"), a("B3", 256, 128), a("BT"), A_.is_ge)
        ts(a("NV"), a("B3", 0, 16), 28.0, A_.is_lt, 4096.0, A_.mult)
        scan(a("CUM", 16, 128), a("ONE", 0, 128), a("BTM"), 0.0, A_.mult, A_.add)
        mms([(a("B3", 384, 8), a("MA"), a("CUM", 31, 8, 16), True, False), (a("B3", 384, 8), a("MB"), a("CUM", 15, 8, 16), False, False),
             (a("B3", 392, 1), a("NBO"), a("CUM", 143, 1), False, False), (a("B3", 393, 1), a("B75"), a("CUM", 143, 1), False, True)])
        tt(a("JL", 0, NW), a("B3", 384, NW), a("JC", 2 * Q, NW), A_.min)
        due(t, "send")
        for k0 in range(0, 16, 4):
            mms([(a("B2", k, 8, 16), a("S", 16 * (1 - h) + k, 128, 32), a("NIN") if h else BO8, h == 0, h == 1)
                 for k in range(15 - k0, 11 - k0, -1) for h in range(2)])
        if t in GS:
            act(a("GT"), a("B2", 0, 128), F_.Sign, -0.5, 1.0 / UN)
        else:
            ts(a("GT"), a("B2", 0, 128), 0.0, A_.is_gt, 0.5, A_.subtract)
        mm(a("B2", 128, 128), a("GT"), a("ID"), True, True)
        tt(a("PJ"), a("B2", 128, 128), a("DEO"), A_.mult)
        tt(a("JB"), a("B2", 256, 128), a("PJ"), A_.add)
        due(t, "joint")
        send(t, a("JB"), a("AR", t * JW, JW), T.RL[:, t * JW:(t + 1) * JW], "arr", "ra", "ls", HOPJ)
        send(t, a("JL", 0, NW), a("NN", 16 * t, NW), T.RN[:, 16 * t:16 * t + NW], "na", "rn", "nl", HOPN)
        for h in (1, 0):
            key, same, vm, sm = "B%d" % h, "B4" if h else "B7", a("VM", 256 * h, 128), a("VM", 256 * h + 128, 128)
            scan(a("R", 256 * h, 256), a("SEGA", 0, 256), a(key, 0, 256), 0.0, A_.add, A_.max)
            due(t, "keys")
            ts(a("RA", 16 * h, 16), a("R", 256 * h + 15, 16, 16), V - 1, A_.bitwise_and)
            if last:
                tt(vm, ind(a("RA", 16 * h, 16), a("L2", 0, 8)), a("DM", 0, 128), A_.mult)
                copy(sm, ind(a("RA", 16 * h, 16), a("L2", 8, 8)))
            else:
                tt(a("VM", 256 * h, 256), ind(a("RA", 16 * h, 16), a("L2")), a("DM"), A_.mult)
            tt(a("VF", 8 * h, 8), a("RA", 16 * h, 8), a("NV", 8 * h, 8), A_.add)
            step("chosen")
            mms([(a(same, j, 128, J), a("BJ", 128 * j, 128), vm, False, j == J - 1) for j in range(J)])
            mms([(a(key, 256, 8), vm, BO8, True, last)] + ([] if last else [(a(key, 256, 8), sm, a("NB", 20, 8), False, True)]))
            copy(a("GL", 8 * h, 8), a(key, 256, 8))
            ns = 1 if last else 2
            mms([(a(key, 272, 8), vm, BO8, True, False)] if last else
                [(a(key, 272, 16), a("DM", 0, 128), a("NB", 32, 16), True, False), (a(key, 272, 16), vm, a("NB", 0, 16), False, False),
                 (a(key, 272, 16), sm, a("NB", 16, 16), False, False)])
            new, other = [a("XV", 256 * h + XB + XB * b, XB) for b in range(2)], [a("XV", 256 * h + 3 * XB * b, XB) for b in range(2)]
            if last:
                mms([(a("B3", 128 * h, 128), ONE1, ONE1, True, False), (a("B3", 128 * h, 128), sm, a("NQ"), False, True)])
                tt(a("XV", 256 + 128 * h, 128), a("B3", 128 * h, 128), a("YW", 128 * h, 128), A_.mult)
                tt(a("XN", 128 * h, 128), ind(a("W", 0, DU), a("GL", 8 * h, 8)), a("XV", 256 + 128 * h, 128), A_.add)
                ts(a("XV", 128 * h, 128), a("XN", 128 * h, 128), 0.0, A_.max, 63.0, A_.min)
            elif (t, h) in XS:
                act(a("XN", 128 * h, 128), ind(a("W", 0, DU), a("GL", 8 * h, 8)), F_.Identity)
                mms([(a("B3", 128 * h, 128), a("ID"), a(m, 128 * h, 128), m == "YW", m == "XN") for m in ("YW", "XN")])
                for b in range(2):
                    act(other[b], a("B3", 128 * h + XB * b, XB), F_.Relu, 63.0, -1.0)
                for b in range(2):
                    act(new[b], other[b], F_.Identity, 63.0, -1.0)
            else:
                tt(a("XN", 128 * h, 128), ind(a("W", 0, DU), a("GL", 8 * h, 8)), a("YW", 128 * h, 128), A_.add)
                ts(a("XV", 256 * h + XB, 128), a("XN", 128 * h, 128), 63.0, A_.min)
                for b in range(2):
                    ts(other[b], new[b], -1.0, A_.mult, 63.0, A_.add)
            step("new%d" % h)
            for i in range(8):
                ts(a("EE", 512 * h + XB * i, XB), a(same, XB * i, XB), a("VF", 8 * h + i, 1), A_.is_equal)
            mms([(a(key, 272 + j, 2 * ns, J), a("EE", 512 * h + j, 128, J), a("BI", 0, 2 * ns, 3 - ns), False, j == J - 1) for j in range(J)])
            tt(a("SL", 8 * ns * h, 8 * ns), a(key, 272, 8 * ns), a("JC", 108, 8 * ns), A_.min)
            step("lowest%d" % h)
        for b in range(LA // XB - 1, -1, -1):
            copy(ind(a("W"), a("SL", ns * J * b, ns * J)), a("XV", ns * XB * b, ns * XB))
            if b == LA // XB - 1:
                due(t, "moves")
        marks[t].append(len(ops) - 1)
        if last:
            dma("Y", T.yx[:], T.W[:, 0:V], "st0", [a("W", 0, V)], [], 3.7)
        step("moves")
        lo = 0
        for n in FB[t]:
            for k0 in range(0, 16, FK):
                mms([(a("B5", lo, n), a("ID"), a("S2", 16 * lo + k, n, 16), k == 0, k == 15) for k in range(k0, k0 + FK)])
            lo += n
        act(a("YW", K, lo), a("B5", 0, lo), F_.Relu, 8.0, -8.0)
        due(t, "wake")
        if lo < LF:
            scan(a("M2", 0, 16 * (LF - lo)), a("SEGA", 0, 16 * (LF - lo)), a("S2", 16 * lo), 0.0, A_.add, A_.max)
            ts(a("YW", K + lo, LF - lo), a("M2", 15, LF - lo, 16), 0.5, A_.is_lt, 8.0, A_.mult)
            due(t, "wake")
        if not last:
            run("S", lambda: g.scalar.activation(T.NS[:], T.NV[:], F_.Identity, accum_out=T.SGA[:]), [a("SGA"), a("NS")], [a("NV")], 90 * CYC)
            mm(a("B2", 500, 1), a("O32"), a("SGA"), True, True)
            copy(a("AI", 0, 1), a("B2", 500, 1))
            ts(a("AI", 1, 1), a("AI", 0, 1), 3, A_.bitwise_and)
            ts(a("TT", 0, 1), a("AI", 1, 1), UN, A_.mult, a("TH", 0, 1), A_.add)
            ts(a("TT", 1, 1), a("AI", 1, 1), -1.0, A_.mult, a("TH", 1, 1), A_.add)
        step("count")
        ts(a("JLU"), a("NN", 16 * t, 8), 255.0, A_.add)
        if last:
            act(a(C, 2 * JW, K), a(C, 2 * JW, K), F_.Identity, MAGIC)
            ts(ind(a(C, 0, 2 * JW), a("JLU")), a("AR", t * JW, JW), 1.0, A_.mult, MAGIC, A_.add)
        else:
            act(ind(a(C, 0, 2 * JW), a("JLU")), a("AR", t * JW, JW), F_.Silu)
        act(a("NT"), a("DRN" if last else "DR", 0, Q), F_.Sign, a("NN", 16 * t + 8, 1), 1.0 - UN)
        mms([(a("B2", 384, Q), ONE1, a("ROW", 0, Q), True, False), (a("B2", 384, Q), a("ID"), a("DRN" if last else "DR", 0, Q), False, False)])
        mm(a("B2", 384, Q), a("P1K"), a("NT"), False, True)
        tt(a("IX"), a("B2", 384, Q), a("JC", Q if last else 0, Q), A_.min)
        if last:
            for i, (lo, n) in enumerate(YCS):
                act(a("C3", 16 * lo, 16 * n), ind(a(C), a("IX", lo, n)), F_.Identity, -MAGIC - OFF)
                dma("Y", T.yc[:, 16 * lo:16 * (lo + n)], T.C3[:, 16 * lo:16 * (lo + n)], "st%d" % (2 + i), [a("C3", 16 * lo, 16 * n)], [], 1.8 + 1.5 * n / Q)
        else:
            act(a("C%d" % (t + 1), 2 * JW + 16 * CV[t]), ind(a(C), a("IX", CV[t])), F_.Identity)
            if CV[t]:
                copy(a("C%d" % (t + 1), 2 * JW, 16 * CV[t]), ind(a(C), a("IX", 0, CV[t])))
        step("come")
        act(a("FW"), ind(a("YW"), a("PL")), F_.Identity)
        y = a("B5", 448, Q)
        mms([(y, ONE1, a("ROW", 192, Q), True, False), (y, a("ID"), a("X4"), False, False), (y, a("I75"), a("DR", 0, Q), False, False)])
        mms([(y, a("EP", 15 - p, 128), a("FW", p, Q, 16), False, p == 15) for p in range(16)])
        if not last:
            act(a("TE"), a("X4"), F_.Identity, 19968.0, -12.0)
            ts(a("FL", 2 * Q, Q), y, 0.0, A_.is_le, 1.0, A_.subtract)
            tt(a("FL", Q, Q), y, a("TE"), A_.is_gt)
        ts(a("FL", 0, Q), y, a("NN", 16 * t + 9, 1), A_.is_le)
        tt(a("LL"), y, a("X4"), A_.is_gt)
        x4 = a("B2", 440, Q)
        mms([(x4, a("ID"), a("X4"), True, False), (x4, a("I5"), a("LL"), False, False), (x4, a("NI4"), a("FL", 0, Q), False, True)])
        if last:
            act(a("YF"), x4, F_.Relu, 0.0, 1.0 / 512)
        else:
            act(a("X4"), x4, F_.Relu)
            lists(t + 1)
    dma("Y", T.yf[:], T.YF[:], "st1", [a("YF")], [], 2.2)
    if "order" not in PLAN:
        step("end")
        PLAN["order"] = search(ops, dues, parts, marks, loads)
    for i in PLAN["order"]:
        ops[i][6]()
    for q in cnt:
        g.wait_ge(T.sem["s" + q], cnt[q])
    for s in final:
        g.wait_ge(T.sem[s], final[s])
